import numpy as np
import ml_dtypes


def mxq(x, axis, fmt="e4m3"):
    dtype, down = {"e4m3": (ml_dtypes.float8_e4m3fn, 7), "e5m2": (ml_dtypes.float8_e5m2, 14)}[fmt]
    v = np.moveaxis(np.asarray(x, np.float32).astype(ml_dtypes.bfloat16).astype(np.float64), axis, -1)
    blocks = v.reshape(v.shape[:-1] + (-1, 32))
    amax = np.abs(blocks).max(-1, keepdims=True)
    byte = np.maximum(np.where(amax > 0, np.frexp(amax)[1] - 1 + 127, 0) - down, 1)
    scale = np.exp2(byte - 127.0)
    codes = (blocks / scale).astype(np.float32).astype(dtype).astype(np.float64)
    return np.moveaxis((codes * scale).reshape(v.shape), -1, axis)


WIDE = False


def mx_kscale(k):
    if not WIDE:
        return np.ones(k)
    levels = np.array([10, -10, 5, -5, 0])
    if k % 512:
        return np.exp2(np.random.permutation(np.resize(levels, k // 32))).repeat(32)
    a = np.empty((k // 512, 16))
    for p in range(k // 512):
        a[p, :8] = np.random.permutation(np.resize(levels, 8))
        for g in range(8):
            far = levels[np.abs(levels - a[p, g]) >= 10]
            a[p, g + 8] = far[np.random.randint(len(far))]
    return np.exp2(a.ravel()).repeat(32)


def f64(x):
    return np.asarray(x).astype(np.float64)


def striped(idx):
    return np.tile(idx.reshape(-1, 16).T, (8, 1)).astype(np.uint16)


def unstriped(offs):
    return offs[:16].T.reshape(-1).astype(np.int64)


E2M1 = np.array([0.0, 0.5, 1.0, 1.5, 2.0, 3.0, 4.0, 6.0, -0.0, -0.5, -1.0, -1.5, -2.0, -3.0, -4.0, -6.0])


def pack_weight(w, fmt):
    k, n = w.shape
    w = f64(np.asarray(w, np.float32).astype(ml_dtypes.bfloat16)).reshape(k // 32, 32, n)
    amax = np.abs(w).max(1)
    if fmt == "e4m3":
        byte = np.frexp(amax)[1] - 1 + 127 - 7
    else:
        mant, ex = np.frexp(amax / 6.0)
        byte = np.where(mant > 0.5, ex, ex - 1) + 127
    byte = np.clip(np.where(amax > 0, byte, 1), 1, 254)
    scaled = (w * np.exp2(127.0 - byte)[:, None, :]).reshape(k, n).astype(np.float32)
    by_word = np.ascontiguousarray(scaled.reshape(k // 512, 128, 4, n).transpose(0, 1, 3, 2))
    if fmt == "e4m3":
        words = by_word.astype(ml_dtypes.float8_e4m3fn).view(np.uint8)
    else:
        c = by_word.astype(ml_dtypes.float4_e2m1fn).view(np.uint8) & 0xF
        words = (c[..., 0::2] | (c[..., 1::2] << 4)).reshape(k // 512, 128, 2 * n)
    return np.ascontiguousarray(words), np.ascontiguousarray(byte.astype(np.uint8).reshape(k // 512, 16, n))


def unpack_weight(words, scales, fmt):
    g, _, n = scales.shape
    words = np.ascontiguousarray(words).reshape(g, 128, n, -1)
    if fmt == "e4m3":
        vals = words.view(ml_dtypes.float8_e4m3fn).astype(np.float64)
    else:
        nib = np.empty((g, 128, n, 4), np.uint8)
        nib[..., 0::2] = words & 0xF
        nib[..., 1::2] = words >> 4
        vals = E2M1[nib]
    vals = vals * np.repeat(np.exp2(scales.astype(np.float64) - 127.0), 8, axis=1)[..., None]
    return vals.transpose(0, 1, 3, 2).reshape(g * 512, n)


def gelu(v):
    return 0.5 * v * (1.0 + np.tanh(np.sqrt(2.0 / np.pi) * (v + 0.044715 * v**3)))


def often(T, S):
    return np.random.permutation(T)[(T * np.random.uniform(0, 1, S) ** 4).astype(np.int64)]


K, T, S, T2, P, H, N = 1024, 4096, 1024, 2048, 512, 1024, 512


def setup_inputs():
    n = np.random.standard_normal
    s, u = mx_kscale(K)[:, None], mx_kscale(H)[:, None]
    tab_words, tab_scales = pack_weight(n((K, T)) * s, "e4m3")
    tab2_words, tab2_scales = pack_weight(n((K, T2)) * s, "e4m3")
    w2_words, w2_scales = pack_weight(n((K, H)) / np.sqrt(K) / s, "e2m1")
    return {
        "tab_words": tab_words, "tab_scales": tab_scales,
        "offs": striped(np.random.permutation(T)[:S]),
        "w1": (0.7 * n((K, H)) / np.sqrt(K) / s).astype(np.float32),
        "pos1": striped(often(S, P)),
        "tab2_words": tab2_words, "tab2_scales": tab2_scales,
        "offs2": striped(np.random.permutation(T2)[:P]),
        "w2_words": w2_words, "w2_scales": w2_scales,
        "gain": (np.exp(0.3 * n(H)) * u[:, 0]).astype(np.float32),
        "w3": (1.5 * n((H, N)) / np.sqrt(H) / u).astype(np.float32),
    }


def reference(tab_words, tab_scales, offs, w1, pos1, tab2_words, tab2_scales, offs2,
              w2_words, w2_scales, gain, w3):
    v = unpack_weight(tab_words, tab_scales, "e4m3")[:, unstriped(offs)]
    h = mxq(f64(w1), 0, "e4m3").T @ v
    a = h[:, unstriped(pos1)]
    v2 = unpack_weight(tab2_words, tab2_scales, "e4m3")[:, unstriped(offs2)]
    w2 = unpack_weight(w2_words, w2_scales, "e2m1")
    b = w2.T @ v2
    d = np.sqrt(np.exp(a) + np.square(b))
    z = f64(gain)[:, None] * (b / d)
    return mxq(f64(w3), 0, "e4m3").T @ mxq(z, 0, "e4m3")

@@ -1,0 +1,318 @@
+from contextlib import ExitStack
+
+import concourse.mybir as mybir
+from concourse.masks import make_identity
+
+K, T, S, T2, M, H, N = 1024, 4096, 1024, 2048, 512, 1024, 512
+FLOPS = 2 * K * H * S + 2 * K * H * M + 2 * H * N * M
+
+F32 = mybir.dt.float32
+BF16 = mybir.dt.bfloat16
+I32 = mybir.dt.int32
+U32 = mybir.dt.uint32
+U16 = mybir.dt.uint16
+U8 = mybir.dt.uint8
+FP8X4 = mybir.dt.float8_e4m3fn_x4
+FP4X4 = mybir.dt.float4_e2m1fn_x4
+ACT = mybir.ActivationFunctionType
+MULT = mybir.AluOpType.mult
+
+P = 128
+PACK = 4
+PASS = P * PACK
+BANK = 512
+HALF = M // 2
+
+
+def tile_list_wavelet_tree_contexts_kernel(
+    tc, tab_words, tab_scales, offs, w1, pos1, tab2_words, tab2_scales, offs2, w2_words, w2_scales, gain, w3, out
+):
+    nc = tc.nc
+    with ExitStack() as ctx:
+        lists = ctx.enter_context(tc.tile_pool(name="lists", bufs=1))
+        keep = ctx.enter_context(tc.tile_pool(name="keep", bufs=1))
+        psum = ctx.enter_context(tc.psum_pool(name="psum", bufs=1))
+
+        def held(name, shape, dtype, after=None):
+            return keep.tile(shape, dtype, name=name, tag=after or name, align_bytes=64)
+
+        def ring(tag, name, shape, dtype, bufs):
+            return keep.tile(shape, dtype, name=name, tag=tag, bufs=bufs, align_bytes=64)
+
+        banks = []
+
+        def bank(name):
+            banks.append(psum.tile([P, BANK], F32, name=name, tag=f"bank{len(banks) % 8}"))
+            return banks[-1]
+
+        def copy_on(engine, dst, src):
+            if engine == "vector":
+                nc.vector.tensor_copy(out=dst, in_=src)
+            else:
+                nc.scalar.copy(out=dst, in_=src)
+
+        idx = lists.tile([P, S // 16], U16, name="idx")
+        idx2 = lists.tile([P, M // 16], U16, name="idx2")
+        parent = lists.tile([P, M // 16], U16, name="parent")
+
+        def load_scale_rows(name, src, width, first):
+            rows = held(name, [P, width], U8)
+            nc.sync.dma_start(
+                out=rows[first : first + 32, :].bitcast(I32), in_=src.bitcast(I32).rearrange("a q c -> q a c")
+            )
+            return rows
+
+        def load_words(name, src, a, width):
+            words = held(name, [P, width], U32)
+            nc.sync.dma_start(out=words[:].bitcast(I32), in_=src[a].rearrange("p c i -> p (c i)").bitcast(I32))
+            return words
+
+        def load_w1(a, b):
+            raw = ring("raw", f"w1_raw{a}{b}", [P, PACK, PASS], F32, 4)
+            nc.sync.dma_start(
+                out=raw[:],
+                in_=w1[a * PASS : (a + 1) * PASS, b * PASS : (b + 1) * PASS].rearrange("(p j) c -> p j c", j=PACK),
+            )
+            return raw
+
+        w1_raw = {}
+        nc.sync.dma_start(idx[:], offs)
+        tab_s = load_scale_rows("tab_s", tab_scales, T, 0)
+        w1_raw[0, 0] = load_w1(0, 0)
+        tab_w = [load_words("tab_w0", tab_words, 0, T)]
+        nc.sync.dma_start(idx2[:], offs2)
+        tab2_s = load_scale_rows("tab2_s", tab2_scales, T2, 64)
+        w2_s_raw = load_scale_rows("w2_s_raw", w2_scales, H, 0)
+        w1_raw[1, 0] = load_w1(1, 0)
+        tab_w.append(load_words("tab_w1", tab_words, 1, T))
+        nc.sync.dma_start(parent[:], pos1)
+        w1_raw[0, 1] = load_w1(0, 1)
+        w1_raw[1, 1] = load_w1(1, 1)
+        w2_w_raw = held("w2_w_raw", [P, 2, H // 2], I32)
+        nc.sync.dma_start(out=w2_w_raw[:], in_=w2_words.bitcast(I32).rearrange("a p c -> p a c"))
+        tab2_w = [load_words(f"tab2_w{a}", tab2_words, a, T2) for a in range(2)]
+        w3_raw = []
+        for b in range(2):
+            raw = ring("raw", f"w3_raw{b}", [P, PACK, N], F32, 4)
+            rows = w3[b * PASS : (b + 1) * PASS, :].rearrange("(g t i) n -> t g i n", t=PACK, i=8)
+            for t in range(PACK):
+                nc.sync.dma_start(out=raw[:, t, :], in_=rows[t])
+            w3_raw.append(raw)
+
+        for rows, spans in ((tab_s, ((32, 64), (64, P))), (tab2_s, ((0, 64), (96, P)))):
+            for lo, hi in spans:
+                nc.vector.memset(rows[lo:hi, :].bitcast(I32), 0)
+
+        gain_rows = held("gain_rows", [P, P], F32)
+        nc.gpsimd.memset(gain_rows[:], 0.0)
+        for b in range(2):
+            nc.gpsimd.dma_start(
+                out=gain_rows[b * PACK : (b + 1) * PACK, :].rearrange("t (g i) -> t g i", i=8),
+                in_=gain[b * PASS : (b + 1) * PASS].rearrange("(g t i) -> t g i", t=PACK, i=8),
+            )
+        planes = {}
+        for name, width in (("v_s", S), ("v2_s", M), ("w2_s", H)):
+            planes[name] = held(name, [P, 2 * width], U8)
+            nc.vector.memset(planes[name][:].bitcast(I32), 0)
+
+        def to_plane(name, rows, first):
+            plane = planes[name]
+            for q in range(4):
+                nc.gpsimd.dma_start(
+                    out=plane[32 * q : 32 * q + 4, :].bitcast(I32),
+                    in_=rows[first + 8 * q : first + 8 * q + 8, :].bitcast(I32),
+                )
+            return plane
+
+        picked_s = held("picked_s", [P, S], U8)
+        nc.vector.tensor_copy(out=picked_s[:], in_=tab_s[:].indirect(idx[:]))
+        v_s = to_plane("v_s", picked_s, 0)
+        picked2_s = held("picked2_s", [P, M], U8)
+        nc.vector.tensor_copy(out=picked2_s[:], in_=tab2_s[:].indirect(idx2[:]))
+        v2_s = to_plane("v2_s", picked2_s, 64)
+        w2_s_rows = held("w2_s_rows", [32, H], U8)
+        nc.vector.tensor_copy(
+            out=w2_s_rows[:].bitcast(I32).rearrange("p (b t g w) -> p b t g w", t=PACK, g=16, w=2),
+            in_=w2_s_raw[0:32, :].bitcast(I32).rearrange("p (b g t w) -> p b t g w", t=PACK, g=16, w=2),
+        )
+        w2_s = to_plane("w2_s", w2_s_rows, 0)
+        identity = held("identity", [P, P], F32)
+        make_identity(nc, identity[:])
+
+        def quantise_w1(a, b, engine, after=None):
+            grouped = held(f"w1_g{a}{b}", [P, PASS * PACK], BF16, after)
+            codes = held(f"w1_c{a}{b}", [P, PASS], U32)
+            scales = held(f"w1_s{a}{b}", [P, PASS], U8)
+            dst = grouped[:].rearrange("p (t g h i j) -> p t g h j i", t=PACK, g=16, h=2, i=4)
+            src = w1_raw[a, b][:].rearrange("p j (g t h i) -> p t g h j i", t=PACK, h=2, i=4)
+            for pair in range(2):
+                for t in (2 * pair, 2 * pair + 1):
+                    copy_on(engine, dst[:, t], src[:, t])
+                cols = slice(pair * 2 * P, (pair + 1) * 2 * P)
+                nc.vector.quantize_mx(
+                    out=codes[:, cols].bitcast(FP8X4),
+                    scales=scales[:, cols],
+                    in_=grouped[:, pair * 2 * PASS : (pair + 1) * 2 * PASS],
+                )
+            return codes, scales
+
+        def gather_words(name, window, offsets, width, after=None):
+            picked = held(name, [P, width], U32, after)
+            nc.vector.tensor_copy(out=picked[:], in_=window[:].indirect(offsets))
+            return picked
+
+        w1_q, v_w = {}, {}
+        for a in range(2):
+            w1_q[a, 0] = quantise_w1(a, 0, "scalar")
+            for half in range(2):
+                v_w[a, half] = gather_words(f"v_w{a}{half}", tab_w[a], idx[:, 32 * half : 32 * (half + 1)], BANK)
+        w1_q[0, 1] = quantise_w1(0, 1, "vector", "tab_w1")
+
+        damping = {}
+
+        def first_product(b, t, half):
+            if half == 0:
+                damping[b, t] = held(f"damping{b}{t}", [P, S], F32)
+            acc = bank(f"h{b}{t}{half}")
+            for a in range(2):
+                codes, scales = w1_q[a, b]
+                nc.tensor.matmul_mx(
+                    out=acc[:],
+                    lhsT=codes[:, t * P : (t + 1) * P].bitcast(FP8X4),
+                    lhsT_scale=scales[:, t * P : (t + 1) * P],
+                    rhs=v_w[a, half][:].bitcast(FP8X4),
+                    rhs_scale=v_s[:, a * S + half * BANK : a * S + (half + 1) * BANK],
+                    start=(a == 0),
+                    stop=(a == 1),
+                )
+            nc.scalar.activation(out=damping[b, t][:, half * BANK : (half + 1) * BANK], in_=acc[:], func=ACT.Exp, scale=-0.5)
+
+        def pick(b, t, dst):
+            nc.vector.tensor_copy(out=dst, in_=damping[b, t][:].indirect(parent[:]))
+            return dst
+
+        order = [(0, 0), (1, 0), (0, 1), (1, 1), (2, 0), (2, 1), (3, 0), (3, 1)]
+        picked = {}
+        picked0 = held("picked0", [P, PACK, M], F32)
+        for t, half in order:
+            first_product(0, t, half)
+            if half == 1:
+                picked[0, t] = pick(0, t, picked0[:, t, :])
+            if (t, half) == (0, 1):
+                w1_q[1, 1] = quantise_w1(1, 1, "scalar", "damping00")
+
+        turned = bank("turned")
+        nc.tensor.transpose(turned[:, 0:P], gain_rows[:], identity[:])
+        gains = held("gains", [P, 2 * PACK], F32)
+        nc.scalar.copy(out=gains[:], in_=turned[:, 0 : 2 * PACK])
+        inv_gains = held("inv_gains", [P, 2 * PACK], F32)
+        nc.vector.reciprocal(out=inv_gains[:], in_=gains[:])
+
+        w2_w = held("w2_w", [P, 2 * 2 * H], U8, "damping01")
+        nc.vector.tensor_copy(
+            out=w2_w[:].bitcast(I32).rearrange("p (ab t g w) -> p ab t g w", t=PACK, g=16, w=4),
+            in_=w2_w_raw[:].rearrange("p a (b g t w) -> p (a b) t g w", t=PACK, g=16, w=4),
+        )
+        v2_w = [gather_words(f"v2_w{a}", tab2_w[a], idx2[:], M, f"damping0{2 + a}") for a in range(2)]
+
+        for t, half in order:
+            first_product(1, t, half)
+        picked[1, 0] = pick(1, 0, held("picked10", [P, M], F32)[:])
+
+        def quantise_w3(b, engine, after):
+            grouped = held(f"w3_g{b}", [P, N * PACK], BF16, after)
+            codes = held(f"w3_c{b}", [P, N], U32)
+            scales = held(f"w3_s{b}", [P, N], U8)
+            copy_on(
+                engine,
+                grouped[:].rearrange("p (c i t) -> p c t i", i=4, t=PACK),
+                w3_raw[b][:].rearrange("p t (c i) -> p c t i", i=4),
+            )
+            nc.vector.quantize_mx(out=codes[:].bitcast(FP8X4), scales=scales[:], in_=grouped[:])
+            return codes, scales
+
+        def second_product(b, t, ratio):
+            acc = bank(f"b{b}{t}")
+            for a in range(2):
+                col = ((2 * a + b) * PACK + t) * P
+                nc.tensor.matmul_mx(
+                    out=acc[:],
+                    lhsT=w2_w[:, 2 * col : 2 * (col + P)].bitcast(FP4X4),
+                    lhsT_scale=w2_s[:, col : col + P],
+                    rhs=v2_w[a][:].bitcast(FP8X4),
+                    rhs_scale=v2_s[:, a * M : (a + 1) * M],
+                    start=(a == 0),
+                    stop=(a == 1),
+                )
+            slot = b * PACK + t
+            nc.vector.scalar_tensor_tensor(
+                out=ratio[:, t, :], in0=acc[:], scalar=gains[:, slot : slot + 1], in1=picked[b, t], op0=MULT, op1=MULT
+            )
+
+        def squares(b, ratio):
+            square = held(f"square{b}", [P, PACK, M], F32, "tab_w0")
+            for t in range(PACK):
+                slot = b * PACK + t
+                nc.scalar.activation(
+                    out=square[:, t, :], in_=ratio[:, t, :], func=ACT.Square, scale=inv_gains[:, slot : slot + 1]
+                )
+            norms = []
+            for half in range(2):
+                norm = held(f"norm{b}{half}", [P, PACK, HALF], F32)
+                nc.scalar.activation(
+                    out=norm[:], in_=square[:, :, half * HALF : (half + 1) * HALF], func=ACT.Abs_reciprocal_sqrt, bias=1.0
+                )
+                norms.append(norm)
+            return norms
+
+        def normalise(b, half, ratio, norm):
+            z = held(f"z{b}{half}", [P, HALF * PACK], BF16)
+            nc.vector.tensor_tensor(
+                out=z[:].rearrange("p (c i t) -> p c t i", i=4, t=PACK),
+                in0=ratio[:, :, half * HALF : (half + 1) * HALF].rearrange("p t (c i) -> p c t i", i=4),
+                in1=norm[:].rearrange("p t (c i) -> p c t i", i=4),
+                op=MULT,
+            )
+            codes = held(f"z_c{b}{half}", [P, HALF], U32)
+            scales = held(f"z_s{b}{half}", [P, HALF], U8)
+            nc.vector.quantize_mx(out=codes[:].bitcast(FP8X4), scales=scales[:], in_=z[:])
+            return codes, scales
+
+        w3_q = [quantise_w3(0, "scalar", None)]
+        ratios = [held(f"ratio{b}", [P, PACK, M], F32, f"tab2_w{1 - b}") for b in range(2)]
+        for t in range(PACK):
+            second_product(0, t, ratios[0])
+        norms0 = squares(0, ratios[0])
+        picked1 = held("picked1", [P, PACK - 1, M], F32, "picked0")
+        second_product(1, 0, ratios[1])
+        for t in range(1, PACK):
+            picked[1, t] = pick(1, t, picked1[:, t - 1, :])
+            second_product(1, t, ratios[1])
+        norms1 = squares(1, ratios[1])
+        z_q = {}
+        for half in range(2):
+            z_q[0, half] = normalise(0, half, ratios[0], norms0[half])
+        for half in range(2):
+            z_q[1, half] = normalise(1, half, ratios[1], norms1[half])
+        w3_q.append(quantise_w3(1, "scalar", "z00"))
+
+        out_rows = out.rearrange("(j p) m -> p j m", p=P)
+        for half in range(2):
+            cols = slice(half * HALF, (half + 1) * HALF)
+            for pair, engine in enumerate((("scalar", "scalar"), ("scalar", "vector"))[half]):
+                staged = held(f"staged{half}{pair}", [P, 2, HALF], F32)
+                for j in range(2):
+                    n0 = (2 * pair + j) * P
+                    acc = bank(f"o{half}{pair}{j}")
+                    for b in range(2):
+                        nc.tensor.matmul_mx(
+                            out=acc[:, 0:HALF],
+                            lhsT=w3_q[b][0][:, n0 : n0 + P].bitcast(FP8X4),
+                            lhsT_scale=w3_q[b][1][:, n0 : n0 + P],
+                            rhs=z_q[b, half][0][:].bitcast(FP8X4),
+                            rhs_scale=z_q[b, half][1][:],
+                            start=(b == 0),
+                            stop=(b == 1),
+                        )
+                    copy_on(engine, staged[:, j, :], acc[:, 0:HALF])
+                nc.sync.dma_start(out=out_rows[:, 2 * pair : 2 * pair + 2, cols], in_=staged[:])

@@ -16,12 +16,15 @@ FP8X4 = mybir.dt.float8_e4m3fn_x4
 FP4X4 = mybir.dt.float4_e2m1fn_x4
 ACT = mybir.ActivationFunctionType
 MULT = mybir.AluOpType.mult
+ADD = mybir.AluOpType.add
 
 P = 128
 PACK = 4
 PASS = P * PACK
 BANK = 512
 HALF = M // 2
+ORDER = (2, 3, 0, 1)
+PIECES = (((0, 256), (256, 512)), ((0, 256), (256, 384), (384, 512)))
 
 
 def tile_list_wavelet_tree_contexts_kernel(
@@ -36,14 +39,8 @@ def tile_list_wavelet_tree_contexts_kernel(
         def held(name, shape, dtype, after=None):
             return keep.tile(shape, dtype, name=name, tag=after or name, align_bytes=64)
 
-        def ring(tag, name, shape, dtype, bufs):
-            return keep.tile(shape, dtype, name=name, tag=tag, bufs=bufs, align_bytes=64)
-
-        banks = []
-
-        def bank(name):
-            banks.append(psum.tile([P, BANK], F32, name=name, tag=f"bank{len(banks) % 8}"))
-            return banks[-1]
+        def bank(name, number):
+            return psum.tile([P, BANK], F32, name=name, tag=f"bank{number}")
 
         def copy_on(engine, dst, src):
             if engine == "vector":
@@ -68,7 +65,7 @@ def tile_list_wavelet_tree_contexts_kernel(
             return words
 
         def load_w1(a, b):
-            raw = ring("raw", f"w1_raw{a}{b}", [P, PACK, PASS], F32, 4)
+            raw = held(f"w1_raw{a}{b}", [P, PACK, PASS], F32)
             nc.sync.dma_start(
                 out=raw[:],
                 in_=w1[a * PASS : (a + 1) * PASS, b * PASS : (b + 1) * PASS].rearrange("(p j) c -> p j c", j=PACK),
@@ -83,8 +80,8 @@ def tile_list_wavelet_tree_contexts_kernel(
         nc.sync.dma_start(idx2[:], offs2)
         tab2_s = load_scale_rows("tab2_s", tab2_scales, T2, 64)
         w2_s_raw = load_scale_rows("w2_s_raw", w2_scales, H, 0)
-        w1_raw[1, 0] = load_w1(1, 0)
         tab_w.append(load_words("tab_w1", tab_words, 1, T))
+        w1_raw[1, 0] = load_w1(1, 0)
         nc.sync.dma_start(parent[:], pos1)
         w1_raw[0, 1] = load_w1(0, 1)
         w1_raw[1, 1] = load_w1(1, 1)
@@ -93,7 +90,7 @@ def tile_list_wavelet_tree_contexts_kernel(
         tab2_w = [load_words(f"tab2_w{a}", tab2_words, a, T2) for a in range(2)]
         w3_raw = []
         for b in range(2):
-            raw = ring("raw", f"w3_raw{b}", [P, PACK, N], F32, 4)
+            raw = held(f"w3_raw{b}", [P, PACK, N], F32, f"w1_raw{b}0")
             rows = w3[b * PASS : (b + 1) * PASS, :].rearrange("(g t i) n -> t g i n", t=PACK, i=8)
             for t in range(PACK):
                 nc.sync.dma_start(out=raw[:, t, :], in_=rows[t])
@@ -139,21 +136,17 @@ def tile_list_wavelet_tree_contexts_kernel(
         identity = held("identity", [P, P], F32)
         make_identity(nc, identity[:])
 
-        def quantise_w1(a, b, engine, after=None):
-            grouped = held(f"w1_g{a}{b}", [P, PASS * PACK], BF16, after)
+        def quantise_w1(a, b, engines, after=(None, None)):
             codes = held(f"w1_c{a}{b}", [P, PASS], U32)
             scales = held(f"w1_s{a}{b}", [P, PASS], U8)
-            dst = grouped[:].rearrange("p (t g h i j) -> p t g h j i", t=PACK, g=16, h=2, i=4)
             src = w1_raw[a, b][:].rearrange("p j (g t h i) -> p t g h j i", t=PACK, h=2, i=4)
-            for pair in range(2):
-                for t in (2 * pair, 2 * pair + 1):
-                    copy_on(engine, dst[:, t], src[:, t])
+            for pair in (1, 0):
+                grouped = held(f"w1_g{a}{b}{pair}", [P, 2 * PASS], BF16, after[pair])
+                dst = grouped[:].rearrange("p (u g h i j) -> p u g h j i", u=2, g=16, h=2, i=4)
+                for u in range(2):
+                    copy_on(engines[pair], dst[:, u], src[:, 2 * pair + u])
                 cols = slice(pair * 2 * P, (pair + 1) * 2 * P)
-                nc.vector.quantize_mx(
-                    out=codes[:, cols].bitcast(FP8X4),
-                    scales=scales[:, cols],
-                    in_=grouped[:, pair * 2 * PASS : (pair + 1) * 2 * PASS],
-                )
+                nc.vector.quantize_mx(out=codes[:, cols].bitcast(FP8X4), scales=scales[:, cols], in_=grouped[:])
             return codes, scales
 
         def gather_words(name, window, offsets, width, after=None):
@@ -162,18 +155,18 @@ def tile_list_wavelet_tree_contexts_kernel(
             return picked
 
         w1_q, v_w = {}, {}
+        w1_q[0, 0] = quantise_w1(0, 0, ("scalar", "scalar"))
         for a in range(2):
-            w1_q[a, 0] = quantise_w1(a, 0, "scalar")
             for half in range(2):
                 v_w[a, half] = gather_words(f"v_w{a}{half}", tab_w[a], idx[:, 32 * half : 32 * (half + 1)], BANK)
-        w1_q[0, 1] = quantise_w1(0, 1, "vector", "tab_w1")
+        w1_q[1, 0] = quantise_w1(1, 0, ("scalar", "vector"))
 
         damping = {}
 
-        def first_product(b, t, half):
+        def first_product(b, t, half, number):
             if half == 0:
                 damping[b, t] = held(f"damping{b}{t}", [P, S], F32)
-            acc = bank(f"h{b}{t}{half}")
+            acc = bank(f"h{b}{t}{half}", number)
             for a in range(2):
                 codes, scales = w1_q[a, b]
                 nc.tensor.matmul_mx(
@@ -191,48 +184,53 @@ def tile_list_wavelet_tree_contexts_kernel(
             nc.vector.tensor_copy(out=dst, in_=damping[b, t][:].indirect(parent[:]))
             return dst
 
-        order = [(0, 0), (1, 0), (0, 1), (1, 1), (2, 0), (2, 1), (3, 0), (3, 1)]
         picked = {}
-        picked0 = held("picked0", [P, PACK, M], F32)
-        for t, half in order:
-            first_product(0, t, half)
-            if half == 1:
-                picked[0, t] = pick(0, t, picked0[:, t, :])
-            if (t, half) == (0, 1):
-                w1_q[1, 1] = quantise_w1(1, 1, "scalar", "damping00")
+        first0 = held("picked_first", [P, M], F32)
+        middle0 = held("picked_middle", [P, 2, M], F32)
+        last0 = held("picked_last", [P, M], F32)
+        for place, (t, dst) in enumerate(zip(ORDER, (first0[:], middle0[:, 0, :], middle0[:, 1, :], last0[:]))):
+            for half in range(2):
+                first_product(0, t, half, 2 * place + half)
+            picked[0, t] = pick(0, t, dst)
+        w1_q[0, 1] = quantise_w1(0, 1, ("scalar", "vector"), ("damping02", None))
+        w1_q[1, 1] = quantise_w1(1, 1, ("scalar", "scalar"))
 
-        turned = bank("turned")
+        turned = bank("turned", 4)
         nc.tensor.transpose(turned[:, 0:P], gain_rows[:], identity[:])
         gains = held("gains", [P, 2 * PACK], F32)
         nc.scalar.copy(out=gains[:], in_=turned[:, 0 : 2 * PACK])
-        inv_gains = held("inv_gains", [P, 2 * PACK], F32)
-        nc.vector.reciprocal(out=inv_gains[:], in_=gains[:])
+        gains_squared = held("gains_squared", [P, 2 * PACK], F32)
+        nc.scalar.activation(out=gains_squared[:], in_=gains[:], func=ACT.Square)
 
-        w2_w = held("w2_w", [P, 2 * 2 * H], U8, "damping01")
+        w2_w = held("w2_w", [P, 2 * 2 * H], U8, "damping03")
         nc.vector.tensor_copy(
             out=w2_w[:].bitcast(I32).rearrange("p (ab t g w) -> p ab t g w", t=PACK, g=16, w=4),
             in_=w2_w_raw[:].rearrange("p a (b g t w) -> p (a b) t g w", t=PACK, g=16, w=4),
         )
-        v2_w = [gather_words(f"v2_w{a}", tab2_w[a], idx2[:], M, f"damping0{2 + a}") for a in range(2)]
+        v2_w = [gather_words(f"v2_w{a}", tab2_w[a], idx2[:], M, f"damping0{a}") for a in range(2)]
 
-        for t, half in order:
-            first_product(1, t, half)
-        picked[1, 0] = pick(1, 0, held("picked10", [P, M], F32)[:])
+        for place, t in enumerate(ORDER):
+            for half in range(2):
+                first_product(1, t, half, (2 * place + half) % 4)
 
-        def quantise_w3(b, engine, after):
+        def quantise_w3(b, after):
             grouped = held(f"w3_g{b}", [P, N * PACK], BF16, after)
             codes = held(f"w3_c{b}", [P, N], U32)
             scales = held(f"w3_s{b}", [P, N], U8)
-            copy_on(
-                engine,
-                grouped[:].rearrange("p (c i t) -> p c t i", i=4, t=PACK),
-                w3_raw[b][:].rearrange("p t (c i) -> p c t i", i=4),
-            )
+            for n0 in range(0, N, P):
+                nc.gpsimd.tensor_scalar(
+                    out=grouped[:, n0 * PACK : (n0 + P) * PACK].rearrange("p (n t) -> p n t", t=PACK),
+                    in0=w3_raw[b][:, :, n0 : n0 + P].rearrange("p t n -> p n t"),
+                    scalar1=1.0,
+                    scalar2=0.0,
+                    op0=MULT,
+                    op1=ADD,
+                )
             nc.vector.quantize_mx(out=codes[:].bitcast(FP8X4), scales=scales[:], in_=grouped[:])
             return codes, scales
 
         def second_product(b, t, ratio):
-            acc = bank(f"b{b}{t}")
+            acc = bank(f"b{b}{t}", 4 + ORDER.index(t))
             for a in range(2):
                 col = ((2 * a + b) * PACK + t) * P
                 nc.tensor.matmul_mx(
@@ -249,70 +247,73 @@ def tile_list_wavelet_tree_contexts_kernel(
                 out=ratio[:, t, :], in0=acc[:], scalar=gains[:, slot : slot + 1], in1=picked[b, t], op0=MULT, op1=MULT
             )
 
-        def squares(b, ratio):
-            square = held(f"square{b}", [P, PACK, M], F32, "tab_w0")
-            for t in range(PACK):
+        def squares(b, ratio, after):
+            square = held(f"square{b}", [P, PACK, M], F32, after)
+            for t in ORDER:
                 slot = b * PACK + t
                 nc.scalar.activation(
                     out=square[:, t, :], in_=ratio[:, t, :], func=ACT.Square, scale=inv_gains[:, slot : slot + 1]
                 )
             norms = []
-            for half in range(2):
-                norm = held(f"norm{b}{half}", [P, PACK, HALF], F32)
-                nc.scalar.activation(
-                    out=norm[:], in_=square[:, :, half * HALF : (half + 1) * HALF], func=ACT.Abs_reciprocal_sqrt, bias=1.0
-                )
+            for lo, hi in PIECES[b]:
+                norm = held(f"norm{b}{lo}", [P, PACK, hi - lo], F32)
+                nc.scalar.activation(out=norm[:], in_=square[:, :, lo:hi], func=ACT.Abs_reciprocal_sqrt, bias=1.0)
                 norms.append(norm)
             return norms
 
-        def normalise(b, half, ratio, norm):
-            z = held(f"z{b}{half}", [P, HALF * PACK], BF16)
+        def normalise(b, lo, hi, ratio, norm):
+            z = held(f"z{b}{lo}", [P, (hi - lo) * PACK], BF16)
             nc.vector.tensor_tensor(
                 out=z[:].rearrange("p (c i t) -> p c t i", i=4, t=PACK),
-                in0=ratio[:, :, half * HALF : (half + 1) * HALF].rearrange("p t (c i) -> p c t i", i=4),
+                in0=ratio[:, :, lo:hi].rearrange("p t (c i) -> p c t i", i=4),
                 in1=norm[:].rearrange("p t (c i) -> p c t i", i=4),
                 op=MULT,
             )
-            codes = held(f"z_c{b}{half}", [P, HALF], U32)
-            scales = held(f"z_s{b}{half}", [P, HALF], U8)
+            codes = held(f"z_c{b}{lo}", [P, hi - lo], U32)
+            scales = held(f"z_s{b}{lo}", [P, hi - lo], U8)
             nc.vector.quantize_mx(out=codes[:].bitcast(FP8X4), scales=scales[:], in_=z[:])
-            return codes, scales
+            return lo, hi, codes, scales
 
-        w3_q = [quantise_w3(0, "scalar", None)]
-        ratios = [held(f"ratio{b}", [P, PACK, M], F32, f"tab2_w{1 - b}") for b in range(2)]
-        for t in range(PACK):
+        inv_gains = held("inv_gains", [P, 2 * PACK], F32, "w1_c11")
+        nc.scalar.activation(out=inv_gains[:], in_=gains_squared[:], func=ACT.Abs_reciprocal_sqrt)
+        ratios = [held("ratio0", [P, PACK, M], F32)]
+        for t in ORDER:
             second_product(0, t, ratios[0])
-        norms0 = squares(0, ratios[0])
-        picked1 = held("picked1", [P, PACK - 1, M], F32, "picked0")
-        second_product(1, 0, ratios[1])
-        for t in range(1, PACK):
-            picked[1, t] = pick(1, t, picked1[:, t - 1, :])
+        norms0 = squares(0, ratios[0], "tab_w0")
+        first1 = held("picked_first1", [P, M], F32, "picked_last")
+        rest1 = held("picked_rest1", [P, PACK - 1, M], F32, "picked_middle")
+        for t, dst in zip(ORDER, (first1[:], rest1[:, 0, :], rest1[:, 1, :], rest1[:, 2, :])):
+            picked[1, t] = pick(1, t, dst)
+        ratios.append(held("ratio1", [P, PACK, M], F32, f"damping1{ORDER[-1]}"))
+        for t in ORDER:
             second_product(1, t, ratios[1])
-        norms1 = squares(1, ratios[1])
-        z_q = {}
-        for half in range(2):
-            z_q[0, half] = normalise(0, half, ratios[0], norms0[half])
-        for half in range(2):
-            z_q[1, half] = normalise(1, half, ratios[1], norms1[half])
-        w3_q.append(quantise_w3(1, "scalar", "z00"))
+        norms1 = squares(1, ratios[1], "tab_w0")
+        w3_q = [quantise_w3(0, "picked_first"), quantise_w3(1, "picked_last")]
+        z_q = []
+        for b, norms in enumerate((norms0, norms1)):
+            z_q.append([normalise(b, lo, hi, ratios[b], norm) for (lo, hi), norm in zip(PIECES[b], norms)])
+
+        def z_columns(b, lo, hi):
+            first, codes, scales = [(x, c, s) for x, y, c, s in z_q[b] if x <= lo and hi <= y][0]
+            return codes[:, lo - first : hi - first], scales[:, lo - first : hi - first]
 
         out_rows = out.rearrange("(j p) m -> p j m", p=P)
-        for half in range(2):
-            cols = slice(half * HALF, (half + 1) * HALF)
-            for pair, engine in enumerate((("scalar", "scalar"), ("scalar", "vector"))[half]):
-                staged = held(f"staged{half}{pair}", [P, 2, HALF], F32)
+        for piece, (lo, hi) in enumerate(PIECES[1]):
+            for pair, engine in enumerate(("scalar", "vector" if hi == M else "scalar")):
+                staged = held(f"staged{lo}{pair}", [P, 2, hi - lo], F32)
                 for j in range(2):
                     n0 = (2 * pair + j) * P
-                    acc = bank(f"o{half}{pair}{j}")
+                    acc = bank(f"o{lo}{pair}{j}", 4 * (piece % 2) + 2 * pair + j)
                     for b in range(2):
+                        codes, scales = z_columns(b, lo, hi)
                         nc.tensor.matmul_mx(
-                            out=acc[:, 0:HALF],
+                            out=acc[:, 0 : hi - lo],
                             lhsT=w3_q[b][0][:, n0 : n0 + P].bitcast(FP8X4),
                             lhsT_scale=w3_q[b][1][:, n0 : n0 + P],
-                            rhs=z_q[b, half][0][:].bitcast(FP8X4),
-                            rhs_scale=z_q[b, half][1][:],
+                            rhs=codes.bitcast(FP8X4),
+                            rhs_scale=scales,
                             start=(b == 0),
                             stop=(b == 1),
                         )
-                    copy_on(engine, staged[:, j, :], acc[:, 0:HALF])
-                nc.sync.dma_start(out=out_rows[:, 2 * pair : 2 * pair + 2, cols], in_=staged[:])
+                    copy_on(engine, staged[:, j, :], acc[:, 0 : hi - lo])
+                nc.sync.dma_start(out=out_rows[:, 2 * pair : 2 * pair + 2, lo:hi], in_=staged[:])

@@ -24,7 +24,7 @@ PASS = P * PACK
 BANK = 512
 HALF = M // 2
 ORDER = (2, 3, 0, 1)
-PIECES = (((0, 256), (256, 512)), ((0, 256), (256, 384), (384, 512)))
+PIECES = (((0, 512),), ((0, 256), (256, 384), (384, 512)))
 
 
 def tile_list_wavelet_tree_contexts_kernel(
@@ -213,19 +213,25 @@ def tile_list_wavelet_tree_contexts_kernel(
             for half in range(2):
                 first_product(1, t, half, (2 * place + half) % 4)
 
-        def quantise_w3(b, after):
+        def quantise_w3(b, engine, after):
             grouped = held(f"w3_g{b}", [P, N * PACK], BF16, after)
             codes = held(f"w3_c{b}", [P, N], U32)
             scales = held(f"w3_s{b}", [P, N], U8)
-            for n0 in range(0, N, P):
-                nc.gpsimd.tensor_scalar(
-                    out=grouped[:, n0 * PACK : (n0 + P) * PACK].rearrange("p (n t) -> p n t", t=PACK),
-                    in0=w3_raw[b][:, :, n0 : n0 + P].rearrange("p t n -> p n t"),
-                    scalar1=1.0,
-                    scalar2=0.0,
-                    op0=MULT,
-                    op1=ADD,
+            if engine == "scalar":
+                nc.scalar.copy(
+                    out=grouped[:].rearrange("p (c i t) -> p c t i", i=4, t=PACK),
+                    in_=w3_raw[b][:].rearrange("p t (c i) -> p c t i", i=4),
                 )
+            else:
+                for n0 in range(0, N, P):
+                    nc.gpsimd.tensor_scalar(
+                        out=grouped[:, n0 * PACK : (n0 + P) * PACK].rearrange("p (n t) -> p n t", t=PACK),
+                        in0=w3_raw[b][:, :, n0 : n0 + P].rearrange("p t n -> p n t"),
+                        scalar1=1.0,
+                        scalar2=0.0,
+                        op0=MULT,
+                        op1=ADD,
+                    )
             nc.vector.quantize_mx(out=codes[:].bitcast(FP8X4), scales=scales[:], in_=grouped[:])
             return codes, scales
 
@@ -287,8 +293,8 @@ def tile_list_wavelet_tree_contexts_kernel(
         ratios.append(held("ratio1", [P, PACK, M], F32, f"damping1{ORDER[-1]}"))
         for t in ORDER:
             second_product(1, t, ratios[1])
-        norms1 = squares(1, ratios[1], "tab_w0")
-        w3_q = [quantise_w3(0, "picked_first"), quantise_w3(1, "picked_last")]
+        w3_q = [quantise_w3(0, "gpsimd", "picked_first"), quantise_w3(1, "scalar", "tab_w0")]
+        norms1 = squares(1, ratios[1], "w1_raw10")
         z_q = []
         for b, norms in enumerate((norms0, norms1)):
             z_q.append([normalise(b, lo, hi, ratios[b], norm) for (lo, hi), norm in zip(PIECES[b], norms)])

@@ -22,9 +22,7 @@ P = 128
 PACK = 4
 PASS = P * PACK
 BANK = 512
-HALF = M // 2
-ORDER = (2, 3, 0, 1)
-PIECES = (((0, 512),), ((0, 256), (256, 384), (384, 512)))
+PIECES = ((0, 256), (256, 384), (384, 512))
 
 
 def tile_list_wavelet_tree_contexts_kernel(
@@ -42,12 +40,6 @@ def tile_list_wavelet_tree_contexts_kernel(
         def bank(name, number):
             return psum.tile([P, BANK], F32, name=name, tag=f"bank{number}")
 
-        def copy_on(engine, dst, src):
-            if engine == "vector":
-                nc.vector.tensor_copy(out=dst, in_=src)
-            else:
-                nc.scalar.copy(out=dst, in_=src)
-
         idx = lists.tile([P, S // 16], U16, name="idx")
         idx2 = lists.tile([P, M // 16], U16, name="idx2")
         parent = lists.tile([P, M // 16], U16, name="parent")
@@ -59,43 +51,70 @@ def tile_list_wavelet_tree_contexts_kernel(
             )
             return rows
 
-        def load_words(name, src, a, width):
-            words = held(name, [P, width], U32)
-            nc.sync.dma_start(out=words[:].bitcast(I32), in_=src[a].rearrange("p c i -> p (c i)").bitcast(I32))
-            return words
+        def load_words(dst, src, a):
+            nc.sync.dma_start(out=dst.bitcast(I32), in_=src[a].rearrange("p c i -> p (c i)").bitcast(I32))
 
-        def load_w1(a, b):
-            raw = held(f"w1_raw{a}{b}", [P, PACK, PASS], F32)
+        def load_w1(a, b, after=None):
+            raw = held(f"w1_raw{a}{b}", [P, PACK, PASS], F32, after)
             nc.sync.dma_start(
                 out=raw[:],
                 in_=w1[a * PASS : (a + 1) * PASS, b * PASS : (b + 1) * PASS].rearrange("(p j) c -> p j c", j=PACK),
             )
             return raw
 
-        w1_raw = {}
+        def to_plane(queue, name, rows, first, width):
+            plane = held(name, [P, 2 * width], U8)
+            nc.vector.memset(plane[:].bitcast(I32), 0)
+            for q in range(4):
+                queue.dma_start(
+                    out=plane[32 * q : 32 * q + 4, :].bitcast(I32),
+                    in_=rows[first + 8 * q : first + 8 * q + 8, :].bitcast(I32),
+                )
+            return plane
+
+        def gather(name, dtype, window, offsets, width, after=None):
+            picked = held(name, [P, width], dtype, after)
+            nc.vector.tensor_copy(out=picked[:], in_=window.indirect(offsets))
+            return picked
+
+        def quantise_w1(a, b, raw, engines, widths):
+            codes = held(f"w1_c{a}{b}", [P, PASS], U32)
+            scales = held(f"w1_s{a}{b}", [P, PASS], U8)
+            t0 = 0
+            for width in widths:
+                grouped = held(f"w1_g{a}{b}{t0}", [P, width * PASS], BF16)
+                for u in range(width):
+                    t = t0 + u
+                    dst = grouped[:, u * PASS : (u + 1) * PASS]
+                    if engines[t] == "gpsimd":
+                        nc.gpsimd.tensor_scalar(
+                            out=dst.rearrange("p (g i j) -> p g i j", g=16, j=PACK),
+                            in0=raw[:].rearrange("p j (g t i) -> p t g i j", t=PACK, i=8)[:, t],
+                            scalar1=1.0,
+                            scalar2=0.0,
+                            op0=MULT,
+                            op1=ADD,
+                        )
+                    else:
+                        dst = dst.rearrange("p (g h i j) -> p g h j i", g=16, h=2, i=4)
+                        src = raw[:].rearrange("p j (g t h i) -> p t g h j i", t=PACK, h=2, i=4)[:, t]
+                        if engines[t] == "vector":
+                            nc.vector.tensor_copy(out=dst, in_=src)
+                        else:
+                            nc.scalar.copy(out=dst, in_=src)
+                cols = slice(t0 * P, (t0 + width) * P)
+                nc.vector.quantize_mx(out=codes[:, cols].bitcast(FP8X4), scales=scales[:, cols], in_=grouped[:])
+                t0 = t0 + width
+            return codes, scales
+
         nc.sync.dma_start(idx[:], offs)
         tab_s = load_scale_rows("tab_s", tab_scales, T, 0)
-        w1_raw[0, 0] = load_w1(0, 0)
-        tab_w = [load_words("tab_w0", tab_words, 0, T)]
         nc.sync.dma_start(idx2[:], offs2)
         tab2_s = load_scale_rows("tab2_s", tab2_scales, T2, 64)
-        w2_s_raw = load_scale_rows("w2_s_raw", w2_scales, H, 0)
-        tab_w.append(load_words("tab_w1", tab_words, 1, T))
-        w1_raw[1, 0] = load_w1(1, 0)
+        w1_raw = {(0, 0): load_w1(0, 0)}
+        tab_w0 = held("tab_w0", [P, T], U32)
+        load_words(tab_w0[:], tab_words, 0)
         nc.sync.dma_start(parent[:], pos1)
-        w1_raw[0, 1] = load_w1(0, 1)
-        w1_raw[1, 1] = load_w1(1, 1)
-        w2_w_raw = held("w2_w_raw", [P, 2, H // 2], I32)
-        nc.sync.dma_start(out=w2_w_raw[:], in_=w2_words.bitcast(I32).rearrange("a p c -> p a c"))
-        tab2_w = [load_words(f"tab2_w{a}", tab2_words, a, T2) for a in range(2)]
-        w3_raw = []
-        for b in range(2):
-            raw = held(f"w3_raw{b}", [P, PACK, N], F32, f"w1_raw{b}0")
-            rows = w3[b * PASS : (b + 1) * PASS, :].rearrange("(g t i) n -> t g i n", t=PACK, i=8)
-            for t in range(PACK):
-                nc.sync.dma_start(out=raw[:, t, :], in_=rows[t])
-            w3_raw.append(raw)
-
         for rows, spans in ((tab_s, ((32, 64), (64, P))), (tab2_s, ((0, 64), (96, P)))):
             for lo, hi in spans:
                 nc.vector.memset(rows[lo:hi, :].bitcast(I32), 0)
@@ -107,219 +126,208 @@ def tile_list_wavelet_tree_contexts_kernel(
                 out=gain_rows[b * PACK : (b + 1) * PACK, :].rearrange("t (g i) -> t g i", i=8),
                 in_=gain[b * PASS : (b + 1) * PASS].rearrange("(g t i) -> t g i", t=PACK, i=8),
             )
-        planes = {}
-        for name, width in (("v_s", S), ("v2_s", M), ("w2_s", H)):
-            planes[name] = held(name, [P, 2 * width], U8)
-            nc.vector.memset(planes[name][:].bitcast(I32), 0)
-
-        def to_plane(name, rows, first):
-            plane = planes[name]
-            for q in range(4):
-                nc.gpsimd.dma_start(
-                    out=plane[32 * q : 32 * q + 4, :].bitcast(I32),
-                    in_=rows[first + 8 * q : first + 8 * q + 8, :].bitcast(I32),
-                )
-            return plane
-
-        picked_s = held("picked_s", [P, S], U8)
-        nc.vector.tensor_copy(out=picked_s[:], in_=tab_s[:].indirect(idx[:]))
-        v_s = to_plane("v_s", picked_s, 0)
-        picked2_s = held("picked2_s", [P, M], U8)
-        nc.vector.tensor_copy(out=picked2_s[:], in_=tab2_s[:].indirect(idx2[:]))
-        v2_s = to_plane("v2_s", picked2_s, 64)
-        w2_s_rows = held("w2_s_rows", [32, H], U8)
-        nc.vector.tensor_copy(
-            out=w2_s_rows[:].bitcast(I32).rearrange("p (b t g w) -> p b t g w", t=PACK, g=16, w=2),
-            in_=w2_s_raw[0:32, :].bitcast(I32).rearrange("p (b g t w) -> p b t g w", t=PACK, g=16, w=2),
-        )
-        w2_s = to_plane("w2_s", w2_s_rows, 0)
         identity = held("identity", [P, P], F32)
         make_identity(nc, identity[:])
 
-        def quantise_w1(a, b, engines, after=(None, None)):
-            codes = held(f"w1_c{a}{b}", [P, PASS], U32)
-            scales = held(f"w1_s{a}{b}", [P, PASS], U8)
-            src = w1_raw[a, b][:].rearrange("p j (g t h i) -> p t g h j i", t=PACK, h=2, i=4)
-            for pair in (1, 0):
-                grouped = held(f"w1_g{a}{b}{pair}", [P, 2 * PASS], BF16, after[pair])
-                dst = grouped[:].rearrange("p (u g h i j) -> p u g h j i", u=2, g=16, h=2, i=4)
-                for u in range(2):
-                    copy_on(engines[pair], dst[:, u], src[:, 2 * pair + u])
-                cols = slice(pair * 2 * P, (pair + 1) * 2 * P)
-                nc.vector.quantize_mx(out=codes[:, cols].bitcast(FP8X4), scales=scales[:, cols], in_=grouped[:])
-            return codes, scales
+        picked_s = gather("picked_s", U8, tab_s[:], idx[:], S)
+        v_s = to_plane(nc.sync, "v_s", picked_s, 0, S)
+        tab_w1 = held("tab_w1", [P, T], U32, "tab_s")
+        load_words(tab_w1[:], tab_words, 1)
 
-        def gather_words(name, window, offsets, width, after=None):
-            picked = held(name, [P, width], U32, after)
-            nc.vector.tensor_copy(out=picked[:], in_=window[:].indirect(offsets))
-            return picked
+        picked2_s = gather("picked2_s", U8, tab2_s[:], idx2[:], M)
+        v2_s = to_plane(nc.gpsimd, "v2_s", picked2_s, 64, M)
 
-        w1_q, v_w = {}, {}
-        w1_q[0, 0] = quantise_w1(0, 0, ("scalar", "scalar"))
-        for a in range(2):
-            for half in range(2):
-                v_w[a, half] = gather_words(f"v_w{a}{half}", tab_w[a], idx[:, 32 * half : 32 * (half + 1)], BANK)
-        w1_q[1, 0] = quantise_w1(1, 0, ("scalar", "vector"))
-
-        damping = {}
-
-        def first_product(b, t, half, number):
-            if half == 0:
-                damping[b, t] = held(f"damping{b}{t}", [P, S], F32)
-            acc = bank(f"h{b}{t}{half}", number)
-            for a in range(2):
-                codes, scales = w1_q[a, b]
-                nc.tensor.matmul_mx(
-                    out=acc[:],
-                    lhsT=codes[:, t * P : (t + 1) * P].bitcast(FP8X4),
-                    lhsT_scale=scales[:, t * P : (t + 1) * P],
-                    rhs=v_w[a, half][:].bitcast(FP8X4),
-                    rhs_scale=v_s[:, a * S + half * BANK : a * S + (half + 1) * BANK],
-                    start=(a == 0),
-                    stop=(a == 1),
-                )
-            nc.scalar.activation(out=damping[b, t][:, half * BANK : (half + 1) * BANK], in_=acc[:], func=ACT.Exp, scale=-0.5)
-
-        def pick(b, t, dst):
-            nc.vector.tensor_copy(out=dst, in_=damping[b, t][:].indirect(parent[:]))
-            return dst
-
-        picked = {}
-        first0 = held("picked_first", [P, M], F32)
-        middle0 = held("picked_middle", [P, 2, M], F32)
-        last0 = held("picked_last", [P, M], F32)
-        for place, (t, dst) in enumerate(zip(ORDER, (first0[:], middle0[:, 0, :], middle0[:, 1, :], last0[:]))):
-            for half in range(2):
-                first_product(0, t, half, 2 * place + half)
-            picked[0, t] = pick(0, t, dst)
-        w1_q[0, 1] = quantise_w1(0, 1, ("scalar", "vector"), ("damping02", None))
-        w1_q[1, 1] = quantise_w1(1, 1, ("scalar", "scalar"))
-
-        turned = bank("turned", 4)
+        turned = bank("turned", 7)
         nc.tensor.transpose(turned[:, 0:P], gain_rows[:], identity[:])
         gains = held("gains", [P, 2 * PACK], F32)
         nc.scalar.copy(out=gains[:], in_=turned[:, 0 : 2 * PACK])
-        gains_squared = held("gains_squared", [P, 2 * PACK], F32)
-        nc.scalar.activation(out=gains_squared[:], in_=gains[:], func=ACT.Square)
+        inv_gains = held("inv_gains", [P, 2 * PACK], F32)
+        nc.vector.reciprocal(out=inv_gains[:], in_=gains[:])
 
-        w2_w = held("w2_w", [P, 2 * 2 * H], U8, "damping03")
+        w1_q = {(0, 0): quantise_w1(0, 0, w1_raw[0, 0], ("scalar",) * 4, (2, 2))}
+        w1_raw[1, 0] = load_w1(1, 0, "w1_g000")
+        w1_raw[0, 1] = load_w1(0, 1, "w1_raw00")
+        w1_raw[1, 1] = load_w1(1, 1, "w1_g002")
+        w2_s_raw = held("w2_s_raw", [P, 2 * H], U8, "tab2_s")
+        nc.gpsimd.memset(w2_s_raw[:].bitcast(I32), 0)
+        for q in range(4):
+            nc.sync.dma_start(
+                out=w2_s_raw[32 * q : 32 * q + 4, :].bitcast(I32).rearrange("r (a c) -> r a c", a=2),
+                in_=w2_scales.bitcast(I32)[:, 4 * q : 4 * q + 4, :].rearrange("a r c -> r a c"),
+            )
+        w2_w_raw = held("w2_w_raw", [P, 2, H // 2], I32, "picked_s")
+        nc.sync.dma_start(out=w2_w_raw[:], in_=w2_words.bitcast(I32).rearrange("a p c -> p a c"))
+
+        v_w = {}
+        for half in range(2):
+            v_w[0, half] = gather(f"v_w0{half}", U32, tab_w0[:], idx[:, 32 * half : 32 * (half + 1)], BANK)
+        tab2_w = held("tab2_w", [P, 2 * T2], U32, "tab_w0")
+        for a in range(2):
+            load_words(tab2_w[:, a * T2 : (a + 1) * T2], tab2_words, a)
+
+        for half in range(2):
+            v_w[1, half] = gather(f"v_w1{half}", U32, tab_w1[:], idx[:, 32 * half : 32 * (half + 1)], BANK)
+
+        def load_w3(b, after):
+            raw = held(f"w3_raw{b}", [P, PACK * N], F32, after)
+            rows = w3[b * PASS : (b + 1) * PASS, :].rearrange("(g t i) n -> t g i n", t=PACK, i=8)
+            for t in range(PACK):
+                nc.sync.dma_start(out=raw[:, t * N : (t + 1) * N], in_=rows[t])
+            return raw
+
+        damping = {}
+
+        def first_pass(acc, a, b, t, half):
+            codes, scales = w1_q[a, b]
+            nc.tensor.matmul_mx(
+                out=acc[:],
+                lhsT=codes[:, t * P : (t + 1) * P].bitcast(FP8X4),
+                lhsT_scale=scales[:, t * P : (t + 1) * P],
+                rhs=v_w[a, half][:].bitcast(FP8X4),
+                rhs_scale=v_s[:, a * S + half * BANK : a * S + (half + 1) * BANK],
+                start=(a == 0),
+                stop=(a == 1),
+            )
+
+        def first_product(b, banks):
+            together = len(banks) // 2
+            for t0 in range(0, PACK, together):
+                accs = {}
+                for t in range(t0, t0 + together):
+                    for half in range(2):
+                        accs[t, half] = bank(f"h{b}{t}{half}", banks[2 * (t - t0) + half])
+                        first_pass(accs[t, half], 0, b, t, half)
+                for t in range(t0, t0 + together):
+                    damping[b, t] = held(f"damping{b}{t}", [P, S], F32)
+                    for half in range(2):
+                        first_pass(accs[t, half], 1, b, t, half)
+                        nc.scalar.activation(
+                            out=damping[b, t][:, half * BANK : (half + 1) * BANK],
+                            in_=accs[t, half][:],
+                            func=ACT.Exp,
+                            scale=-0.5,
+                        )
+
+        def picks(b):
+            return [gather(f"picked{b}{t}", F32, damping[b, t][:], parent[:], M, f"picked{t}" if t else None) for t in range(PACK)]
+
+        w1_q[1, 0] = quantise_w1(1, 0, w1_raw[1, 0], ("vector", "scalar", "vector", "scalar"), (1, 1, 2))
+        w3_raw = [load_w3(0, "tab_s"), load_w3(1, "w1_g000")]
+        first_product(0, range(8))
+        w1_q[0, 1] = quantise_w1(0, 1, w1_raw[0, 1], ("gpsimd",) * 4, (2, 2))
+        w1_q[1, 1] = quantise_w1(1, 1, w1_raw[1, 1], ("gpsimd", "gpsimd", "scalar", "scalar"), (2, 2))
+        picked = [picks(0)]
+        first_product(1, range(4, 8))
+
+        w2_s = held("w2_s", [P, 2 * H], U8)
+        nc.vector.tensor_copy(
+            out=w2_s[:].bitcast(I32).rearrange("p (ab t g w) -> p ab t g w", t=PACK, g=16, w=2),
+            in_=w2_s_raw[:].bitcast(I32).rearrange("p (ab g t w) -> p ab t g w", t=PACK, g=16, w=2),
+        )
+        w2_w = held("w2_w", [P, 2 * 2 * H], U8)
         nc.vector.tensor_copy(
             out=w2_w[:].bitcast(I32).rearrange("p (ab t g w) -> p ab t g w", t=PACK, g=16, w=4),
             in_=w2_w_raw[:].rearrange("p a (b g t w) -> p (a b) t g w", t=PACK, g=16, w=4),
         )
-        v2_w = [gather_words(f"v2_w{a}", tab2_w[a], idx2[:], M, f"damping0{a}") for a in range(2)]
+        v2_w = [gather(f"v2_w{a}", U32, tab2_w[:, a * T2 : (a + 1) * T2], idx2[:], M) for a in range(2)]
 
-        for place, t in enumerate(ORDER):
-            for half in range(2):
-                first_product(1, t, half, (2 * place + half) % 4)
-
-        def quantise_w3(b, engine, after):
-            grouped = held(f"w3_g{b}", [P, N * PACK], BF16, after)
-            codes = held(f"w3_c{b}", [P, N], U32)
-            scales = held(f"w3_s{b}", [P, N], U8)
-            if engine == "scalar":
-                nc.scalar.copy(
-                    out=grouped[:].rearrange("p (c i t) -> p c t i", i=4, t=PACK),
-                    in_=w3_raw[b][:].rearrange("p t (c i) -> p c t i", i=4),
-                )
-            else:
-                for n0 in range(0, N, P):
-                    nc.gpsimd.tensor_scalar(
-                        out=grouped[:, n0 * PACK : (n0 + P) * PACK].rearrange("p (n t) -> p n t", t=PACK),
-                        in0=w3_raw[b][:, :, n0 : n0 + P].rearrange("p t n -> p n t"),
-                        scalar1=1.0,
-                        scalar2=0.0,
-                        op0=MULT,
-                        op1=ADD,
+        def second_product(b):
+            ratio = held(f"ratio{b}", [P, PACK, M], F32)
+            square = held(f"square{b}", [P, PACK, M], F32, ("w1_raw00", "w1_g002")[b])
+            for t in range(PACK):
+                acc = bank(f"b{b}{t}", t)
+                for a in range(2):
+                    col = ((2 * a + b) * PACK + t) * P
+                    nc.tensor.matmul_mx(
+                        out=acc[:],
+                        lhsT=w2_w[:, 2 * col : 2 * (col + P)].bitcast(FP4X4),
+                        lhsT_scale=w2_s[:, col : col + P],
+                        rhs=v2_w[a][:].bitcast(FP8X4),
+                        rhs_scale=v2_s[:, a * M : (a + 1) * M],
+                        start=(a == 0),
+                        stop=(a == 1),
                     )
-            nc.vector.quantize_mx(out=codes[:].bitcast(FP8X4), scales=scales[:], in_=grouped[:])
-            return codes, scales
-
-        def second_product(b, t, ratio):
-            acc = bank(f"b{b}{t}", 4 + ORDER.index(t))
-            for a in range(2):
-                col = ((2 * a + b) * PACK + t) * P
-                nc.tensor.matmul_mx(
-                    out=acc[:],
-                    lhsT=w2_w[:, 2 * col : 2 * (col + P)].bitcast(FP4X4),
-                    lhsT_scale=w2_s[:, col : col + P],
-                    rhs=v2_w[a][:].bitcast(FP8X4),
-                    rhs_scale=v2_s[:, a * M : (a + 1) * M],
-                    start=(a == 0),
-                    stop=(a == 1),
-                )
-            slot = b * PACK + t
-            nc.vector.scalar_tensor_tensor(
-                out=ratio[:, t, :], in0=acc[:], scalar=gains[:, slot : slot + 1], in1=picked[b, t], op0=MULT, op1=MULT
-            )
-
-        def squares(b, ratio, after):
-            square = held(f"square{b}", [P, PACK, M], F32, after)
-            for t in ORDER:
                 slot = b * PACK + t
+                nc.vector.scalar_tensor_tensor(
+                    out=ratio[:, t, :], in0=acc[:], scalar=gains[:, slot : slot + 1], in1=picked[b][t][:], op0=MULT, op1=MULT
+                )
                 nc.scalar.activation(
                     out=square[:, t, :], in_=ratio[:, t, :], func=ACT.Square, scale=inv_gains[:, slot : slot + 1]
                 )
-            norms = []
-            for lo, hi in PIECES[b]:
-                norm = held(f"norm{b}{lo}", [P, PACK, hi - lo], F32)
-                nc.scalar.activation(out=norm[:], in_=square[:, :, lo:hi], func=ACT.Abs_reciprocal_sqrt, bias=1.0)
-                norms.append(norm)
-            return norms
+            return ratio, square
 
-        def normalise(b, lo, hi, ratio, norm):
-            z = held(f"z{b}{lo}", [P, (hi - lo) * PACK], BF16)
+        def inverse_root(name, square, lo, hi, after=None):
+            norm = held(name, [P, PACK, hi - lo], F32, after)
+            nc.scalar.activation(out=norm[:], in_=square[:, :, lo:hi], func=ACT.Abs_reciprocal_sqrt, bias=1.0)
+            return norm
+
+        def normalise(name, ratio, norm, lo, hi):
+            z = held(name, [P, (hi - lo) * PACK], BF16)
             nc.vector.tensor_tensor(
                 out=z[:].rearrange("p (c i t) -> p c t i", i=4, t=PACK),
                 in0=ratio[:, :, lo:hi].rearrange("p t (c i) -> p c t i", i=4),
                 in1=norm[:].rearrange("p t (c i) -> p c t i", i=4),
                 op=MULT,
             )
-            codes = held(f"z_c{b}{lo}", [P, hi - lo], U32)
-            scales = held(f"z_s{b}{lo}", [P, hi - lo], U8)
+            codes = held(name + "_c", [P, hi - lo], U32)
+            scales = held(name + "_s", [P, hi - lo], U8)
             nc.vector.quantize_mx(out=codes[:].bitcast(FP8X4), scales=scales[:], in_=z[:])
-            return lo, hi, codes, scales
+            return codes, scales
 
-        inv_gains = held("inv_gains", [P, 2 * PACK], F32, "w1_c11")
-        nc.scalar.activation(out=inv_gains[:], in_=gains_squared[:], func=ACT.Abs_reciprocal_sqrt)
-        ratios = [held("ratio0", [P, PACK, M], F32)]
-        for t in ORDER:
-            second_product(0, t, ratios[0])
-        norms0 = squares(0, ratios[0], "tab_w0")
-        first1 = held("picked_first1", [P, M], F32, "picked_last")
-        rest1 = held("picked_rest1", [P, PACK - 1, M], F32, "picked_middle")
-        for t, dst in zip(ORDER, (first1[:], rest1[:, 0, :], rest1[:, 1, :], rest1[:, 2, :])):
-            picked[1, t] = pick(1, t, dst)
-        ratios.append(held("ratio1", [P, PACK, M], F32, f"damping1{ORDER[-1]}"))
-        for t in ORDER:
-            second_product(1, t, ratios[1])
-        w3_q = [quantise_w3(0, "gpsimd", "picked_first"), quantise_w3(1, "scalar", "tab_w0")]
-        norms1 = squares(1, ratios[1], "w1_raw10")
-        z_q = []
-        for b, norms in enumerate((norms0, norms1)):
-            z_q.append([normalise(b, lo, hi, ratios[b], norm) for (lo, hi), norm in zip(PIECES[b], norms)])
+        def quantise_w3(b):
+            grouped = held(f"w3_g{b}", [P, N * PACK], BF16)
+            codes = held(f"w3_c{b}", [P, N], U32)
+            scales = held(f"w3_s{b}", [P, N], U8)
+            raw = w3_raw[b][:].rearrange("p (t n) -> p n t", t=PACK)
+            for n0 in range(0, N, P):
+                nc.gpsimd.tensor_scalar(
+                    out=grouped[:, n0 * PACK : (n0 + P) * PACK].rearrange("p (n t) -> p n t", t=PACK),
+                    in0=raw[:, n0 : n0 + P, :],
+                    scalar1=1.0,
+                    scalar2=0.0,
+                    op0=MULT,
+                    op1=ADD,
+                )
+            nc.vector.quantize_mx(out=codes[:].bitcast(FP8X4), scales=scales[:], in_=grouped[:])
+            return codes, scales
 
-        def z_columns(b, lo, hi):
-            first, codes, scales = [(x, c, s) for x, y, c, s in z_q[b] if x <= lo and hi <= y][0]
-            return codes[:, lo - first : hi - first], scales[:, lo - first : hi - first]
+        ratio0, square0 = second_product(0)
+        norm0 = inverse_root("norm0", square0, 0, M, "w1_c11")
+        picked.append(picks(1))
+        ratio1, square1 = second_product(1)
+        norms1 = [inverse_root(f"norm1{lo}", square1, lo, hi) for lo, hi in PIECES]
+        z0 = normalise("z0", ratio0, norm0, 0, M)
+        w3_q = [quantise_w3(b) for b in range(2)]
+
+        def last_pass(acc, b, z, first, j, place, lo, hi, start, stop):
+            nc.tensor.matmul_mx(
+                out=acc[:, place * (hi - lo) : (place + 1) * (hi - lo)],
+                lhsT=w3_q[b][0][:, j * P : (j + 1) * P].bitcast(FP8X4),
+                lhsT_scale=w3_q[b][1][:, j * P : (j + 1) * P],
+                rhs=z[0][:, lo - first : hi - first].bitcast(FP8X4),
+                rhs_scale=z[1][:, lo - first : hi - first],
+                start=start,
+                stop=stop,
+            )
 
         out_rows = out.rearrange("(j p) m -> p j m", p=P)
-        for piece, (lo, hi) in enumerate(PIECES[1]):
-            for pair, engine in enumerate(("scalar", "vector" if hi == M else "scalar")):
-                staged = held(f"staged{lo}{pair}", [P, 2, hi - lo], F32)
-                for j in range(2):
-                    n0 = (2 * pair + j) * P
-                    acc = bank(f"o{lo}{pair}{j}", 4 * (piece % 2) + 2 * pair + j)
-                    for b in range(2):
-                        codes, scales = z_columns(b, lo, hi)
-                        nc.tensor.matmul_mx(
-                            out=acc[:, 0 : hi - lo],
-                            lhsT=w3_q[b][0][:, n0 : n0 + P].bitcast(FP8X4),
-                            lhsT_scale=w3_q[b][1][:, n0 : n0 + P],
-                            rhs=codes.bitcast(FP8X4),
-                            rhs_scale=scales,
-                            start=(b == 0),
-                            stop=(b == 1),
-                        )
-                    copy_on(engine, staged[:, j, :], acc[:, 0 : hi - lo])
-                nc.sync.dma_start(out=out_rows[:, 2 * pair : 2 * pair + 2, lo:hi], in_=staged[:])
+        accs = {}
+        for piece, (lo, hi) in enumerate(PIECES):
+            for pair in range(2):
+                accs[piece, pair] = bank(f"o{piece}{pair}", (4 + 2 * piece + pair) % 8)
+                for place in range(2):
+                    last_pass(accs[piece, pair], 0, z0, 0, 2 * pair + place, place, lo, hi, place == 0, False)
+        for piece, (lo, hi) in enumerate(PIECES):
+            z1 = normalise(f"z1{lo}", ratio1, norms1[piece], lo, hi)
+            for pair in range(2):
+                acc = accs[piece, pair]
+                for place in range(2):
+                    last_pass(acc, 1, z1, lo, 2 * pair + place, place, lo, hi, False, place == 1)
+                staged = held(f"staged{piece}{pair}", [P, 2 * (hi - lo)], F32)
+                if hi == M and pair == 1:
+                    nc.vector.tensor_copy(out=staged[:], in_=acc[:, 0 : 2 * (hi - lo)])
+                else:
+                    nc.scalar.copy(out=staged[:], in_=acc[:, 0 : 2 * (hi - lo)])
+                nc.sync.dma_start(
+                    out=out_rows[:, 2 * pair : 2 * pair + 2, lo:hi], in_=staged[:].rearrange("p (j m) -> p j m", j=2)
+                )

@@ -16,7 +16,6 @@ FP8X4 = mybir.dt.float8_e4m3fn_x4
 FP4X4 = mybir.dt.float4_e2m1fn_x4
 ACT = mybir.ActivationFunctionType
 MULT = mybir.AluOpType.mult
-ADD = mybir.AluOpType.add
 
 P = 128
 PACK = 4
@@ -77,6 +76,12 @@ def tile_list_wavelet_tree_contexts_kernel(
             nc.vector.tensor_copy(out=picked[:], in_=window.indirect(offsets))
             return picked
 
+        def round_on(engine, dst, src):
+            if engine == "vector":
+                nc.vector.tensor_copy(out=dst, in_=src)
+            else:
+                nc.scalar.copy(out=dst, in_=src)
+
         def quantise_w1(a, b, raw, engines, widths):
             codes = held(f"w1_c{a}{b}", [P, PASS], U32)
             scales = held(f"w1_s{a}{b}", [P, PASS], U8)
@@ -86,22 +91,11 @@ def tile_list_wavelet_tree_contexts_kernel(
                 for u in range(width):
                     t = t0 + u
                     dst = grouped[:, u * PASS : (u + 1) * PASS]
-                    if engines[t] == "gpsimd":
-                        nc.gpsimd.tensor_scalar(
-                            out=dst.rearrange("p (g i j) -> p g i j", g=16, j=PACK),
-                            in0=raw[:].rearrange("p j (g t i) -> p t g i j", t=PACK, i=8)[:, t],
-                            scalar1=1.0,
-                            scalar2=0.0,
-                            op0=MULT,
-                            op1=ADD,
-                        )
-                    else:
-                        dst = dst.rearrange("p (g h i j) -> p g h j i", g=16, h=2, i=4)
-                        src = raw[:].rearrange("p j (g t h i) -> p t g h j i", t=PACK, h=2, i=4)[:, t]
-                        if engines[t] == "vector":
-                            nc.vector.tensor_copy(out=dst, in_=src)
-                        else:
-                            nc.scalar.copy(out=dst, in_=src)
+                    round_on(
+                        engines[t],
+                        dst.rearrange("p (g h i j) -> p g h j i", g=16, h=2, i=4),
+                        raw[:].rearrange("p j (g t h i) -> p t g h j i", t=PACK, h=2, i=4)[:, t],
+                    )
                 cols = slice(t0 * P, (t0 + width) * P)
                 nc.vector.quantize_mx(out=codes[:, cols].bitcast(FP8X4), scales=scales[:, cols], in_=grouped[:])
                 t0 = t0 + width
@@ -214,8 +208,8 @@ def tile_list_wavelet_tree_contexts_kernel(
         w1_q[1, 0] = quantise_w1(1, 0, w1_raw[1, 0], ("vector", "scalar", "vector", "scalar"), (1, 1, 2))
         w3_raw = [load_w3(0, "tab_s"), load_w3(1, "w1_g000")]
         first_product(0, range(8))
-        w1_q[0, 1] = quantise_w1(0, 1, w1_raw[0, 1], ("gpsimd",) * 4, (2, 2))
-        w1_q[1, 1] = quantise_w1(1, 1, w1_raw[1, 1], ("gpsimd", "gpsimd", "scalar", "scalar"), (2, 2))
+        w1_q[0, 1] = quantise_w1(0, 1, w1_raw[0, 1], ("vector",) * 4, (4,))
+        w1_q[1, 1] = quantise_w1(1, 1, w1_raw[1, 1], ("scalar",) * 4, (2, 2))
         picked = [picks(0)]
         first_product(1, range(4, 8))
 
@@ -264,9 +258,9 @@ def tile_list_wavelet_tree_contexts_kernel(
         def normalise(name, ratio, norm, lo, hi):
             z = held(name, [P, (hi - lo) * PACK], BF16)
             nc.vector.tensor_tensor(
-                out=z[:].rearrange("p (c i t) -> p c t i", i=4, t=PACK),
-                in0=ratio[:, :, lo:hi].rearrange("p t (c i) -> p c t i", i=4),
-                in1=norm[:].rearrange("p t (c i) -> p c t i", i=4),
+                out=z[:].rearrange("p (c i t) -> p c t i", i=2, t=PACK),
+                in0=ratio[:, :, lo:hi].rearrange("p t (c i) -> p c t i", i=2),
+                in1=norm[:].rearrange("p t (c i) -> p c t i", i=2),
                 op=MULT,
             )
             codes = held(name + "_c", [P, hi - lo], U32)
@@ -274,20 +268,15 @@ def tile_list_wavelet_tree_contexts_kernel(
             nc.vector.quantize_mx(out=codes[:].bitcast(FP8X4), scales=scales[:], in_=z[:])
             return codes, scales
 
-        def quantise_w3(b):
-            grouped = held(f"w3_g{b}", [P, N * PACK], BF16)
+        def quantise_w3(b, engine, after):
+            grouped = held(f"w3_g{b}", [P, N * PACK], BF16, after)
             codes = held(f"w3_c{b}", [P, N], U32)
             scales = held(f"w3_s{b}", [P, N], U8)
-            raw = w3_raw[b][:].rearrange("p (t n) -> p n t", t=PACK)
-            for n0 in range(0, N, P):
-                nc.gpsimd.tensor_scalar(
-                    out=grouped[:, n0 * PACK : (n0 + P) * PACK].rearrange("p (n t) -> p n t", t=PACK),
-                    in0=raw[:, n0 : n0 + P, :],
-                    scalar1=1.0,
-                    scalar2=0.0,
-                    op0=MULT,
-                    op1=ADD,
-                )
+            round_on(
+                engine,
+                grouped[:].rearrange("p (c i t) -> p c t i", i=4, t=PACK),
+                w3_raw[b][:].rearrange("p (t c i) -> p c t i", t=PACK, i=4),
+            )
             nc.vector.quantize_mx(out=codes[:].bitcast(FP8X4), scales=scales[:], in_=grouped[:])
             return codes, scales
 
@@ -297,7 +286,7 @@ def tile_list_wavelet_tree_contexts_kernel(
         ratio1, square1 = second_product(1)
         norms1 = [inverse_root(f"norm1{lo}", square1, lo, hi) for lo, hi in PIECES]
         z0 = normalise("z0", ratio0, norm0, 0, M)
-        w3_q = [quantise_w3(b) for b in range(2)]
+        w3_q = [quantise_w3(0, "scalar", None), quantise_w3(1, "vector", "picked3")]
 
         def last_pass(acc, b, z, first, j, place, lo, hi, start, stop):
             nc.tensor.matmul_mx(

@@ -16,6 +16,7 @@ FP8X4 = mybir.dt.float8_e4m3fn_x4
 FP4X4 = mybir.dt.float4_e2m1fn_x4
 ACT = mybir.ActivationFunctionType
 MULT = mybir.AluOpType.mult
+ADD = mybir.AluOpType.add
 
 P = 128
 PACK = 4
@@ -82,20 +83,28 @@ def tile_list_wavelet_tree_contexts_kernel(
             else:
                 nc.scalar.copy(out=dst, in_=src)
 
-        def quantise_w1(a, b, raw, engines, widths):
+        def round_on_gpsimd(dst, src):
+            nc.gpsimd.tensor_scalar(out=dst, in0=src, scalar1=1.0, scalar2=0.0, op0=MULT, op1=ADD)
+
+        def quantise_w1(a, b, raw, groups, after=None):
             codes = held(f"w1_c{a}{b}", [P, PASS], U32)
             scales = held(f"w1_s{a}{b}", [P, PASS], U8)
+            src = raw[:].rearrange("p j (g t i) -> p t g j i", t=PACK, i=4)
             t0 = 0
-            for width in widths:
-                grouped = held(f"w1_g{a}{b}{t0}", [P, width * PASS], BF16)
-                for u in range(width):
-                    t = t0 + u
-                    dst = grouped[:, u * PASS : (u + 1) * PASS]
-                    round_on(
-                        engines[t],
-                        dst.rearrange("p (g h i j) -> p g h j i", g=16, h=2, i=4),
-                        raw[:].rearrange("p j (g t h i) -> p t g h j i", t=PACK, h=2, i=4)[:, t],
-                    )
+            for shares in groups:
+                width = sum(share for engine, share in shares)
+                grouped = held(f"w1_g{a}{b}{t0}", [P, width * PASS], BF16, after if t0 else None)
+                dst = grouped[:].rearrange("p (t g i j) -> p t g j i", t=width, i=4, j=PACK)
+                u = 0
+                for engine, share in shares:
+                    if engine == "gpsimd":
+                        for v in range(u, u + share):
+                            round_on_gpsimd(
+                                dst[:, v].rearrange("p g j i -> p g i j"), src[:, t0 + v].rearrange("p g j i -> p g i j")
+                            )
+                    else:
+                        round_on(engine, dst[:, u : u + share], src[:, t0 + u : t0 + u + share])
+                    u = u + share
                 cols = slice(t0 * P, (t0 + width) * P)
                 nc.vector.quantize_mx(out=codes[:, cols].bitcast(FP8X4), scales=scales[:, cols], in_=grouped[:])
                 t0 = t0 + width
@@ -117,8 +126,8 @@ def tile_list_wavelet_tree_contexts_kernel(
         nc.gpsimd.memset(gain_rows[:], 0.0)
         for b in range(2):
             nc.gpsimd.dma_start(
-                out=gain_rows[b * PACK : (b + 1) * PACK, :].rearrange("t (g i) -> t g i", i=8),
-                in_=gain[b * PASS : (b + 1) * PASS].rearrange("(g t i) -> t g i", t=PACK, i=8),
+                out=gain_rows[b * PACK : (b + 1) * PACK, :].rearrange("t (g i) -> t g i", i=4),
+                in_=gain[b * PASS : (b + 1) * PASS].rearrange("(g t i) -> t g i", t=PACK, i=4),
             )
         identity = held("identity", [P, P], F32)
         make_identity(nc, identity[:])
@@ -129,42 +138,42 @@ def tile_list_wavelet_tree_contexts_kernel(
         load_words(tab_w1[:], tab_words, 1)
 
         picked2_s = gather("picked2_s", U8, tab2_s[:], idx2[:], M)
-        v2_s = to_plane(nc.gpsimd, "v2_s", picked2_s, 64, M)
+        w1_raw[1, 0] = load_w1(1, 0, "tab2_s")
+        v2_s = to_plane(nc.sync, "v2_s", picked2_s, 64, M)
 
         turned = bank("turned", 7)
         nc.tensor.transpose(turned[:, 0:P], gain_rows[:], identity[:])
         gains = held("gains", [P, 2 * PACK], F32)
         nc.scalar.copy(out=gains[:], in_=turned[:, 0 : 2 * PACK])
-        inv_gains = held("inv_gains", [P, 2 * PACK], F32)
-        nc.vector.reciprocal(out=inv_gains[:], in_=gains[:])
+        gains_squared = held("gains_squared", [P, 2 * PACK], F32)
+        nc.scalar.activation(out=gains_squared[:], in_=turned[:, 0 : 2 * PACK], func=ACT.Square)
 
-        w1_q = {(0, 0): quantise_w1(0, 0, w1_raw[0, 0], ("scalar",) * 4, (2, 2))}
-        w1_raw[1, 0] = load_w1(1, 0, "w1_g000")
+        w1_q = {(0, 0): quantise_w1(0, 0, w1_raw[0, 0], ((("scalar", 2),), (("scalar", 2),)))}
         w1_raw[0, 1] = load_w1(0, 1, "w1_raw00")
         w1_raw[1, 1] = load_w1(1, 1, "w1_g002")
-        w2_s_raw = held("w2_s_raw", [P, 2 * H], U8, "tab2_s")
+        w2_s_raw = held("w2_s_raw", [P, 2 * H], U8, "picked_s")
         nc.gpsimd.memset(w2_s_raw[:].bitcast(I32), 0)
         for q in range(4):
             nc.sync.dma_start(
                 out=w2_s_raw[32 * q : 32 * q + 4, :].bitcast(I32).rearrange("r (a c) -> r a c", a=2),
                 in_=w2_scales.bitcast(I32)[:, 4 * q : 4 * q + 4, :].rearrange("a r c -> r a c"),
             )
-        w2_w_raw = held("w2_w_raw", [P, 2, H // 2], I32, "picked_s")
+        w2_w_raw = held("w2_w_raw", [P, 2, H // 2], I32, "gain_rows")
         nc.sync.dma_start(out=w2_w_raw[:], in_=w2_words.bitcast(I32).rearrange("a p c -> p a c"))
 
         v_w = {}
         for half in range(2):
             v_w[0, half] = gather(f"v_w0{half}", U32, tab_w0[:], idx[:, 32 * half : 32 * (half + 1)], BANK)
-        tab2_w = held("tab2_w", [P, 2 * T2], U32, "tab_w0")
+        tab2_w = [held(f"tab2_w{a}", [P, T2], U32, after) for a, after in enumerate(("identity", "tab_w0"))]
         for a in range(2):
-            load_words(tab2_w[:, a * T2 : (a + 1) * T2], tab2_words, a)
+            load_words(tab2_w[a][:], tab2_words, a)
 
         for half in range(2):
             v_w[1, half] = gather(f"v_w1{half}", U32, tab_w1[:], idx[:, 32 * half : 32 * (half + 1)], BANK)
 
         def load_w3(b, after):
             raw = held(f"w3_raw{b}", [P, PACK * N], F32, after)
-            rows = w3[b * PASS : (b + 1) * PASS, :].rearrange("(g t i) n -> t g i n", t=PACK, i=8)
+            rows = w3[b * PASS : (b + 1) * PASS, :].rearrange("(g t i) n -> t g i n", t=PACK, i=4)
             for t in range(PACK):
                 nc.sync.dma_start(out=raw[:, t * N : (t + 1) * N], in_=rows[t])
             return raw
@@ -202,32 +211,39 @@ def tile_list_wavelet_tree_contexts_kernel(
                             scale=-0.5,
                         )
 
-        def picks(b):
-            return [gather(f"picked{b}{t}", F32, damping[b, t][:], parent[:], M, f"picked{t}" if t else None) for t in range(PACK)]
+        def pick(dst, b, t):
+            nc.vector.tensor_copy(out=dst, in_=damping[b, t][:].indirect(parent[:]))
+            return dst
 
-        w1_q[1, 0] = quantise_w1(1, 0, w1_raw[1, 0], ("vector", "scalar", "vector", "scalar"), (1, 1, 2))
-        w3_raw = [load_w3(0, "tab_s"), load_w3(1, "w1_g000")]
+        w1_q[1, 0] = quantise_w1(1, 0, w1_raw[1, 0], ((("vector", 1),), (("scalar", 1),), (("vector", 1), ("scalar", 1))))
+        w3_raw = [load_w3(0, "tab2_s")]
         first_product(0, range(8))
-        w1_q[0, 1] = quantise_w1(0, 1, w1_raw[0, 1], ("vector",) * 4, (4,))
-        w1_q[1, 1] = quantise_w1(1, 1, w1_raw[1, 1], ("scalar",) * 4, (2, 2))
-        picked = [picks(0)]
+        w1_q[0, 1] = quantise_w1(0, 1, w1_raw[0, 1], ((("vector", 2), ("gpsimd", 2)),))
+        w3_raw.append(load_w3(1, "w1_raw00"))
+        w1_q[1, 1] = quantise_w1(1, 1, w1_raw[1, 1], ((("gpsimd", 2),), (("scalar", 2),)), "w1_c10")
+        picked = [
+            [
+                pick(held(f"picked0{t}", [P, M], F32, after)[:], 0, t)
+                for t, after in enumerate((None, None, "w1_g010", "w1_g110"))
+            ]
+        ]
         first_product(1, range(4, 8))
 
         w2_s = held("w2_s", [P, 2 * H], U8)
-        nc.vector.tensor_copy(
-            out=w2_s[:].bitcast(I32).rearrange("p (ab t g w) -> p ab t g w", t=PACK, g=16, w=2),
-            in_=w2_s_raw[:].bitcast(I32).rearrange("p (ab g t w) -> p ab t g w", t=PACK, g=16, w=2),
+        nc.gpsimd.tensor_copy(
+            out=w2_s[:].bitcast(I32).rearrange("p (ab t g w) -> p ab t g w", t=PACK, g=32, w=1),
+            in_=w2_s_raw[:].bitcast(I32).rearrange("p (ab g t w) -> p ab t g w", t=PACK, g=32, w=1),
         )
         w2_w = held("w2_w", [P, 2 * 2 * H], U8)
-        nc.vector.tensor_copy(
-            out=w2_w[:].bitcast(I32).rearrange("p (ab t g w) -> p ab t g w", t=PACK, g=16, w=4),
-            in_=w2_w_raw[:].rearrange("p a (b g t w) -> p (a b) t g w", t=PACK, g=16, w=4),
+        nc.gpsimd.tensor_copy(
+            out=w2_w[:].bitcast(I32).rearrange("p (ab t g w) -> p ab t g w", t=PACK, g=32, w=2),
+            in_=w2_w_raw[:].rearrange("p a (b g t w) -> p (a b) t g w", t=PACK, g=32, w=2),
         )
-        v2_w = [gather(f"v2_w{a}", U32, tab2_w[:, a * T2 : (a + 1) * T2], idx2[:], M) for a in range(2)]
+        v2_w = [gather(f"v2_w{a}", U32, tab2_w[a][:], idx2[:], M, ("w1_c10", "damping03")[a]) for a in range(2)]
 
         def second_product(b):
             ratio = held(f"ratio{b}", [P, PACK, M], F32)
-            square = held(f"square{b}", [P, PACK, M], F32, ("w1_raw00", "w1_g002")[b])
+            square = held(f"square{b}", [P, PACK, M], F32, "tab_s")
             for t in range(PACK):
                 acc = bank(f"b{b}{t}", t)
                 for a in range(2):
@@ -243,7 +259,7 @@ def tile_list_wavelet_tree_contexts_kernel(
                     )
                 slot = b * PACK + t
                 nc.vector.scalar_tensor_tensor(
-                    out=ratio[:, t, :], in0=acc[:], scalar=gains[:, slot : slot + 1], in1=picked[b][t][:], op0=MULT, op1=MULT
+                    out=ratio[:, t, :], in0=acc[:], scalar=gains[:, slot : slot + 1], in1=picked[b][t], op0=MULT, op1=MULT
                 )
                 nc.scalar.activation(
                     out=square[:, t, :], in_=ratio[:, t, :], func=ACT.Square, scale=inv_gains[:, slot : slot + 1]
@@ -255,38 +271,53 @@ def tile_list_wavelet_tree_contexts_kernel(
             nc.scalar.activation(out=norm[:], in_=square[:, :, lo:hi], func=ACT.Abs_reciprocal_sqrt, bias=1.0)
             return norm
 
-        def normalise(name, ratio, norm, lo, hi):
-            z = held(name, [P, (hi - lo) * PACK], BF16)
-            nc.vector.tensor_tensor(
-                out=z[:].rearrange("p (c i t) -> p c t i", i=2, t=PACK),
-                in0=ratio[:, :, lo:hi].rearrange("p t (c i) -> p c t i", i=2),
-                in1=norm[:].rearrange("p t (c i) -> p c t i", i=2),
+        def normalise(engine, z, ratio, norm, lo, hi):
+            engine.tensor_tensor(
+                out=z.rearrange("p (c i t) -> p c t i", i=4, t=PACK),
+                in0=ratio[:, :, lo:hi].rearrange("p t (c i) -> p c t i", i=4),
+                in1=norm.rearrange("p t (c i) -> p c t i", i=4),
                 op=MULT,
             )
-            codes = held(name + "_c", [P, hi - lo], U32)
-            scales = held(name + "_s", [P, hi - lo], U8)
+
+        def quantise_z(name, z, width, after=None):
+            codes = held(name + "_c", [P, width], U32, after)
+            scales = held(name + "_s", [P, width], U8)
             nc.vector.quantize_mx(out=codes[:].bitcast(FP8X4), scales=scales[:], in_=z[:])
             return codes, scales
 
-        def quantise_w3(b, engine, after):
-            grouped = held(f"w3_g{b}", [P, N * PACK], BF16, after)
-            codes = held(f"w3_c{b}", [P, N], U32)
+        def round_w3(b):
+            grouped = held(f"w3_g{b}", [P, N * PACK], BF16)
+            for n0 in range(0, N, P):
+                round_on_gpsimd(
+                    grouped[:, n0 * PACK : (n0 + P) * PACK].rearrange("p (n t) -> p n t", t=PACK),
+                    w3_raw[b][:].rearrange("p (t n) -> p n t", t=PACK)[:, n0 : n0 + P, :],
+                )
+            return grouped
+
+        def quantise_w3(b, after):
+            codes = held(f"w3_c{b}", [P, N], U32, after)
             scales = held(f"w3_s{b}", [P, N], U8)
-            round_on(
-                engine,
-                grouped[:].rearrange("p (c i t) -> p c t i", i=4, t=PACK),
-                w3_raw[b][:].rearrange("p (t c i) -> p c t i", t=PACK, i=4),
-            )
-            nc.vector.quantize_mx(out=codes[:].bitcast(FP8X4), scales=scales[:], in_=grouped[:])
+            nc.vector.quantize_mx(out=codes[:].bitcast(FP8X4), scales=scales[:], in_=w3_g[b][:])
             return codes, scales
 
+        w3_g = [round_w3(b) for b in range(2)]
+        inv_gains = held("inv_gains", [P, 2 * PACK], F32, "w1_c11")
+        nc.scalar.activation(out=inv_gains[:], in_=gains_squared[:], func=ACT.Abs_reciprocal_sqrt)
+        picked.append([pick(held("picked10", [P, M], F32)[:], 1, 0)])
         ratio0, square0 = second_product(0)
-        norm0 = inverse_root("norm0", square0, 0, M, "w1_c11")
-        picked.append(picks(1))
+        norms0 = [inverse_root(f"norm0{lo}", square0, lo, lo + M // 2) for lo in (0, M // 2)]
+        z0_values = held("z0", [P, M * PACK], BF16)
+        for lo in range(0, M // 2, P):
+            normalise(nc.gpsimd, z0_values[:, lo * PACK : (lo + P) * PACK], ratio0, norms0[0][:, :, lo : lo + P], lo, lo + P)
+        picked[1].extend(
+            pick(held(f"picked1{t}", [P, M], F32, after)[:], 1, t)
+            for t, after in ((1, "w1_g010"), (2, "w1_g110"), (3, "picked01"))
+        )
         ratio1, square1 = second_product(1)
         norms1 = [inverse_root(f"norm1{lo}", square1, lo, hi) for lo, hi in PIECES]
-        z0 = normalise("z0", ratio0, norm0, 0, M)
-        w3_q = [quantise_w3(0, "scalar", None), quantise_w3(1, "vector", "picked3")]
+        normalise(nc.vector, z0_values[:, M // 2 * PACK :], ratio0, norms0[1][:], M // 2, M)
+        w3_q = [quantise_w3(0, "w1_g110"), quantise_w3(1, "picked01")]
+        z0 = quantise_z("z0", z0_values, M, "w3_g0")
 
         def last_pass(acc, b, z, first, j, place, lo, hi, start, stop):
             nc.tensor.matmul_mx(
@@ -307,16 +338,15 @@ def tile_list_wavelet_tree_contexts_kernel(
                 for place in range(2):
                     last_pass(accs[piece, pair], 0, z0, 0, 2 * pair + place, place, lo, hi, place == 0, False)
         for piece, (lo, hi) in enumerate(PIECES):
-            z1 = normalise(f"z1{lo}", ratio1, norms1[piece], lo, hi)
+            z1_values = held(f"z1{lo}", [P, (hi - lo) * PACK], BF16, ("z0", "w3_g1", None)[piece])
+            normalise(nc.vector, z1_values[:], ratio1, norms1[piece][:], lo, hi)
+            z1 = quantise_z(f"z1{lo}", z1_values, hi - lo)
             for pair in range(2):
                 acc = accs[piece, pair]
                 for place in range(2):
                     last_pass(acc, 1, z1, lo, 2 * pair + place, place, lo, hi, False, place == 1)
                 staged = held(f"staged{piece}{pair}", [P, 2 * (hi - lo)], F32)
-                if hi == M and pair == 1:
-                    nc.vector.tensor_copy(out=staged[:], in_=acc[:, 0 : 2 * (hi - lo)])
-                else:
-                    nc.scalar.copy(out=staged[:], in_=acc[:, 0 : 2 * (hi - lo)])
+                round_on("vector" if hi == M and pair == 1 else "scalar", staged[:], acc[:, 0 : 2 * (hi - lo)])
                 nc.sync.dma_start(
                     out=out_rows[:, 2 * pair : 2 * pair + 2, lo:hi], in_=staged[:].rearrange("p (j m) -> p j m", j=2)
                 )

@@ -89,22 +89,23 @@ def tile_list_wavelet_tree_contexts_kernel(
         def quantise_w1(a, b, raw, groups, after=None):
             codes = held(f"w1_c{a}{b}", [P, PASS], U32)
             scales = held(f"w1_s{a}{b}", [P, PASS], U8)
-            src = raw[:].rearrange("p j (g t i) -> p t g j i", t=PACK, i=4)
             t0 = 0
-            for shares in groups:
-                width = sum(share for engine, share in shares)
+            for engines in groups:
+                width = len(engines)
                 grouped = held(f"w1_g{a}{b}{t0}", [P, width * PASS], BF16, after if t0 else None)
-                dst = grouped[:].rearrange("p (t g i j) -> p t g j i", t=width, i=4, j=PACK)
-                u = 0
-                for engine, share in shares:
+                for u, engine in enumerate(engines):
+                    dst = grouped[:, u * PASS : (u + 1) * PASS]
                     if engine == "gpsimd":
-                        for v in range(u, u + share):
-                            round_on_gpsimd(
-                                dst[:, v].rearrange("p g j i -> p g i j"), src[:, t0 + v].rearrange("p g j i -> p g i j")
-                            )
+                        round_on_gpsimd(
+                            dst.rearrange("p (g i j) -> p g i j", g=16, j=PACK),
+                            raw[:].rearrange("p j (g t i) -> p t g i j", t=PACK, i=8)[:, t0 + u],
+                        )
                     else:
-                        round_on(engine, dst[:, u : u + share], src[:, t0 + u : t0 + u + share])
-                    u = u + share
+                        round_on(
+                            engine,
+                            dst.rearrange("p (g h i j) -> p g h j i", g=16, h=2, i=4),
+                            raw[:].rearrange("p j (g t h i) -> p t g h j i", t=PACK, h=2, i=4)[:, t0 + u],
+                        )
                 cols = slice(t0 * P, (t0 + width) * P)
                 nc.vector.quantize_mx(out=codes[:, cols].bitcast(FP8X4), scales=scales[:, cols], in_=grouped[:])
                 t0 = t0 + width
@@ -126,8 +127,8 @@ def tile_list_wavelet_tree_contexts_kernel(
         nc.gpsimd.memset(gain_rows[:], 0.0)
         for b in range(2):
             nc.gpsimd.dma_start(
-                out=gain_rows[b * PACK : (b + 1) * PACK, :].rearrange("t (g i) -> t g i", i=4),
-                in_=gain[b * PASS : (b + 1) * PASS].rearrange("(g t i) -> t g i", t=PACK, i=4),
+                out=gain_rows[b * PACK : (b + 1) * PACK, :].rearrange("t (g i) -> t g i", i=8),
+                in_=gain[b * PASS : (b + 1) * PASS].rearrange("(g t i) -> t g i", t=PACK, i=8),
             )
         identity = held("identity", [P, P], F32)
         make_identity(nc, identity[:])
@@ -138,8 +139,7 @@ def tile_list_wavelet_tree_contexts_kernel(
         load_words(tab_w1[:], tab_words, 1)
 
         picked2_s = gather("picked2_s", U8, tab2_s[:], idx2[:], M)
-        w1_raw[1, 0] = load_w1(1, 0, "tab2_s")
-        v2_s = to_plane(nc.sync, "v2_s", picked2_s, 64, M)
+        v2_s = to_plane(nc.gpsimd, "v2_s", picked2_s, 64, M)
 
         turned = bank("turned", 7)
         nc.tensor.transpose(turned[:, 0:P], gain_rows[:], identity[:])
@@ -148,32 +148,33 @@ def tile_list_wavelet_tree_contexts_kernel(
         gains_squared = held("gains_squared", [P, 2 * PACK], F32)
         nc.scalar.activation(out=gains_squared[:], in_=turned[:, 0 : 2 * PACK], func=ACT.Square)
 
-        w1_q = {(0, 0): quantise_w1(0, 0, w1_raw[0, 0], ((("scalar", 2),), (("scalar", 2),)))}
+        w1_q = {(0, 0): quantise_w1(0, 0, w1_raw[0, 0], (("scalar", "scalar"), ("scalar", "scalar")))}
+        w1_raw[1, 0] = load_w1(1, 0, "w1_g000")
         w1_raw[0, 1] = load_w1(0, 1, "w1_raw00")
         w1_raw[1, 1] = load_w1(1, 1, "w1_g002")
-        w2_s_raw = held("w2_s_raw", [P, 2 * H], U8, "picked_s")
+        w2_s_raw = held("w2_s_raw", [P, 2 * H], U8, "tab2_s")
         nc.gpsimd.memset(w2_s_raw[:].bitcast(I32), 0)
         for q in range(4):
             nc.sync.dma_start(
                 out=w2_s_raw[32 * q : 32 * q + 4, :].bitcast(I32).rearrange("r (a c) -> r a c", a=2),
                 in_=w2_scales.bitcast(I32)[:, 4 * q : 4 * q + 4, :].rearrange("a r c -> r a c"),
             )
-        w2_w_raw = held("w2_w_raw", [P, 2, H // 2], I32, "gain_rows")
+        w2_w_raw = held("w2_w_raw", [P, 2, H // 2], I32, "picked_s")
         nc.sync.dma_start(out=w2_w_raw[:], in_=w2_words.bitcast(I32).rearrange("a p c -> p a c"))
 
         v_w = {}
         for half in range(2):
             v_w[0, half] = gather(f"v_w0{half}", U32, tab_w0[:], idx[:, 32 * half : 32 * (half + 1)], BANK)
-        tab2_w = [held(f"tab2_w{a}", [P, T2], U32, after) for a, after in enumerate(("identity", "tab_w0"))]
+        tab2_w = held("tab2_w", [P, 2 * T2], U32, "tab_w0")
         for a in range(2):
-            load_words(tab2_w[a][:], tab2_words, a)
+            load_words(tab2_w[:, a * T2 : (a + 1) * T2], tab2_words, a)
 
         for half in range(2):
             v_w[1, half] = gather(f"v_w1{half}", U32, tab_w1[:], idx[:, 32 * half : 32 * (half + 1)], BANK)
 
         def load_w3(b, after):
             raw = held(f"w3_raw{b}", [P, PACK * N], F32, after)
-            rows = w3[b * PASS : (b + 1) * PASS, :].rearrange("(g t i) n -> t g i n", t=PACK, i=4)
+            rows = w3[b * PASS : (b + 1) * PASS, :].rearrange("(g t i) n -> t g i n", t=PACK, i=8)
             for t in range(PACK):
                 nc.sync.dma_start(out=raw[:, t * N : (t + 1) * N], in_=rows[t])
             return raw
@@ -215,12 +216,11 @@ def tile_list_wavelet_tree_contexts_kernel(
             nc.vector.tensor_copy(out=dst, in_=damping[b, t][:].indirect(parent[:]))
             return dst
 
-        w1_q[1, 0] = quantise_w1(1, 0, w1_raw[1, 0], ((("vector", 1),), (("scalar", 1),), (("vector", 1), ("scalar", 1))))
-        w3_raw = [load_w3(0, "tab2_s")]
+        w1_q[1, 0] = quantise_w1(1, 0, w1_raw[1, 0], (("vector",), ("scalar",), ("vector", "scalar")))
+        w3_raw = [load_w3(0, "tab_s"), load_w3(1, "w1_g000")]
         first_product(0, range(8))
-        w1_q[0, 1] = quantise_w1(0, 1, w1_raw[0, 1], ((("vector", 2), ("gpsimd", 2)),))
-        w3_raw.append(load_w3(1, "w1_raw00"))
-        w1_q[1, 1] = quantise_w1(1, 1, w1_raw[1, 1], ((("gpsimd", 2),), (("scalar", 2),)), "w1_c10")
+        w1_q[0, 1] = quantise_w1(0, 1, w1_raw[0, 1], (("vector", "vector", "gpsimd", "gpsimd"),))
+        w1_q[1, 1] = quantise_w1(1, 1, w1_raw[1, 1], (("gpsimd", "gpsimd"), ("scalar", "scalar")), "w1_c10")
         picked = [
             [
                 pick(held(f"picked0{t}", [P, M], F32, after)[:], 0, t)
@@ -231,19 +231,19 @@ def tile_list_wavelet_tree_contexts_kernel(
 
         w2_s = held("w2_s", [P, 2 * H], U8)
         nc.gpsimd.tensor_copy(
-            out=w2_s[:].bitcast(I32).rearrange("p (ab t g w) -> p ab t g w", t=PACK, g=32, w=1),
-            in_=w2_s_raw[:].bitcast(I32).rearrange("p (ab g t w) -> p ab t g w", t=PACK, g=32, w=1),
+            out=w2_s[:].bitcast(I32).rearrange("p (ab t g w) -> p ab t g w", t=PACK, g=16, w=2),
+            in_=w2_s_raw[:].bitcast(I32).rearrange("p (ab g t w) -> p ab t g w", t=PACK, g=16, w=2),
         )
         w2_w = held("w2_w", [P, 2 * 2 * H], U8)
         nc.gpsimd.tensor_copy(
-            out=w2_w[:].bitcast(I32).rearrange("p (ab t g w) -> p ab t g w", t=PACK, g=32, w=2),
-            in_=w2_w_raw[:].rearrange("p a (b g t w) -> p (a b) t g w", t=PACK, g=32, w=2),
+            out=w2_w[:].bitcast(I32).rearrange("p (ab t g w) -> p ab t g w", t=PACK, g=16, w=4),
+            in_=w2_w_raw[:].rearrange("p a (b g t w) -> p (a b) t g w", t=PACK, g=16, w=4),
         )
-        v2_w = [gather(f"v2_w{a}", U32, tab2_w[a][:], idx2[:], M, ("w1_c10", "damping03")[a]) for a in range(2)]
+        v2_w = [gather(f"v2_w{a}", U32, tab2_w[:, a * T2 : (a + 1) * T2], idx2[:], M, ("w1_c10", "damping03")[a]) for a in range(2)]
 
         def second_product(b):
             ratio = held(f"ratio{b}", [P, PACK, M], F32)
-            square = held(f"square{b}", [P, PACK, M], F32, "tab_s")
+            square = held(f"square{b}", [P, PACK, M], F32, "w1_raw00")
             for t in range(PACK):
                 acc = bank(f"b{b}{t}", t)
                 for a in range(2):

@@ -23,6 +23,7 @@ PACK = 4
 PASS = P * PACK
 BANK = 512
 PIECES = ((0, 256), (256, 384), (384, 512))
+SHARE = 192
 
 
 def tile_list_wavelet_tree_contexts_kernel(
@@ -92,7 +93,7 @@ def tile_list_wavelet_tree_contexts_kernel(
             t0 = 0
             for engines in groups:
                 width = len(engines)
-                grouped = held(f"w1_g{a}{b}{t0}", [P, width * PASS], BF16, after if t0 else None)
+                grouped = held(f"w1_g{a}{b}{t0}", [P, width * PASS], BF16, after)
                 for u, engine in enumerate(engines):
                     dst = grouped[:, u * PASS : (u + 1) * PASS]
                     if engine == "gpsimd":
@@ -219,12 +220,12 @@ def tile_list_wavelet_tree_contexts_kernel(
         w1_q[1, 0] = quantise_w1(1, 0, w1_raw[1, 0], (("vector",), ("scalar",), ("vector", "scalar")))
         w3_raw = [load_w3(0, "tab_s"), load_w3(1, "w1_g000")]
         first_product(0, range(8))
-        w1_q[0, 1] = quantise_w1(0, 1, w1_raw[0, 1], (("vector", "vector", "gpsimd", "gpsimd"),))
-        w1_q[1, 1] = quantise_w1(1, 1, w1_raw[1, 1], (("gpsimd", "gpsimd"), ("scalar", "scalar")), "w1_c10")
+        w1_q[0, 1] = quantise_w1(0, 1, w1_raw[0, 1], (("gpsimd",) * PACK,))
+        w1_q[1, 1] = quantise_w1(1, 1, w1_raw[1, 1], (("gpsimd", "gpsimd", "scalar", "scalar"),), "w1_g010")
         picked = [
             [
                 pick(held(f"picked0{t}", [P, M], F32, after)[:], 0, t)
-                for t, after in enumerate((None, None, "w1_g010", "w1_g110"))
+                for t, after in enumerate((None, None, "w1_raw00", "w1_g002"))
             ]
         ]
         first_product(1, range(4, 8))
@@ -234,16 +235,20 @@ def tile_list_wavelet_tree_contexts_kernel(
             out=w2_s[:].bitcast(I32).rearrange("p (ab t g w) -> p ab t g w", t=PACK, g=16, w=2),
             in_=w2_s_raw[:].bitcast(I32).rearrange("p (ab g t w) -> p ab t g w", t=PACK, g=16, w=2),
         )
-        w2_w = held("w2_w", [P, 2 * 2 * H], U8)
+        w2_w = held("w2_w", [P, 2 * 2 * H], U8, "damping03")
         nc.gpsimd.tensor_copy(
             out=w2_w[:].bitcast(I32).rearrange("p (ab t g w) -> p ab t g w", t=PACK, g=16, w=4),
             in_=w2_w_raw[:].rearrange("p a (b g t w) -> p (a b) t g w", t=PACK, g=16, w=4),
         )
-        v2_w = [gather(f"v2_w{a}", U32, tab2_w[:, a * T2 : (a + 1) * T2], idx2[:], M, ("w1_c10", "damping03")[a]) for a in range(2)]
+        v2_w = held("v2_w", [P, 2 * M], U32, "w1_g010")
+        for a in range(2):
+            nc.vector.tensor_copy(
+                out=v2_w[:, a * M : (a + 1) * M], in_=tab2_w[:, a * T2 : (a + 1) * T2].indirect(idx2[:])
+            )
 
         def second_product(b):
             ratio = held(f"ratio{b}", [P, PACK, M], F32)
-            square = held(f"square{b}", [P, PACK, M], F32, "w1_raw00")
+            square = held(f"square{b}", [P, PACK, M], F32, ("tab_w0", "w1_g000")[b])
             for t in range(PACK):
                 acc = bank(f"b{b}{t}", t)
                 for a in range(2):
@@ -252,7 +257,7 @@ def tile_list_wavelet_tree_contexts_kernel(
                         out=acc[:],
                         lhsT=w2_w[:, 2 * col : 2 * (col + P)].bitcast(FP4X4),
                         lhsT_scale=w2_s[:, col : col + P],
-                        rhs=v2_w[a][:].bitcast(FP8X4),
+                        rhs=v2_w[:, a * M : (a + 1) * M].bitcast(FP8X4),
                         rhs_scale=v2_s[:, a * M : (a + 1) * M],
                         start=(a == 0),
                         stop=(a == 1),
@@ -285,38 +290,45 @@ def tile_list_wavelet_tree_contexts_kernel(
             nc.vector.quantize_mx(out=codes[:].bitcast(FP8X4), scales=scales[:], in_=z[:])
             return codes, scales
 
-        def round_w3(b):
-            grouped = held(f"w3_g{b}", [P, N * PACK], BF16)
-            for n0 in range(0, N, P):
+        def round_w3_on_gpsimd(b, width):
+            for n0 in range(0, width, P):
                 round_on_gpsimd(
-                    grouped[:, n0 * PACK : (n0 + P) * PACK].rearrange("p (n t) -> p n t", t=PACK),
+                    w3_g[b][:, n0 * PACK : (n0 + P) * PACK].rearrange("p (n t) -> p n t", t=PACK),
                     w3_raw[b][:].rearrange("p (t n) -> p n t", t=PACK)[:, n0 : n0 + P, :],
                 )
-            return grouped
 
-        def quantise_w3(b, after):
+        def quantise_w3(b, after, parts):
             codes = held(f"w3_c{b}", [P, N], U32, after)
             scales = held(f"w3_s{b}", [P, N], U8)
-            nc.vector.quantize_mx(out=codes[:].bitcast(FP8X4), scales=scales[:], in_=w3_g[b][:])
+            width = N // len(parts)
+            for place, grouped in enumerate(parts):
+                cols = slice(place * width, (place + 1) * width)
+                nc.vector.quantize_mx(out=codes[:, cols].bitcast(FP8X4), scales=scales[:, cols], in_=grouped[:])
             return codes, scales
 
-        w3_g = [round_w3(b) for b in range(2)]
+        w3_g = [held("w3_g0", [P, N * PACK], BF16), held("w3_g1", [P, N // 2 * PACK], BF16)]
+        round_w3_on_gpsimd(0, N)
+        round_w3_on_gpsimd(1, N // 2)
         inv_gains = held("inv_gains", [P, 2 * PACK], F32, "w1_c11")
         nc.scalar.activation(out=inv_gains[:], in_=gains_squared[:], func=ACT.Abs_reciprocal_sqrt)
         picked.append([pick(held("picked10", [P, M], F32)[:], 1, 0)])
         ratio0, square0 = second_product(0)
-        norms0 = [inverse_root(f"norm0{lo}", square0, lo, lo + M // 2) for lo in (0, M // 2)]
+        norms0 = [inverse_root(f"norm0{lo}", square0, lo, hi) for lo, hi in ((0, SHARE), (SHARE, M))]
         z0_values = held("z0", [P, M * PACK], BF16)
-        for lo in range(0, M // 2, P):
-            normalise(nc.gpsimd, z0_values[:, lo * PACK : (lo + P) * PACK], ratio0, norms0[0][:, :, lo : lo + P], lo, lo + P)
+        normalise(nc.gpsimd, z0_values[:, : SHARE * PACK], ratio0, norms0[0][:], 0, SHARE)
+        w3_g.append(held("w3_g2", [P, N // 2 * PACK], BF16, "tab_w0"))
+        nc.scalar.copy(
+            out=w3_g[2][:].rearrange("p (c i t) -> p c t i", i=4, t=PACK),
+            in_=w3_raw[1][:].rearrange("p (t c i) -> p c t i", t=PACK, i=4)[:, N // 8 :],
+        )
         picked[1].extend(
             pick(held(f"picked1{t}", [P, M], F32, after)[:], 1, t)
-            for t, after in ((1, "w1_g010"), (2, "w1_g110"), (3, "picked01"))
+            for t, after in ((1, "w1_raw00"), (2, "w1_g002"), (3, "picked01"))
         )
         ratio1, square1 = second_product(1)
         norms1 = [inverse_root(f"norm1{lo}", square1, lo, hi) for lo, hi in PIECES]
-        normalise(nc.vector, z0_values[:, M // 2 * PACK :], ratio0, norms0[1][:], M // 2, M)
-        w3_q = [quantise_w3(0, "w1_g110"), quantise_w3(1, "picked01")]
+        normalise(nc.vector, z0_values[:, SHARE * PACK :], ratio0, norms0[1][:], SHARE, M)
+        w3_q = [quantise_w3(0, "w1_g002", w3_g[:1]), quantise_w3(1, "picked01", w3_g[1:])]
         z0 = quantise_z("z0", z0_values, M, "w3_g0")
 
         def last_pass(acc, b, z, first, j, place, lo, hi, start, stop):
@@ -338,7 +350,7 @@ def tile_list_wavelet_tree_contexts_kernel(
                 for place in range(2):
                     last_pass(accs[piece, pair], 0, z0, 0, 2 * pair + place, place, lo, hi, place == 0, False)
         for piece, (lo, hi) in enumerate(PIECES):
-            z1_values = held(f"z1{lo}", [P, (hi - lo) * PACK], BF16, ("z0", "w3_g1", None)[piece])
+            z1_values = held(f"z1{lo}", [P, (hi - lo) * PACK], BF16, ("z0", "tab_w0", None)[piece])
             normalise(nc.vector, z1_values[:], ratio1, norms1[piece][:], lo, hi)
             z1 = quantise_z(f"z1{lo}", z1_values, hi - lo)
             for pair in range(2):

@@ -23,7 +23,6 @@ PACK = 4
 PASS = P * PACK
 BANK = 512
 PIECES = ((0, 256), (256, 384), (384, 512))
-SHARE = 192
 
 
 def tile_list_wavelet_tree_contexts_kernel(
@@ -221,13 +220,8 @@ def tile_list_wavelet_tree_contexts_kernel(
         w3_raw = [load_w3(0, "tab_s"), load_w3(1, "w1_g000")]
         first_product(0, range(8))
         w1_q[0, 1] = quantise_w1(0, 1, w1_raw[0, 1], (("gpsimd",) * PACK,))
-        w1_q[1, 1] = quantise_w1(1, 1, w1_raw[1, 1], (("gpsimd", "gpsimd", "scalar", "scalar"),), "w1_g010")
-        picked = [
-            [
-                pick(held(f"picked0{t}", [P, M], F32, after)[:], 0, t)
-                for t, after in enumerate((None, None, "w1_raw00", "w1_g002"))
-            ]
-        ]
+        w1_q[1, 1] = quantise_w1(1, 1, w1_raw[1, 1], (("scalar",) * PACK,), "w1_c10")
+        picked = [[pick(held(f"picked0{t}", [P, M], F32)[:], 0, t) for t in range(PACK)]]
         first_product(1, range(4, 8))
 
         w2_s = held("w2_s", [P, 2 * H], U8)
@@ -235,12 +229,12 @@ def tile_list_wavelet_tree_contexts_kernel(
             out=w2_s[:].bitcast(I32).rearrange("p (ab t g w) -> p ab t g w", t=PACK, g=16, w=2),
             in_=w2_s_raw[:].bitcast(I32).rearrange("p (ab g t w) -> p ab t g w", t=PACK, g=16, w=2),
         )
-        w2_w = held("w2_w", [P, 2 * 2 * H], U8, "damping03")
+        w2_w = held("w2_w", [P, 2 * 2 * H], U8, "w1_g010")
         nc.gpsimd.tensor_copy(
             out=w2_w[:].bitcast(I32).rearrange("p (ab t g w) -> p ab t g w", t=PACK, g=16, w=4),
             in_=w2_w_raw[:].rearrange("p a (b g t w) -> p (a b) t g w", t=PACK, g=16, w=4),
         )
-        v2_w = held("v2_w", [P, 2 * M], U32, "w1_g010")
+        v2_w = held("v2_w", [P, 2 * M], U32, "w1_c10")
         for a in range(2):
             nc.vector.tensor_copy(
                 out=v2_w[:, a * M : (a + 1) * M], in_=tab2_w[:, a * T2 : (a + 1) * T2].indirect(idx2[:])
@@ -248,7 +242,7 @@ def tile_list_wavelet_tree_contexts_kernel(
 
         def second_product(b):
             ratio = held(f"ratio{b}", [P, PACK, M], F32)
-            square = held(f"square{b}", [P, PACK, M], F32, ("tab_w0", "w1_g000")[b])
+            square = held(f"square{b}", [P, PACK, M], F32, ("tab_w0", "w1_raw00")[b])
             for t in range(PACK):
                 acc = bank(f"b{b}{t}", t)
                 for a in range(2):
@@ -271,94 +265,98 @@ def tile_list_wavelet_tree_contexts_kernel(
                 )
             return ratio, square
 
-        def inverse_root(name, square, lo, hi, after=None):
-            norm = held(name, [P, PACK, hi - lo], F32, after)
+        def inverse_root(name, square, lo, hi):
+            norm = held(name, [P, PACK, hi - lo], F32)
             nc.scalar.activation(out=norm[:], in_=square[:, :, lo:hi], func=ACT.Abs_reciprocal_sqrt, bias=1.0)
             return norm
 
-        def normalise(engine, z, ratio, norm, lo, hi):
-            engine.tensor_tensor(
+        def normalise(z, ratio, norm, lo, hi):
+            nc.vector.tensor_tensor(
                 out=z.rearrange("p (c i t) -> p c t i", i=4, t=PACK),
                 in0=ratio[:, :, lo:hi].rearrange("p t (c i) -> p c t i", i=4),
                 in1=norm.rearrange("p t (c i) -> p c t i", i=4),
                 op=MULT,
             )
 
-        def quantise_z(name, z, width, after=None):
-            codes = held(name + "_c", [P, width], U32, after)
+        def quantise_z(name, z, width):
+            codes = held(name + "_c", [P, width], U32)
             scales = held(name + "_s", [P, width], U8)
             nc.vector.quantize_mx(out=codes[:].bitcast(FP8X4), scales=scales[:], in_=z[:])
             return codes, scales
 
-        def round_w3_on_gpsimd(b, width):
-            for n0 in range(0, width, P):
+        def round_w3(b):
+            grouped = held(f"w3_g{b}", [P, N * PACK], BF16)
+            for n0 in range(0, N, P):
                 round_on_gpsimd(
-                    w3_g[b][:, n0 * PACK : (n0 + P) * PACK].rearrange("p (n t) -> p n t", t=PACK),
+                    grouped[:, n0 * PACK : (n0 + P) * PACK].rearrange("p (n t) -> p n t", t=PACK),
                     w3_raw[b][:].rearrange("p (t n) -> p n t", t=PACK)[:, n0 : n0 + P, :],
                 )
+            return grouped
 
-        def quantise_w3(b, after, parts):
+        def quantise_w3(b, after):
             codes = held(f"w3_c{b}", [P, N], U32, after)
             scales = held(f"w3_s{b}", [P, N], U8)
-            width = N // len(parts)
-            for place, grouped in enumerate(parts):
-                cols = slice(place * width, (place + 1) * width)
-                nc.vector.quantize_mx(out=codes[:, cols].bitcast(FP8X4), scales=scales[:, cols], in_=grouped[:])
+            nc.vector.quantize_mx(out=codes[:].bitcast(FP8X4), scales=scales[:], in_=w3_g[b][:])
             return codes, scales
 
-        w3_g = [held("w3_g0", [P, N * PACK], BF16), held("w3_g1", [P, N // 2 * PACK], BF16)]
-        round_w3_on_gpsimd(0, N)
-        round_w3_on_gpsimd(1, N // 2)
+        w3_g = [round_w3(b) for b in range(2)]
         inv_gains = held("inv_gains", [P, 2 * PACK], F32, "w1_c11")
         nc.scalar.activation(out=inv_gains[:], in_=gains_squared[:], func=ACT.Abs_reciprocal_sqrt)
         picked.append([pick(held("picked10", [P, M], F32)[:], 1, 0)])
         ratio0, square0 = second_product(0)
-        norms0 = [inverse_root(f"norm0{lo}", square0, lo, hi) for lo, hi in ((0, SHARE), (SHARE, M))]
-        z0_values = held("z0", [P, M * PACK], BF16)
-        normalise(nc.gpsimd, z0_values[:, : SHARE * PACK], ratio0, norms0[0][:], 0, SHARE)
-        w3_g.append(held("w3_g2", [P, N // 2 * PACK], BF16, "tab_w0"))
-        nc.scalar.copy(
-            out=w3_g[2][:].rearrange("p (c i t) -> p c t i", i=4, t=PACK),
-            in_=w3_raw[1][:].rearrange("p (t c i) -> p c t i", t=PACK, i=4)[:, N // 8 :],
-        )
+        half = M // 2
+        early = [inverse_root("norm00", square0, 0, half)]
         picked[1].extend(
             pick(held(f"picked1{t}", [P, M], F32, after)[:], 1, t)
-            for t, after in ((1, "w1_raw00"), (2, "w1_g002"), (3, "picked01"))
+            for t, after in ((1, "picked02"), (2, "picked03"), (3, "picked01"))
         )
         ratio1, square1 = second_product(1)
-        norms1 = [inverse_root(f"norm1{lo}", square1, lo, hi) for lo, hi in PIECES]
-        normalise(nc.vector, z0_values[:, SHARE * PACK :], ratio0, norms0[1][:], SHARE, M)
-        w3_q = [quantise_w3(0, "w1_g002", w3_g[:1]), quantise_w3(1, "picked01", w3_g[1:])]
-        z0 = quantise_z("z0", z0_values, M, "w3_g0")
+        early.append(inverse_root("norm10", square1, 0, half))
+        norm1 = inverse_root("norm11", square1, half, M)
+        norm0 = held("norm01", [P, PACK * half], F32, "w1_raw00")
+        late = []
+        for lo, hi in PIECES[1:]:
+            late.append(norm0[:, (lo - half) * PACK : (hi - half) * PACK].rearrange("p (t m) -> p t m", t=PACK))
+            nc.scalar.activation(out=late[-1], in_=square0[:, :, lo:hi], func=ACT.Abs_reciprocal_sqrt, bias=1.0)
 
-        def last_pass(acc, b, z, first, j, place, lo, hi, start, stop):
+        def children(b, lo, hi, ratio, norm, after=None):
+            values = held(f"z{b}{lo}_values", [P, (hi - lo) * PACK], BF16, after)
+            normalise(values[:], ratio, norm, lo, hi)
+            return values
+
+        def last_pass(acc, step, b, z, first, j, place, lo, hi):
             nc.tensor.matmul_mx(
                 out=acc[:, place * (hi - lo) : (place + 1) * (hi - lo)],
                 lhsT=w3_q[b][0][:, j * P : (j + 1) * P].bitcast(FP8X4),
                 lhsT_scale=w3_q[b][1][:, j * P : (j + 1) * P],
                 rhs=z[0][:, lo - first : hi - first].bitcast(FP8X4),
                 rhs_scale=z[1][:, lo - first : hi - first],
-                start=start,
-                stop=stop,
+                start=(step == 0 and place == 0),
+                stop=(step == 1 and place == 1),
             )
 
         out_rows = out.rearrange("(j p) m -> p j m", p=P)
-        accs = {}
-        for piece, (lo, hi) in enumerate(PIECES):
+
+        def last_product(piece, operands):
+            lo, hi = PIECES[piece]
+            accs = [bank(f"o{piece}{pair}", (4 + 2 * piece + pair) % 8) for pair in range(2)]
+            for step, (b, z, first) in enumerate(operands):
+                for pair in range(2):
+                    for place in range(2):
+                        last_pass(accs[pair], step, b, z, first, 2 * pair + place, place, lo, hi)
             for pair in range(2):
-                accs[piece, pair] = bank(f"o{piece}{pair}", (4 + 2 * piece + pair) % 8)
-                for place in range(2):
-                    last_pass(accs[piece, pair], 0, z0, 0, 2 * pair + place, place, lo, hi, place == 0, False)
-        for piece, (lo, hi) in enumerate(PIECES):
-            z1_values = held(f"z1{lo}", [P, (hi - lo) * PACK], BF16, ("z0", "tab_w0", None)[piece])
-            normalise(nc.vector, z1_values[:], ratio1, norms1[piece][:], lo, hi)
-            z1 = quantise_z(f"z1{lo}", z1_values, hi - lo)
-            for pair in range(2):
-                acc = accs[piece, pair]
-                for place in range(2):
-                    last_pass(acc, 1, z1, lo, 2 * pair + place, place, lo, hi, False, place == 1)
                 staged = held(f"staged{piece}{pair}", [P, 2 * (hi - lo)], F32)
-                round_on("vector" if hi == M and pair == 1 else "scalar", staged[:], acc[:, 0 : 2 * (hi - lo)])
+                round_on("vector" if hi == M and pair else "scalar", staged[:], accs[pair][:, 0 : 2 * (hi - lo)])
                 nc.sync.dma_start(
                     out=out_rows[:, 2 * pair : 2 * pair + 2, lo:hi], in_=staged[:].rearrange("p (j m) -> p j m", j=2)
                 )
+
+        values = children(0, 0, half, ratio0, early[0][:])
+        w3_q = [quantise_w3(0, "picked03"), quantise_w3(1, "picked01")]
+        z0 = quantise_z("z00", values, half)
+        z1 = quantise_z("z10", children(1, 0, half, ratio1, early[1][:]), half)
+        last_product(0, ((0, z0, 0), (1, z1, 0)))
+        z1 = quantise_z("z11", children(1, half, M, ratio1, norm1[:], "z10_values"), half)
+        z0 = [quantise_z(f"z0{lo}", children(0, lo, hi, ratio0, norm), hi - lo) for (lo, hi), norm in zip(PIECES[1:], late)]
+        for piece in (1, 2):
+            last_product(piece, ((1, z1, half), (0, z0[piece - 1], PIECES[piece][0])))

@@ -152,22 +152,22 @@ def tile_list_wavelet_tree_contexts_kernel(
         w1_raw[1, 0] = load_w1(1, 0, "w1_g000")
         w1_raw[0, 1] = load_w1(0, 1, "w1_raw00")
         w1_raw[1, 1] = load_w1(1, 1, "w1_g002")
-        w2_s_raw = held("w2_s_raw", [P, 2 * H], U8, "tab2_s")
+        w2_s_raw = held("w2_s_raw", [P, 2 * H], U8, "picked_s")
         nc.gpsimd.memset(w2_s_raw[:].bitcast(I32), 0)
         for q in range(4):
             nc.sync.dma_start(
                 out=w2_s_raw[32 * q : 32 * q + 4, :].bitcast(I32).rearrange("r (a c) -> r a c", a=2),
                 in_=w2_scales.bitcast(I32)[:, 4 * q : 4 * q + 4, :].rearrange("a r c -> r a c"),
             )
-        w2_w_raw = held("w2_w_raw", [P, 2, H // 2], I32, "picked_s")
-        nc.sync.dma_start(out=w2_w_raw[:], in_=w2_words.bitcast(I32).rearrange("a p c -> p a c"))
+        tab2_w = [held(f"tab2_w{a}", [P, T2], U32, after) for a, after in enumerate(("gain_rows", "identity"))]
+        for a in range(2):
+            load_words(tab2_w[a][:], tab2_words, a)
 
         v_w = {}
         for half in range(2):
             v_w[0, half] = gather(f"v_w0{half}", U32, tab_w0[:], idx[:, 32 * half : 32 * (half + 1)], BANK)
-        tab2_w = held("tab2_w", [P, 2 * T2], U32, "tab_w0")
-        for a in range(2):
-            load_words(tab2_w[:, a * T2 : (a + 1) * T2], tab2_words, a)
+        w2_w_raw = held("w2_w_raw", [P, 2, H // 2], I32, "tab_w0")
+        nc.sync.dma_start(out=w2_w_raw[:], in_=w2_words.bitcast(I32).rearrange("a p c -> p a c"))
 
         for half in range(2):
             v_w[1, half] = gather(f"v_w1{half}", U32, tab_w1[:], idx[:, 32 * half : 32 * (half + 1)], BANK)
@@ -202,7 +202,7 @@ def tile_list_wavelet_tree_contexts_kernel(
                         accs[t, half] = bank(f"h{b}{t}{half}", banks[2 * (t - t0) + half])
                         first_pass(accs[t, half], 0, b, t, half)
                 for t in range(t0, t0 + together):
-                    damping[b, t] = held(f"damping{b}{t}", [P, S], F32)
+                    damping[b, t] = held(f"damping{b}{t}", [P, S], F32, f"damping{t}")
                     for half in range(2):
                         first_pass(accs[t, half], 1, b, t, half)
                         nc.scalar.activation(
@@ -221,28 +221,33 @@ def tile_list_wavelet_tree_contexts_kernel(
         first_product(0, range(8))
         w1_q[0, 1] = quantise_w1(0, 1, w1_raw[0, 1], (("gpsimd",) * PACK,))
         w1_q[1, 1] = quantise_w1(1, 1, w1_raw[1, 1], (("scalar",) * PACK,), "w1_c10")
-        picked = [[pick(held(f"picked0{t}", [P, M], F32)[:], 0, t) for t in range(PACK)]]
+        picked = [
+            [
+                pick(held(f"picked0{t}", [P, M], F32, after)[:], 0, t)
+                for t, after in enumerate((None, None, None, "w1_raw00"))
+            ]
+        ]
         first_product(1, range(4, 8))
 
-        w2_s = held("w2_s", [P, 2 * H], U8)
+        w2_s = held("w2_s", [P, 2 * H], U8, "w1_c10")
         nc.gpsimd.tensor_copy(
             out=w2_s[:].bitcast(I32).rearrange("p (ab t g w) -> p ab t g w", t=PACK, g=16, w=2),
             in_=w2_s_raw[:].bitcast(I32).rearrange("p (ab g t w) -> p ab t g w", t=PACK, g=16, w=2),
         )
-        w2_w = held("w2_w", [P, 2 * 2 * H], U8, "w1_g010")
+        w2_w = held("w2_w", [P, 2 * 2 * H], U8, "picked_s")
         nc.gpsimd.tensor_copy(
             out=w2_w[:].bitcast(I32).rearrange("p (ab t g w) -> p ab t g w", t=PACK, g=16, w=4),
             in_=w2_w_raw[:].rearrange("p a (b g t w) -> p (a b) t g w", t=PACK, g=16, w=4),
         )
-        v2_w = held("v2_w", [P, 2 * M], U32, "w1_c10")
+        v2_w = held("v2_w", [P, 2 * M], U32, "w1_g002")
         for a in range(2):
             nc.vector.tensor_copy(
-                out=v2_w[:, a * M : (a + 1) * M], in_=tab2_w[:, a * T2 : (a + 1) * T2].indirect(idx2[:])
+                out=v2_w[:, a * M : (a + 1) * M], in_=tab2_w[a][:].indirect(idx2[:])
             )
 
         def second_product(b):
-            ratio = held(f"ratio{b}", [P, PACK, M], F32)
-            square = held(f"square{b}", [P, PACK, M], F32, ("tab_w0", "w1_raw00")[b])
+            ratio = held(f"ratio{b}", [P, PACK, M], F32, ("damping1", None)[b])
+            square = held(f"square{b}", [P, PACK, M], F32, ("tab_w0", "square1")[b])
             for t in range(PACK):
                 acc = bank(f"b{b}{t}", t)
                 for a in range(2):
@@ -302,18 +307,18 @@ def tile_list_wavelet_tree_contexts_kernel(
         w3_g = [round_w3(b) for b in range(2)]
         inv_gains = held("inv_gains", [P, 2 * PACK], F32, "w1_c11")
         nc.scalar.activation(out=inv_gains[:], in_=gains_squared[:], func=ACT.Abs_reciprocal_sqrt)
-        picked.append([pick(held("picked10", [P, M], F32)[:], 1, 0)])
+        picked.append([pick(held(f"picked1{t}", [P, M], F32)[:], 1, t) for t in range(2)])
         ratio0, square0 = second_product(0)
         half = M // 2
         early = [inverse_root("norm00", square0, 0, half)]
         picked[1].extend(
             pick(held(f"picked1{t}", [P, M], F32, after)[:], 1, t)
-            for t, after in ((1, "picked02"), (2, "picked03"), (3, "picked01"))
+            for t, after in ((2, "picked02"), (3, "w1_raw00"))
         )
         ratio1, square1 = second_product(1)
         early.append(inverse_root("norm10", square1, 0, half))
         norm1 = inverse_root("norm11", square1, half, M)
-        norm0 = held("norm01", [P, PACK * half], F32, "w1_raw00")
+        norm0 = held("norm01", [P, PACK * half], F32, "square1")
         late = []
         for lo, hi in PIECES[1:]:
             late.append(norm0[:, (lo - half) * PACK : (hi - half) * PACK].rearrange("p (t m) -> p t m", t=PACK))
@@ -352,7 +357,7 @@ def tile_list_wavelet_tree_contexts_kernel(
                 )
 
         values = children(0, 0, half, ratio0, early[0][:])
-        w3_q = [quantise_w3(0, "picked03"), quantise_w3(1, "picked01")]
+        w3_q = [quantise_w3(0, "picked02"), quantise_w3(1, "w1_raw00")]
         z0 = quantise_z("z00", values, half)
         z1 = quantise_z("z10", children(1, 0, half, ratio1, early[1][:]), half)
         last_product(0, ((0, z0, 0), (1, z1, 0)))

@@ -216,7 +216,7 @@ def tile_list_wavelet_tree_contexts_kernel(
             nc.vector.tensor_copy(out=dst, in_=damping[b, t][:].indirect(parent[:]))
             return dst
 
-        w1_q[1, 0] = quantise_w1(1, 0, w1_raw[1, 0], (("vector",), ("scalar",), ("vector", "scalar")))
+        w1_q[1, 0] = quantise_w1(1, 0, w1_raw[1, 0], (("scalar",), ("scalar",), ("gpsimd", "gpsimd")))
         w3_raw = [load_w3(0, "tab_s"), load_w3(1, "w1_g000")]
         first_product(0, range(8))
         w1_q[0, 1] = quantise_w1(0, 1, w1_raw[0, 1], (("gpsimd",) * PACK,))

@@ -1,3 +1,4 @@
+import math
 from contextlib import ExitStack
 
 import concourse.mybir as mybir
@@ -18,6 +19,9 @@ ACT = mybir.ActivationFunctionType
 MULT = mybir.AluOpType.mult
 ADD = mybir.AluOpType.add
 
+SIZES = {F32: 4, I32: 4, U32: 4, BF16: 2, U8: 1}
+KIB = 1024
+
 P = 128
 PACK = 4
 PASS = P * PACK
@@ -34,8 +38,15 @@ def tile_list_wavelet_tree_contexts_kernel(
         keep = ctx.enter_context(tc.tile_pool(name="keep", bufs=1))
         psum = ctx.enter_context(tc.psum_pool(name="psum", bufs=1))
 
-        def held(name, shape, dtype, after=None):
-            return keep.tile(shape, dtype, name=name, tag=after or name, align_bytes=64)
+        places = {"end": 0}
+
+        def held(name, shape, dtype, after=None, at=0, room=0):
+            if after is None:
+                places[name] = places["end"]
+                places["end"] = places["end"] + max(room, 64, math.prod(shape[1:]) * SIZES[dtype])
+            else:
+                places[name] = places[after] + at
+            return keep.tile(shape, dtype, name=name, offset=places[name], align_bytes=64)
 
         def bank(name, number):
             return psum.tile([P, BANK], F32, name=name, tag=f"bank{number}")
@@ -44,8 +55,8 @@ def tile_list_wavelet_tree_contexts_kernel(
         idx2 = lists.tile([P, M // 16], U16, name="idx2")
         parent = lists.tile([P, M // 16], U16, name="parent")
 
-        def load_scale_rows(name, src, width, first):
-            rows = held(name, [P, width], U8)
+        def load_scale_rows(name, src, width, first, room=0):
+            rows = held(name, [P, width], U8, room=room)
             nc.sync.dma_start(
                 out=rows[first : first + 32, :].bitcast(I32), in_=src.bitcast(I32).rearrange("a q c -> q a c")
             )
@@ -72,8 +83,8 @@ def tile_list_wavelet_tree_contexts_kernel(
                 )
             return plane
 
-        def gather(name, dtype, window, offsets, width, after=None):
-            picked = held(name, [P, width], dtype, after)
+        def gather(name, dtype, window, offsets, width, after=None, at=0, room=0):
+            picked = held(name, [P, width], dtype, after, at, room)
             nc.vector.tensor_copy(out=picked[:], in_=window.indirect(offsets))
             return picked
 
@@ -86,33 +97,40 @@ def tile_list_wavelet_tree_contexts_kernel(
         def round_on_gpsimd(dst, src):
             nc.gpsimd.tensor_scalar(out=dst, in0=src, scalar1=1.0, scalar2=0.0, op0=MULT, op1=ADD)
 
-        def quantise_w1(a, b, raw, groups, after=None):
-            codes = held(f"w1_c{a}{b}", [P, PASS], U32)
-            scales = held(f"w1_s{a}{b}", [P, PASS], U8)
-            t0 = 0
-            for engines in groups:
-                width = len(engines)
-                grouped = held(f"w1_g{a}{b}{t0}", [P, width * PASS], BF16, after)
-                for u, engine in enumerate(engines):
-                    dst = grouped[:, u * PASS : (u + 1) * PASS]
-                    if engine == "gpsimd":
-                        round_on_gpsimd(
-                            dst.rearrange("p (g i j) -> p g i j", g=16, j=PACK),
-                            raw[:].rearrange("p j (g t i) -> p t g i j", t=PACK, i=8)[:, t0 + u],
-                        )
-                    else:
-                        round_on(
-                            engine,
-                            dst.rearrange("p (g h i j) -> p g h j i", g=16, h=2, i=4),
-                            raw[:].rearrange("p j (g t h i) -> p t g h j i", t=PACK, h=2, i=4)[:, t0 + u],
-                        )
-                cols = slice(t0 * P, (t0 + width) * P)
-                nc.vector.quantize_mx(out=codes[:, cols].bitcast(FP8X4), scales=scales[:, cols], in_=grouped[:])
-                t0 = t0 + width
+        def round_w1(a, b, t0, engines, room=0):
+            grouped = held(f"w1_g{a}{b}{t0}", [P, len(engines) * PASS], BF16, room=room)
+            raw = w1_raw[a, b]
+            for u, engine in enumerate(engines):
+                dst = grouped[:, u * PASS : (u + 1) * PASS]
+                if engine == "gpsimd":
+                    round_on_gpsimd(
+                        dst.rearrange("p (g i j) -> p g i j", g=16, j=PACK),
+                        raw[:].rearrange("p j (g t i) -> p t g i j", t=PACK, i=8)[:, t0 + u],
+                    )
+                else:
+                    round_on(
+                        engine,
+                        dst.rearrange("p (g h i j) -> p g h j i", g=16, h=2, i=4),
+                        raw[:].rearrange("p j (g t h i) -> p t g h j i", t=PACK, h=2, i=4)[:, t0 + u],
+                    )
+            return grouped
+
+        def quantise(name, values, after=None, at=0, room=0):
+            width = values.shape[1] // PACK
+            codes = held(name + "_c", [P, width], U32, after, at, room)
+            scales = held(name + "_s", [P, width], U8)
+            nc.vector.quantize_mx(out=codes[:].bitcast(FP8X4), scales=scales[:], in_=values)
             return codes, scales
 
+        w1_q = {}
+
+        def quantise_w1(a, b, t0, values, after=None, at=0, room=0):
+            codes, scales = quantise(f"w1_{a}{b}{t0}", values, after, at, room)
+            for u in range(values.shape[1] // PASS):
+                w1_q[a, b, t0 + u] = codes[:, u * P : (u + 1) * P], scales[:, u * P : (u + 1) * P]
+
         nc.sync.dma_start(idx[:], offs)
-        tab_s = load_scale_rows("tab_s", tab_scales, T, 0)
+        tab_s = load_scale_rows("tab_s", tab_scales, T, 0, 16 * KIB)
         nc.sync.dma_start(idx2[:], offs2)
         tab2_s = load_scale_rows("tab2_s", tab2_scales, T2, 64)
         w1_raw = {(0, 0): load_w1(0, 0)}
@@ -123,17 +141,17 @@ def tile_list_wavelet_tree_contexts_kernel(
             for lo, hi in spans:
                 nc.vector.memset(rows[lo:hi, :].bitcast(I32), 0)
 
-        gain_rows = held("gain_rows", [P, P], F32)
+        gain_rows = held("gain_rows", [P, P], F32, room=8 * KIB)
         nc.gpsimd.memset(gain_rows[:], 0.0)
         for b in range(2):
             nc.gpsimd.dma_start(
                 out=gain_rows[b * PACK : (b + 1) * PACK, :].rearrange("t (g i) -> t g i", i=8),
                 in_=gain[b * PASS : (b + 1) * PASS].rearrange("(g t i) -> t g i", t=PACK, i=8),
             )
-        identity = held("identity", [P, P], F32)
+        identity = held("identity", [P, P], F32, room=8 * KIB)
         make_identity(nc, identity[:])
 
-        picked_s = gather("picked_s", U8, tab_s[:], idx[:], S)
+        picked_s = gather("picked_s", U8, tab_s[:], idx[:], S, room=2 * KIB)
         v_s = to_plane(nc.sync, "v_s", picked_s, 0, S)
         tab_w1 = held("tab_w1", [P, T], U32, "tab_s")
         load_words(tab_w1[:], tab_words, 1)
@@ -145,10 +163,11 @@ def tile_list_wavelet_tree_contexts_kernel(
         nc.tensor.transpose(turned[:, 0:P], gain_rows[:], identity[:])
         gains = held("gains", [P, 2 * PACK], F32)
         nc.scalar.copy(out=gains[:], in_=turned[:, 0 : 2 * PACK])
-        gains_squared = held("gains_squared", [P, 2 * PACK], F32)
-        nc.scalar.activation(out=gains_squared[:], in_=turned[:, 0 : 2 * PACK], func=ACT.Square)
+        inv_gains = held("inv_gains", [P, 2 * PACK], F32)
+        nc.vector.reciprocal(out=inv_gains[:], in_=gains[:])
 
-        w1_q = {(0, 0): quantise_w1(0, 0, w1_raw[0, 0], (("scalar", "scalar"), ("scalar", "scalar")))}
+        for t0 in (0, 2):
+            quantise_w1(0, 0, t0, round_w1(0, 0, t0, ("scalar", "scalar"), 8 * KIB)[:])
         w1_raw[1, 0] = load_w1(1, 0, "w1_g000")
         w1_raw[0, 1] = load_w1(0, 1, "w1_raw00")
         w1_raw[1, 1] = load_w1(1, 1, "w1_g002")
@@ -182,112 +201,94 @@ def tile_list_wavelet_tree_contexts_kernel(
         damping = {}
 
         def first_pass(acc, a, b, t, half):
-            codes, scales = w1_q[a, b]
+            codes, scales = w1_q[a, b, t]
             nc.tensor.matmul_mx(
                 out=acc[:],
-                lhsT=codes[:, t * P : (t + 1) * P].bitcast(FP8X4),
-                lhsT_scale=scales[:, t * P : (t + 1) * P],
+                lhsT=codes.bitcast(FP8X4),
+                lhsT_scale=scales,
                 rhs=v_w[a, half][:].bitcast(FP8X4),
                 rhs_scale=v_s[:, a * S + half * BANK : a * S + (half + 1) * BANK],
                 start=(a == 0),
                 stop=(a == 1),
             )
 
-        def first_product(b, banks):
-            together = len(banks) // 2
-            for t0 in range(0, PACK, together):
-                accs = {}
-                for t in range(t0, t0 + together):
-                    for half in range(2):
-                        accs[t, half] = bank(f"h{b}{t}{half}", banks[2 * (t - t0) + half])
-                        first_pass(accs[t, half], 0, b, t, half)
-                for t in range(t0, t0 + together):
-                    damping[b, t] = held(f"damping{b}{t}", [P, S], F32, f"damping{t}")
-                    for half in range(2):
-                        first_pass(accs[t, half], 1, b, t, half)
-                        nc.scalar.activation(
-                            out=damping[b, t][:, half * BANK : (half + 1) * BANK],
-                            in_=accs[t, half][:],
-                            func=ACT.Exp,
-                            scale=-0.5,
-                        )
+        def first_product(b):
+            for t in range(PACK):
+                accs = [bank(f"h{b}{t}{half}", 2 * t + half) for half in range(2)]
+                for half in range(2):
+                    first_pass(accs[half], 0, b, t, half)
+                damping[b, t] = held(f"damping{b}{t}", [P, S], F32, f"damping0{t}" if b else None)
+                for half in range(2):
+                    first_pass(accs[half], 1, b, t, half)
+                    nc.scalar.activation(
+                        out=damping[b, t][:, half * BANK : (half + 1) * BANK],
+                        in_=accs[half][:],
+                        func=ACT.Exp,
+                        scale=-0.5,
+                    )
 
         def pick(dst, b, t):
             nc.vector.tensor_copy(out=dst, in_=damping[b, t][:].indirect(parent[:]))
             return dst
 
-        w1_q[1, 0] = quantise_w1(1, 0, w1_raw[1, 0], (("scalar",), ("scalar",), ("gpsimd", "gpsimd")))
+        for t0, engines in ((0, ("vector",)), (1, ("vector",)), (2, ("vector", "vector"))):
+            quantise_w1(1, 0, t0, round_w1(1, 0, t0, engines)[:])
         w3_raw = [load_w3(0, "tab_s"), load_w3(1, "w1_g000")]
-        first_product(0, range(8))
-        w1_q[0, 1] = quantise_w1(0, 1, w1_raw[0, 1], (("gpsimd",) * PACK,))
-        w1_q[1, 1] = quantise_w1(1, 1, w1_raw[1, 1], (("scalar",) * PACK,), "w1_c10")
-        picked = [
-            [
-                pick(held(f"picked0{t}", [P, M], F32, after)[:], 0, t)
-                for t, after in enumerate((None, None, None, "w1_raw00"))
-            ]
-        ]
-        first_product(1, range(4, 8))
+        first_product(0)
+        third = round_w1(0, 1, 0, ("gpsimd",) * PACK)
+        picked = [[pick(held(f"picked0{t}", [P, M], F32)[:], 0, t) for t in range(3)]]
+        quantise_w1(0, 1, 0, third[:, : 2 * PASS], "w1_raw01", 2 * KIB)
+        picked[0].append(pick(held("picked03", [P, M], F32, "w1_raw01")[:], 0, 3))
+        v2_w = [gather("v2_w0", U32, tab2_w[0][:], idx2[:], M, "w1_raw01", 4 * KIB)]
+        quantise_w1(1, 1, 0, round_w1(1, 1, 0, ("scalar",) * PACK)[:], room=4 * KIB)
+        quantise_w1(0, 1, 2, third[:, 2 * PASS :], "w1_raw11")
+        v2_w.append(gather("v2_w1", U32, tab2_w[1][:], idx2[:], M, "w1_raw11", 2 * KIB))
+        first_product(1)
 
-        w2_s = held("w2_s", [P, 2 * H], U8, "w1_c10")
+        w2_s = held("w2_s", [P, 2 * H], U8, "w1_g010")
         nc.gpsimd.tensor_copy(
             out=w2_s[:].bitcast(I32).rearrange("p (ab t g w) -> p ab t g w", t=PACK, g=16, w=2),
             in_=w2_s_raw[:].bitcast(I32).rearrange("p (ab g t w) -> p ab t g w", t=PACK, g=16, w=2),
         )
-        w2_w = held("w2_w", [P, 2 * 2 * H], U8, "picked_s")
-        nc.gpsimd.tensor_copy(
-            out=w2_w[:].bitcast(I32).rearrange("p (ab t g w) -> p ab t g w", t=PACK, g=16, w=4),
-            in_=w2_w_raw[:].rearrange("p a (b g t w) -> p (a b) t g w", t=PACK, g=16, w=4),
-        )
-        v2_w = held("v2_w", [P, 2 * M], U32, "w1_g002")
-        for a in range(2):
-            nc.vector.tensor_copy(
-                out=v2_w[:, a * M : (a + 1) * M], in_=tab2_w[a][:].indirect(idx2[:])
+        w2_w = []
+        for b, after in enumerate(("picked_s", None)):
+            w2_w.append(held(f"w2_w{b}", [P, 2 * H], U8, after))
+            nc.gpsimd.tensor_copy(
+                out=w2_w[b][:].bitcast(I32).rearrange("p (a t g w) -> p a t g w", t=PACK, g=16, w=4),
+                in_=w2_w_raw[:].rearrange("p a (b g t w) -> p b a t g w", t=PACK, g=16, w=4)[:, b],
             )
 
-        def second_product(b):
-            ratio = held(f"ratio{b}", [P, PACK, M], F32, ("damping1", None)[b])
-            square = held(f"square{b}", [P, PACK, M], F32, ("tab_w0", "square1")[b])
-            for t in range(PACK):
-                acc = bank(f"b{b}{t}", t)
-                for a in range(2):
-                    col = ((2 * a + b) * PACK + t) * P
-                    nc.tensor.matmul_mx(
-                        out=acc[:],
-                        lhsT=w2_w[:, 2 * col : 2 * (col + P)].bitcast(FP4X4),
-                        lhsT_scale=w2_s[:, col : col + P],
-                        rhs=v2_w[:, a * M : (a + 1) * M].bitcast(FP8X4),
-                        rhs_scale=v2_s[:, a * M : (a + 1) * M],
-                        start=(a == 0),
-                        stop=(a == 1),
-                    )
-                slot = b * PACK + t
-                nc.vector.scalar_tensor_tensor(
-                    out=ratio[:, t, :], in0=acc[:], scalar=gains[:, slot : slot + 1], in1=picked[b][t], op0=MULT, op1=MULT
-                )
-                nc.scalar.activation(
-                    out=square[:, t, :], in_=ratio[:, t, :], func=ACT.Square, scale=inv_gains[:, slot : slot + 1]
-                )
-            return ratio, square
+        ratio = [held("ratio0", [P, PACK, M], F32, "tab_w0", 4 * KIB), held("ratio1", [P, PACK, M], F32)]
+        square = [held(f"square{b}", [P, PACK, M], F32) for b in range(2)]
 
-        def inverse_root(name, square, lo, hi):
-            norm = held(name, [P, PACK, hi - lo], F32)
-            nc.scalar.activation(out=norm[:], in_=square[:, :, lo:hi], func=ACT.Abs_reciprocal_sqrt, bias=1.0)
-            return norm
-
-        def normalise(z, ratio, norm, lo, hi):
-            nc.vector.tensor_tensor(
-                out=z.rearrange("p (c i t) -> p c t i", i=4, t=PACK),
-                in0=ratio[:, :, lo:hi].rearrange("p t (c i) -> p c t i", i=4),
-                in1=norm.rearrange("p t (c i) -> p c t i", i=4),
-                op=MULT,
+        def second_product(b, t):
+            acc = bank(f"b{b}{t}", PACK * b + t)
+            for a in range(2):
+                col = ((2 * a + b) * PACK + t) * P
+                nc.tensor.matmul_mx(
+                    out=acc[:],
+                    lhsT=w2_w[b][:, 2 * P * (PACK * a + t) : 2 * P * (PACK * a + t + 1)].bitcast(FP4X4),
+                    lhsT_scale=w2_s[:, col : col + P],
+                    rhs=v2_w[a][:].bitcast(FP8X4),
+                    rhs_scale=v2_s[:, a * M : (a + 1) * M],
+                    start=(a == 0),
+                    stop=(a == 1),
+                )
+            slot = b * PACK + t
+            nc.vector.scalar_tensor_tensor(
+                out=ratio[b][:, t, :], in0=acc[:], scalar=gains[:, slot : slot + 1], in1=picked[b][t], op0=MULT, op1=MULT
+            )
+            nc.scalar.activation(
+                out=square[b][:, t, :], in_=ratio[b][:, t, :], func=ACT.Square, scale=inv_gains[:, slot : slot + 1]
             )
 
-        def quantise_z(name, z, width):
-            codes = held(name + "_c", [P, width], U32)
-            scales = held(name + "_s", [P, width], U8)
-            nc.vector.quantize_mx(out=codes[:].bitcast(FP8X4), scales=scales[:], in_=z[:])
-            return codes, scales
+        def inverse_root(b, lo, hi, after=None, at=0):
+            one = held(f"one{b}{lo}", [P, 1], F32, room=KIB)
+            nc.gpsimd.memset(one[:], 1.0)
+            norm[b, lo] = held(f"norm{b}{lo}", [P, PACK, hi - lo], F32, after, at)
+            nc.scalar.activation(
+                out=norm[b, lo][:], in_=square[b][:, :, lo:hi], func=ACT.Abs_reciprocal_sqrt, bias=one[:]
+            )
 
         def round_w3(b):
             grouped = held(f"w3_g{b}", [P, N * PACK], BF16)
@@ -298,57 +299,50 @@ def tile_list_wavelet_tree_contexts_kernel(
                 )
             return grouped
 
-        def quantise_w3(b, after):
-            codes = held(f"w3_c{b}", [P, N], U32, after)
-            scales = held(f"w3_s{b}", [P, N], U8)
-            nc.vector.quantize_mx(out=codes[:].bitcast(FP8X4), scales=scales[:], in_=w3_g[b][:])
-            return codes, scales
-
         w3_g = [round_w3(b) for b in range(2)]
-        inv_gains = held("inv_gains", [P, 2 * PACK], F32, "w1_c11")
-        nc.scalar.activation(out=inv_gains[:], in_=gains_squared[:], func=ACT.Abs_reciprocal_sqrt)
-        picked.append([pick(held(f"picked1{t}", [P, M], F32)[:], 1, t) for t in range(2)])
-        ratio0, square0 = second_product(0)
+        picked.append([pick(held("picked10", [P, M], F32)[:], 1, 0)])
+        for t in range(PACK):
+            second_product(0, t)
         half = M // 2
-        early = [inverse_root("norm00", square0, 0, half)]
-        picked[1].extend(
-            pick(held(f"picked1{t}", [P, M], F32, after)[:], 1, t)
-            for t, after in ((2, "picked02"), (3, "w1_raw00"))
-        )
-        ratio1, square1 = second_product(1)
-        early.append(inverse_root("norm10", square1, 0, half))
-        norm1 = inverse_root("norm11", square1, half, M)
-        norm0 = held("norm01", [P, PACK * half], F32, "square1")
-        late = []
-        for lo, hi in PIECES[1:]:
-            late.append(norm0[:, (lo - half) * PACK : (hi - half) * PACK].rearrange("p (t m) -> p t m", t=PACK))
-            nc.scalar.activation(out=late[-1], in_=square0[:, :, lo:hi], func=ACT.Abs_reciprocal_sqrt, bias=1.0)
+        norm = {}
+        inverse_root(0, 0, half, "w1_110_c")
+        second_product(1, 0)
+        for t, after in ((1, "picked02"), (2, "picked03"), (3, "picked10")):
+            picked[1].append(pick(held(f"picked1{t}", [P, M], F32, after)[:], 1, t))
+            second_product(1, t)
+        inverse_root(1, 0, half)
+        inverse_root(1, half, M)
+        for place, (lo, hi) in enumerate(PIECES[1:]):
+            inverse_root(0, lo, hi, "square1", 2 * place * KIB)
 
-        def children(b, lo, hi, ratio, norm, after=None):
+        def children(b, lo, hi, after=None):
             values = held(f"z{b}{lo}_values", [P, (hi - lo) * PACK], BF16, after)
-            normalise(values[:], ratio, norm, lo, hi)
-            return values
-
-        def last_pass(acc, step, b, z, first, j, place, lo, hi):
-            nc.tensor.matmul_mx(
-                out=acc[:, place * (hi - lo) : (place + 1) * (hi - lo)],
-                lhsT=w3_q[b][0][:, j * P : (j + 1) * P].bitcast(FP8X4),
-                lhsT_scale=w3_q[b][1][:, j * P : (j + 1) * P],
-                rhs=z[0][:, lo - first : hi - first].bitcast(FP8X4),
-                rhs_scale=z[1][:, lo - first : hi - first],
-                start=(step == 0 and place == 0),
-                stop=(step == 1 and place == 1),
+            nc.vector.tensor_tensor(
+                out=values[:].rearrange("p (c i t) -> p c t i", i=4, t=PACK),
+                in0=ratio[b][:, :, lo:hi].rearrange("p t (c i) -> p c t i", i=4),
+                in1=norm[b, lo][:].rearrange("p t (c i) -> p c t i", i=4),
+                op=MULT,
             )
+            return values
 
         out_rows = out.rearrange("(j p) m -> p j m", p=P)
 
         def last_product(piece, operands):
             lo, hi = PIECES[piece]
-            accs = [bank(f"o{piece}{pair}", (4 + 2 * piece + pair) % 8) for pair in range(2)]
+            accs = [bank(f"o{piece}{pair}", 2 * piece + pair) for pair in range(2)]
             for step, (b, z, first) in enumerate(operands):
                 for pair in range(2):
                     for place in range(2):
-                        last_pass(accs[pair], step, b, z, first, 2 * pair + place, place, lo, hi)
+                        j = 2 * pair + place
+                        nc.tensor.matmul_mx(
+                            out=accs[pair][:, place * (hi - lo) : (place + 1) * (hi - lo)],
+                            lhsT=w3_q[b][0][:, j * P : (j + 1) * P].bitcast(FP8X4),
+                            lhsT_scale=w3_q[b][1][:, j * P : (j + 1) * P],
+                            rhs=z[0][:, lo - first : hi - first].bitcast(FP8X4),
+                            rhs_scale=z[1][:, lo - first : hi - first],
+                            start=(step == 0 and place == 0),
+                            stop=(step == 1 and place == 1),
+                        )
             for pair in range(2):
                 staged = held(f"staged{piece}{pair}", [P, 2 * (hi - lo)], F32)
                 round_on("vector" if hi == M and pair else "scalar", staged[:], accs[pair][:, 0 : 2 * (hi - lo)])
@@ -356,12 +350,17 @@ def tile_list_wavelet_tree_contexts_kernel(
                     out=out_rows[:, 2 * pair : 2 * pair + 2, lo:hi], in_=staged[:].rearrange("p (j m) -> p j m", j=2)
                 )
 
-        values = children(0, 0, half, ratio0, early[0][:])
-        w3_q = [quantise_w3(0, "picked02"), quantise_w3(1, "w1_raw00")]
-        z0 = quantise_z("z00", values, half)
-        z1 = quantise_z("z10", children(1, 0, half, ratio1, early[1][:]), half)
+        values = children(0, 0, half, "picked02")
+        w3_q = [quantise(f"w3_{b}", w3_g[b][:], "w3_raw1", 2 * b * KIB) for b in range(2)]
+        z0 = quantise("z00", values[:], "w3_g0")
+        other = children(1, 0, half)
+        rest = children(1, half, M)
+        z1 = quantise("z10", other[:], f"one1{half}")
         last_product(0, ((0, z0, 0), (1, z1, 0)))
-        z1 = quantise_z("z11", children(1, half, M, ratio1, norm1[:], "z10_values"), half)
-        z0 = [quantise_z(f"z0{lo}", children(0, lo, hi, ratio0, norm), hi - lo) for (lo, hi), norm in zip(PIECES[1:], late)]
-        for piece in (1, 2):
-            last_product(piece, ((1, z1, half), (0, z0[piece - 1], PIECES[piece][0])))
+        values = [children(0, *PIECES[1])]
+        z1 = quantise("z1h", rest[:], f"one0{half}")
+        values.append(children(0, *PIECES[2]))
+        for piece, after in ((1, f"one0{PIECES[2][0]}"), (2, None)):
+            lo, hi = PIECES[piece]
+            z0 = quantise(f"z0{lo}", values[piece - 1][:], after)
+            last_product(piece, ((1, z1, half), (0, z0, lo)))

@@ -65,8 +65,8 @@ def tile_list_wavelet_tree_contexts_kernel(
         def load_words(dst, src, a):
             nc.sync.dma_start(out=dst.bitcast(I32), in_=src[a].rearrange("p c i -> p (c i)").bitcast(I32))
 
-        def load_w1(a, b, after=None):
-            raw = held(f"w1_raw{a}{b}", [P, PACK, PASS], F32, after)
+        def load_w1(a, b, after=None, room=0):
+            raw = held(f"w1_raw{a}{b}", [P, PACK, PASS], F32, after, room=room)
             nc.sync.dma_start(
                 out=raw[:],
                 in_=w1[a * PASS : (a + 1) * PASS, b * PASS : (b + 1) * PASS].rearrange("(p j) c -> p j c", j=PACK),
@@ -133,7 +133,7 @@ def tile_list_wavelet_tree_contexts_kernel(
         tab_s = load_scale_rows("tab_s", tab_scales, T, 0, 16 * KIB)
         nc.sync.dma_start(idx2[:], offs2)
         tab2_s = load_scale_rows("tab2_s", tab2_scales, T2, 64)
-        w1_raw = {(0, 0): load_w1(0, 0)}
+        w1_raw = {(0, 0): load_w1(0, 0, room=10 * KIB)}
         tab_w0 = held("tab_w0", [P, T], U32)
         load_words(tab_w0[:], tab_words, 0)
         nc.sync.dma_start(parent[:], pos1)
@@ -231,21 +231,20 @@ def tile_list_wavelet_tree_contexts_kernel(
             nc.vector.tensor_copy(out=dst, in_=damping[b, t][:].indirect(parent[:]))
             return dst
 
-        for t0, engines in ((0, ("vector",)), (1, ("vector",)), (2, ("vector", "vector"))):
+        for t0, engines in ((0, ("vector",)), (1, ("scalar",)), (2, ("vector", "scalar"))):
             quantise_w1(1, 0, t0, round_w1(1, 0, t0, engines)[:])
         w3_raw = [load_w3(0, "tab_s"), load_w3(1, "w1_g000")]
         first_product(0)
         third = round_w1(0, 1, 0, ("gpsimd",) * PACK)
         picked = [[pick(held(f"picked0{t}", [P, M], F32)[:], 0, t) for t in range(3)]]
-        quantise_w1(0, 1, 0, third[:, : 2 * PASS], "w1_raw01", 2 * KIB)
+        quantise_w1(0, 1, 0, third[:])
         picked[0].append(pick(held("picked03", [P, M], F32, "w1_raw01")[:], 0, 3))
         v2_w = [gather("v2_w0", U32, tab2_w[0][:], idx2[:], M, "w1_raw01", 4 * KIB)]
-        quantise_w1(1, 1, 0, round_w1(1, 1, 0, ("scalar",) * PACK)[:], room=4 * KIB)
-        quantise_w1(0, 1, 2, third[:, 2 * PASS :], "w1_raw11")
+        quantise_w1(1, 1, 0, round_w1(1, 1, 0, ("scalar",) * PACK)[:], "w1_raw01", 6 * KIB)
         v2_w.append(gather("v2_w1", U32, tab2_w[1][:], idx2[:], M, "w1_raw11", 2 * KIB))
         first_product(1)
 
-        w2_s = held("w2_s", [P, 2 * H], U8, "w1_g010")
+        w2_s = held("w2_s", [P, 2 * H], U8, "w1_g110")
         nc.gpsimd.tensor_copy(
             out=w2_s[:].bitcast(I32).rearrange("p (ab t g w) -> p ab t g w", t=PACK, g=16, w=2),
             in_=w2_s_raw[:].bitcast(I32).rearrange("p (ab g t w) -> p ab t g w", t=PACK, g=16, w=2),
@@ -291,7 +290,7 @@ def tile_list_wavelet_tree_contexts_kernel(
             )
 
         def round_w3(b):
-            grouped = held(f"w3_g{b}", [P, N * PACK], BF16)
+            grouped = held(f"w3_g{b}", [P, N * PACK], BF16, ("w2_w_raw", "w3_raw0")[b])
             for n0 in range(0, N, P):
                 round_on_gpsimd(
                     grouped[:, n0 * PACK : (n0 + P) * PACK].rearrange("p (n t) -> p n t", t=PACK),
@@ -300,7 +299,7 @@ def tile_list_wavelet_tree_contexts_kernel(
             return grouped
 
         w3_g = [round_w3(b) for b in range(2)]
-        picked.append([pick(held("picked10", [P, M], F32)[:], 1, 0)])
+        picked.append([pick(held("picked10", [P, M], F32, "tab2_w1")[:], 1, 0)])
         for t in range(PACK):
             second_product(0, t)
         half = M // 2

@@ -236,11 +236,11 @@ def tile_list_wavelet_tree_contexts_kernel(
         w3_raw = [load_w3(0, "tab_s"), load_w3(1, "w1_g000")]
         first_product(0)
         third = round_w1(0, 1, 0, ("gpsimd",) * PACK)
-        picked = [[pick(held(f"picked0{t}", [P, M], F32)[:], 0, t) for t in range(3)]]
+        picked = [[pick(held(f"picked0{t}", [P, M], F32)[:], 0, t) for t in range(2)]]
         quantise_w1(0, 1, 0, third[:])
-        picked[0].append(pick(held("picked03", [P, M], F32, "w1_raw01")[:], 0, 3))
-        v2_w = [gather("v2_w0", U32, tab2_w[0][:], idx2[:], M, "w1_raw01", 4 * KIB)]
+        picked[0].extend(pick(held(f"picked0{t}", [P, M], F32, "w1_raw01", 2 * (t - 2) * KIB)[:], 0, t) for t in (2, 3))
         quantise_w1(1, 1, 0, round_w1(1, 1, 0, ("scalar",) * PACK)[:], "w1_raw01", 6 * KIB)
+        v2_w = [gather("v2_w0", U32, tab2_w[0][:], idx2[:], M, "w1_raw11")]
         v2_w.append(gather("v2_w1", U32, tab2_w[1][:], idx2[:], M, "w1_raw11", 2 * KIB))
         first_product(1)
 
@@ -291,11 +291,9 @@ def tile_list_wavelet_tree_contexts_kernel(
 
         def round_w3(b):
             grouped = held(f"w3_g{b}", [P, N * PACK], BF16, ("w2_w_raw", "w3_raw0")[b])
-            for n0 in range(0, N, P):
-                round_on_gpsimd(
-                    grouped[:, n0 * PACK : (n0 + P) * PACK].rearrange("p (n t) -> p n t", t=PACK),
-                    w3_raw[b][:].rearrange("p (t n) -> p n t", t=PACK)[:, n0 : n0 + P, :],
-                )
+            round_on_gpsimd(
+                grouped[:].rearrange("p (n t) -> p n t", t=PACK), w3_raw[b][:].rearrange("p (t n) -> p n t", t=PACK)
+            )
             return grouped
 
         w3_g = [round_w3(b) for b in range(2)]

@@ -42,8 +42,8 @@ def tile_list_wavelet_tree_contexts_kernel(
 
         def held(name, shape, dtype, after=None, at=0, room=0):
             if after is None:
-                places[name] = places["end"]
-                places["end"] = places["end"] + max(room, 64, math.prod(shape[1:]) * SIZES[dtype])
+                places[name] = places["end"] + at
+                places["end"] = places[name] + max(room, 64, math.prod(shape[1:]) * SIZES[dtype])
             else:
                 places[name] = places[after] + at
             return keep.tile(shape, dtype, name=name, offset=places[name], align_bytes=64)
@@ -65,16 +65,16 @@ def tile_list_wavelet_tree_contexts_kernel(
         def load_words(dst, src, a):
             nc.sync.dma_start(out=dst.bitcast(I32), in_=src[a].rearrange("p c i -> p (c i)").bitcast(I32))
 
-        def load_w1(a, b, after=None, room=0):
-            raw = held(f"w1_raw{a}{b}", [P, PACK, PASS], F32, after, room=room)
+        def load_w1(a, b, after=None, at=0):
+            raw = held(f"w1_raw{a}{b}", [P, PACK, PASS], F32, after, at)
             nc.sync.dma_start(
                 out=raw[:],
                 in_=w1[a * PASS : (a + 1) * PASS, b * PASS : (b + 1) * PASS].rearrange("(p j) c -> p j c", j=PACK),
             )
             return raw
 
-        def to_plane(queue, name, rows, first, width):
-            plane = held(name, [P, 2 * width], U8)
+        def to_plane(queue, name, rows, first, width, after=None, at=0):
+            plane = held(name, [P, 2 * width], U8, after, at)
             nc.vector.memset(plane[:].bitcast(I32), 0)
             for q in range(4):
                 queue.dma_start(
@@ -97,8 +97,8 @@ def tile_list_wavelet_tree_contexts_kernel(
         def round_on_gpsimd(dst, src):
             nc.gpsimd.tensor_scalar(out=dst, in0=src, scalar1=1.0, scalar2=0.0, op0=MULT, op1=ADD)
 
-        def round_w1(a, b, t0, engines, room=0):
-            grouped = held(f"w1_g{a}{b}{t0}", [P, len(engines) * PASS], BF16, room=room)
+        def round_w1(a, b, t0, engines, room=0, after=None, at=0):
+            grouped = held(f"w1_g{a}{b}{t0}", [P, len(engines) * PASS], BF16, after, at, room)
             raw = w1_raw[a, b]
             for u, engine in enumerate(engines):
                 dst = grouped[:, u * PASS : (u + 1) * PASS]
@@ -131,46 +131,43 @@ def tile_list_wavelet_tree_contexts_kernel(
 
         nc.sync.dma_start(idx[:], offs)
         tab_s = load_scale_rows("tab_s", tab_scales, T, 0, 16 * KIB)
+        w1_raw = {(0, 0): load_w1(0, 0)}
         nc.sync.dma_start(idx2[:], offs2)
         tab2_s = load_scale_rows("tab2_s", tab2_scales, T2, 64)
-        w1_raw = {(0, 0): load_w1(0, 0, room=10 * KIB)}
-        tab_w0 = held("tab_w0", [P, T], U32)
-        load_words(tab_w0[:], tab_words, 0)
+        gain_rows = held("gain_rows", [P, P], F32, room=10 * KIB)
+        nc.gpsimd.memset(gain_rows[:], 0.0)
+        for b in range(2):
+            nc.sync.dma_start(
+                out=gain_rows[b * PACK : (b + 1) * PACK, :].rearrange("t (g i) -> t g i", i=8),
+                in_=gain[b * PASS : (b + 1) * PASS].rearrange("(g t i) -> t g i", t=PACK, i=8),
+            )
+        w1_raw[1, 0] = load_w1(1, 0)
+        tab_w = [held("tab_w0", [P, T], U32)]
+        load_words(tab_w[0][:], tab_words, 0)
         nc.sync.dma_start(parent[:], pos1)
         for rows, spans in ((tab_s, ((32, 64), (64, P))), (tab2_s, ((0, 64), (96, P)))):
             for lo, hi in spans:
                 nc.vector.memset(rows[lo:hi, :].bitcast(I32), 0)
-
-        gain_rows = held("gain_rows", [P, P], F32, room=8 * KIB)
-        nc.gpsimd.memset(gain_rows[:], 0.0)
-        for b in range(2):
-            nc.gpsimd.dma_start(
-                out=gain_rows[b * PACK : (b + 1) * PACK, :].rearrange("t (g i) -> t g i", i=8),
-                in_=gain[b * PASS : (b + 1) * PASS].rearrange("(g t i) -> t g i", t=PACK, i=8),
-            )
         identity = held("identity", [P, P], F32, room=8 * KIB)
         make_identity(nc, identity[:])
 
         picked_s = gather("picked_s", U8, tab_s[:], idx[:], S, room=2 * KIB)
         v_s = to_plane(nc.sync, "v_s", picked_s, 0, S)
-        tab_w1 = held("tab_w1", [P, T], U32, "tab_s")
-        load_words(tab_w1[:], tab_words, 1)
-
+        tab_w.append(held("tab_w1", [P, T], U32, "tab_s"))
+        load_words(tab_w[1][:], tab_words, 1)
         picked2_s = gather("picked2_s", U8, tab2_s[:], idx2[:], M)
-        v2_s = to_plane(nc.gpsimd, "v2_s", picked2_s, 64, M)
 
         turned = bank("turned", 7)
         nc.tensor.transpose(turned[:, 0:P], gain_rows[:], identity[:])
         gains = held("gains", [P, 2 * PACK], F32)
         nc.scalar.copy(out=gains[:], in_=turned[:, 0 : 2 * PACK])
-        inv_gains = held("inv_gains", [P, 2 * PACK], F32)
-        nc.vector.reciprocal(out=inv_gains[:], in_=gains[:])
+        gains_squared = held("gains_squared", [P, 2 * PACK], F32)
+        nc.scalar.activation(out=gains_squared[:], in_=turned[:, 0 : 2 * PACK], func=ACT.Square)
+        no_bias = held("no_bias", [P, 1], F32)
+        nc.gpsimd.memset(no_bias[:], 0.0)
 
-        for t0 in (0, 2):
-            quantise_w1(0, 0, t0, round_w1(0, 0, t0, ("scalar", "scalar"), 8 * KIB)[:])
-        w1_raw[1, 0] = load_w1(1, 0, "w1_g000")
-        w1_raw[0, 1] = load_w1(0, 1, "w1_raw00")
-        w1_raw[1, 1] = load_w1(1, 1, "w1_g002")
+        w1_raw[0, 1] = load_w1(0, 1, "gain_rows")
+        w1_raw[1, 1] = load_w1(1, 1, "identity")
         w2_s_raw = held("w2_s_raw", [P, 2 * H], U8, "picked_s")
         nc.gpsimd.memset(w2_s_raw[:].bitcast(I32), 0)
         for q in range(4):
@@ -178,25 +175,29 @@ def tile_list_wavelet_tree_contexts_kernel(
                 out=w2_s_raw[32 * q : 32 * q + 4, :].bitcast(I32).rearrange("r (a c) -> r a c", a=2),
                 in_=w2_scales.bitcast(I32)[:, 4 * q : 4 * q + 4, :].rearrange("a r c -> r a c"),
             )
-        tab2_w = [held(f"tab2_w{a}", [P, T2], U32, after) for a, after in enumerate(("gain_rows", "identity"))]
+        for a in range(2):
+            quantise_w1(a, 0, 0, round_w1(a, 0, 0, ("scalar",) * PACK, 9 * KIB)[:])
+        tab2_w = [held(f"tab2_w{a}", [P, T2], U32, after, at) for a, (after, at) in enumerate((("w1_raw10", 0), ("w1_g100", KIB)))]
         for a in range(2):
             load_words(tab2_w[a][:], tab2_words, a)
+        v2_s = to_plane(nc.sync, "v2_s", picked2_s, 64, M, "w1_g100")
 
         v_w = {}
         for half in range(2):
-            v_w[0, half] = gather(f"v_w0{half}", U32, tab_w0[:], idx[:, 32 * half : 32 * (half + 1)], BANK)
+            v_w[0, half] = gather(f"v_w0{half}", U32, tab_w[0][:], idx[:, 32 * half : 32 * (half + 1)], BANK)
         w2_w_raw = held("w2_w_raw", [P, 2, H // 2], I32, "tab_w0")
         nc.sync.dma_start(out=w2_w_raw[:], in_=w2_words.bitcast(I32).rearrange("a p c -> p a c"))
-
         for half in range(2):
-            v_w[1, half] = gather(f"v_w1{half}", U32, tab_w1[:], idx[:, 32 * half : 32 * (half + 1)], BANK)
+            v_w[1, half] = gather(f"v_w1{half}", U32, tab_w[1][:], idx[:, 32 * half : 32 * (half + 1)], BANK)
 
-        def load_w3(b, after):
-            raw = held(f"w3_raw{b}", [P, PACK * N], F32, after)
+        def load_w3(b):
+            raw = held(f"w3_raw{b}", [P, PACK * N], F32, "tab_w1", 8 * b * KIB)
             rows = w3[b * PASS : (b + 1) * PASS, :].rearrange("(g t i) n -> t g i n", t=PACK, i=8)
             for t in range(PACK):
                 nc.sync.dma_start(out=raw[:, t * N : (t + 1) * N], in_=rows[t])
             return raw
+
+        w3_raw = [load_w3(b) for b in range(2)]
 
         damping = {}
 
@@ -212,39 +213,50 @@ def tile_list_wavelet_tree_contexts_kernel(
                 stop=(a == 1),
             )
 
-        def first_product(b):
+        def empty(acc, b, t, half):
+            nc.scalar.activation(
+                out=damping[b, t][:, half * BANK : (half + 1) * BANK], in_=acc[:], func=ACT.Exp, scale=-0.5, bias=no_bias[:]
+            )
+
+        def open_banks(b):
+            accs = {}
             for t in range(PACK):
-                accs = [bank(f"h{b}{t}{half}", 2 * t + half) for half in range(2)]
-                for half in range(2):
-                    first_pass(accs[half], 0, b, t, half)
                 damping[b, t] = held(f"damping{b}{t}", [P, S], F32, f"damping0{t}" if b else None)
                 for half in range(2):
-                    first_pass(accs[half], 1, b, t, half)
-                    nc.scalar.activation(
-                        out=damping[b, t][:, half * BANK : (half + 1) * BANK],
-                        in_=accs[half][:],
-                        func=ACT.Exp,
-                        scale=-0.5,
-                    )
+                    accs[t, half] = bank(f"h{b}{t}{half}", 2 * t + half)
+                    first_pass(accs[t, half], 0, b, t, half)
+            return accs
 
         def pick(dst, b, t):
             nc.vector.tensor_copy(out=dst, in_=damping[b, t][:].indirect(parent[:]))
             return dst
 
-        for t0, engines in ((0, ("vector",)), (1, ("scalar",)), (2, ("vector", "scalar"))):
-            quantise_w1(1, 0, t0, round_w1(1, 0, t0, engines)[:])
-        w3_raw = [load_w3(0, "tab_s"), load_w3(1, "w1_g000")]
-        first_product(0)
-        third = round_w1(0, 1, 0, ("gpsimd",) * PACK)
-        picked = [[pick(held(f"picked0{t}", [P, M], F32)[:], 0, t) for t in range(2)]]
-        quantise_w1(0, 1, 0, third[:])
-        picked[0].extend(pick(held(f"picked0{t}", [P, M], F32, "w1_raw01", 2 * (t - 2) * KIB)[:], 0, t) for t in (2, 3))
-        quantise_w1(1, 1, 0, round_w1(1, 1, 0, ("scalar",) * PACK)[:], "w1_raw01", 6 * KIB)
+        accs = open_banks(0)
+        for t, half in ((0, 0), (1, 0), (0, 1), (1, 1), (2, 0), (2, 1), (3, 0), (3, 1)):
+            first_pass(accs[t, half], 1, 0, t, half)
+            empty(accs[t, half], 0, t, half)
+
+        for t0 in range(2):
+            quantise_w1(0, 1, t0, round_w1(0, 1, t0, ("vector",), 3 * KIB, at=2 * KIB)[:])
+        third = round_w1(0, 1, 2, ("gpsimd",) * 2, after="w1_g011", at=KIB // 2)
+        picked = [[pick(held(f"picked0{t}", [P, M], F32, f"w1_g01{t}", -3 * KIB // 2)[:], 0, t) for t in range(2)]]
+        picked[0].append(pick(held("picked02", [P, M], F32, "w1_raw00")[:], 0, 2))
+        quantise_w1(1, 1, 0, round_w1(1, 1, 0, ("gpsimd",) * 2)[:])
+        quantise_w1(0, 1, 2, third[:], "w1_raw11", 4 * KIB)
+        quantise_w1(1, 1, 2, round_w1(1, 1, 2, ("scalar",) * 2)[:], "w1_g110")
+        picked[0].append(pick(held("picked03", [P, M], F32, "w1_raw11", 6 * KIB)[:], 0, 3))
         v2_w = [gather("v2_w0", U32, tab2_w[0][:], idx2[:], M, "w1_raw11")]
         v2_w.append(gather("v2_w1", U32, tab2_w[1][:], idx2[:], M, "w1_raw11", 2 * KIB))
-        first_product(1)
+        accs = open_banks(1)
+        for t in range(PACK):
+            for half in range(2):
+                first_pass(accs[t, half], 1, 1, t, half)
+                empty(accs[t, half], 1, t, half)
 
-        w2_s = held("w2_s", [P, 2 * H], U8, "w1_g110")
+        inv_gains = held("inv_gains", [P, 2 * PACK], F32, "no_bias")
+        nc.scalar.activation(out=inv_gains[:], in_=gains_squared[:], func=ACT.Abs_reciprocal_sqrt)
+
+        w2_s = held("w2_s", [P, 2 * H], U8, "w1_g112")
         nc.gpsimd.tensor_copy(
             out=w2_s[:].bitcast(I32).rearrange("p (ab t g w) -> p ab t g w", t=PACK, g=16, w=2),
             in_=w2_s_raw[:].bitcast(I32).rearrange("p (ab g t w) -> p ab t g w", t=PACK, g=16, w=2),
@@ -257,7 +269,7 @@ def tile_list_wavelet_tree_contexts_kernel(
                 in_=w2_w_raw[:].rearrange("p a (b g t w) -> p b a t g w", t=PACK, g=16, w=4)[:, b],
             )
 
-        ratio = [held("ratio0", [P, PACK, M], F32, "tab_w0", 4 * KIB), held("ratio1", [P, PACK, M], F32)]
+        ratio = [held("ratio0", [P, PACK, M], F32, "tab_w0", 8 * KIB), held("ratio1", [P, PACK, M], F32)]
         square = [held(f"square{b}", [P, PACK, M], F32) for b in range(2)]
 
         def second_product(b, t):
@@ -282,27 +294,24 @@ def tile_list_wavelet_tree_contexts_kernel(
             )
 
         def inverse_root(b, lo, hi, after=None, at=0):
-            one = held(f"one{b}{lo}", [P, 1], F32, room=KIB)
+            one = held(f"one{b}{lo}", [P, 1], F32, room=2 * KIB)
             nc.gpsimd.memset(one[:], 1.0)
             norm[b, lo] = held(f"norm{b}{lo}", [P, PACK, hi - lo], F32, after, at)
             nc.scalar.activation(
                 out=norm[b, lo][:], in_=square[b][:, :, lo:hi], func=ACT.Abs_reciprocal_sqrt, bias=one[:]
             )
 
-        def round_w3(b):
-            grouped = held(f"w3_g{b}", [P, N * PACK], BF16, ("w2_w_raw", "w3_raw0")[b])
+        w3_g = held("w3_g", [P, 2, N * PACK], BF16, "w2_w_raw")
+        for b in range(2):
             round_on_gpsimd(
-                grouped[:].rearrange("p (n t) -> p n t", t=PACK), w3_raw[b][:].rearrange("p (t n) -> p n t", t=PACK)
+                w3_g[:, b].rearrange("p (n t) -> p n t", t=PACK), w3_raw[b][:].rearrange("p (t n) -> p n t", t=PACK)
             )
-            return grouped
-
-        w3_g = [round_w3(b) for b in range(2)]
         picked.append([pick(held("picked10", [P, M], F32, "tab2_w1")[:], 1, 0)])
         for t in range(PACK):
             second_product(0, t)
         half = M // 2
         norm = {}
-        inverse_root(0, 0, half, "w1_110_c")
+        inverse_root(0, 0, half)
         second_product(1, 0)
         for t, after in ((1, "picked02"), (2, "picked03"), (3, "picked10")):
             picked[1].append(pick(held(f"picked1{t}", [P, M], F32, after)[:], 1, t))
@@ -312,10 +321,9 @@ def tile_list_wavelet_tree_contexts_kernel(
         for place, (lo, hi) in enumerate(PIECES[1:]):
             inverse_root(0, lo, hi, "square1", 2 * place * KIB)
 
-        def children(b, lo, hi, after=None):
-            values = held(f"z{b}{lo}_values", [P, (hi - lo) * PACK], BF16, after)
+        def children(values, b, lo, hi):
             nc.vector.tensor_tensor(
-                out=values[:].rearrange("p (c i t) -> p c t i", i=4, t=PACK),
+                out=values.rearrange("p (c i t) -> p c t i", i=4, t=PACK),
                 in0=ratio[b][:, :, lo:hi].rearrange("p t (c i) -> p c t i", i=4),
                 in1=norm[b, lo][:].rearrange("p t (c i) -> p c t i", i=4),
                 op=MULT,
@@ -333,8 +341,8 @@ def tile_list_wavelet_tree_contexts_kernel(
                         j = 2 * pair + place
                         nc.tensor.matmul_mx(
                             out=accs[pair][:, place * (hi - lo) : (place + 1) * (hi - lo)],
-                            lhsT=w3_q[b][0][:, j * P : (j + 1) * P].bitcast(FP8X4),
-                            lhsT_scale=w3_q[b][1][:, j * P : (j + 1) * P],
+                            lhsT=w3_c[:, b * N + j * P : b * N + (j + 1) * P].bitcast(FP8X4),
+                            lhsT_scale=w3_s[:, b * N + j * P : b * N + (j + 1) * P],
                             rhs=z[0][:, lo - first : hi - first].bitcast(FP8X4),
                             rhs_scale=z[1][:, lo - first : hi - first],
                             start=(step == 0 and place == 0),
@@ -347,17 +355,20 @@ def tile_list_wavelet_tree_contexts_kernel(
                     out=out_rows[:, 2 * pair : 2 * pair + 2, lo:hi], in_=staged[:].rearrange("p (j m) -> p j m", j=2)
                 )
 
-        values = children(0, 0, half, "picked02")
-        w3_q = [quantise(f"w3_{b}", w3_g[b][:], "w3_raw1", 2 * b * KIB) for b in range(2)]
-        z0 = quantise("z00", values[:], "w3_g0")
-        other = children(1, 0, half)
-        rest = children(1, half, M)
-        z1 = quantise("z10", other[:], f"one1{half}")
+        def values(name, width, after=None):
+            return held(name, [P, width * PACK], BF16, after)[:]
+
+        early = children(values("z_early0", half, "picked02"), 0, 0, half)
+        w3_c, w3_s = quantise("w3", w3_g[:].rearrange("p b c -> p (b c)"), "w3_raw1")
+        z0 = quantise("z_early0", early, "w3_g")
+        early = children(values("z_early1", half), 1, 0, half)
+        rest = children(values("z_rest", half), 1, half, M)
+        z1 = quantise("z_early1", early, f"one1{half}")
         last_product(0, ((0, z0, 0), (1, z1, 0)))
-        values = [children(0, *PIECES[1])]
-        z1 = quantise("z1h", rest[:], f"one0{half}")
-        values.append(children(0, *PIECES[2]))
+        late = [children(values("z_late1", P), 0, *PIECES[1])]
+        z1 = quantise("z_rest", rest, f"one0{half}")
+        late.append(children(values("z_late2", P), 0, *PIECES[2]))
         for piece, after in ((1, f"one0{PIECES[2][0]}"), (2, None)):
             lo, hi = PIECES[piece]
-            z0 = quantise(f"z0{lo}", values[piece - 1][:], after)
+            z0 = quantise(f"z_late{piece}", late[piece - 1], after)
             last_product(piece, ((1, z1, half), (0, z0, lo)))

@@ -55,8 +55,8 @@ def tile_list_wavelet_tree_contexts_kernel(
         idx2 = lists.tile([P, M // 16], U16, name="idx2")
         parent = lists.tile([P, M // 16], U16, name="parent")
 
-        def load_scale_rows(name, src, width, first, room=0):
-            rows = held(name, [P, width], U8, room=room)
+        def load_scale_rows(name, src, width, first, room, at=0):
+            rows = held(name, [P, width], U8, at=at, room=room)
             nc.sync.dma_start(
                 out=rows[first : first + 32, :].bitcast(I32), in_=src.bitcast(I32).rearrange("a q c -> q a c")
             )
@@ -133,14 +133,7 @@ def tile_list_wavelet_tree_contexts_kernel(
         tab_s = load_scale_rows("tab_s", tab_scales, T, 0, 16 * KIB)
         w1_raw = {(0, 0): load_w1(0, 0)}
         nc.sync.dma_start(idx2[:], offs2)
-        tab2_s = load_scale_rows("tab2_s", tab2_scales, T2, 64)
-        gain_rows = held("gain_rows", [P, P], F32, room=10 * KIB)
-        nc.gpsimd.memset(gain_rows[:], 0.0)
-        for b in range(2):
-            nc.sync.dma_start(
-                out=gain_rows[b * PACK : (b + 1) * PACK, :].rearrange("t (g i) -> t g i", i=8),
-                in_=gain[b * PASS : (b + 1) * PASS].rearrange("(g t i) -> t g i", t=PACK, i=8),
-            )
+        tab2_s = load_scale_rows("tab2_s", tab2_scales, T2, 64, 11 * KIB, 7 * KIB)
         w1_raw[1, 0] = load_w1(1, 0)
         tab_w = [held("tab_w0", [P, T], U32)]
         load_words(tab_w[0][:], tab_words, 0)
@@ -148,7 +141,7 @@ def tile_list_wavelet_tree_contexts_kernel(
         for rows, spans in ((tab_s, ((32, 64), (64, P))), (tab2_s, ((0, 64), (96, P)))):
             for lo, hi in spans:
                 nc.vector.memset(rows[lo:hi, :].bitcast(I32), 0)
-        identity = held("identity", [P, P], F32, room=8 * KIB)
+        identity = held("identity", [P, P], F32)
         make_identity(nc, identity[:])
 
         picked_s = gather("picked_s", U8, tab_s[:], idx[:], S, room=2 * KIB)
@@ -157,17 +150,11 @@ def tile_list_wavelet_tree_contexts_kernel(
         load_words(tab_w[1][:], tab_words, 1)
         picked2_s = gather("picked2_s", U8, tab2_s[:], idx2[:], M)
 
-        turned = bank("turned", 7)
-        nc.tensor.transpose(turned[:, 0:P], gain_rows[:], identity[:])
-        gains = held("gains", [P, 2 * PACK], F32)
-        nc.scalar.copy(out=gains[:], in_=turned[:, 0 : 2 * PACK])
-        gains_squared = held("gains_squared", [P, 2 * PACK], F32)
-        nc.scalar.activation(out=gains_squared[:], in_=turned[:, 0 : 2 * PACK], func=ACT.Square)
         no_bias = held("no_bias", [P, 1], F32)
         nc.gpsimd.memset(no_bias[:], 0.0)
 
-        w1_raw[0, 1] = load_w1(0, 1, "gain_rows")
-        w1_raw[1, 1] = load_w1(1, 1, "identity")
+        w1_raw[0, 1] = load_w1(0, 1, "tab2_s", -7 * KIB)
+        w1_raw[1, 1] = load_w1(1, 1, "tab2_s", KIB)
         w2_s_raw = held("w2_s_raw", [P, 2 * H], U8, "picked_s")
         nc.gpsimd.memset(w2_s_raw[:].bitcast(I32), 0)
         for q in range(4):
@@ -177,6 +164,13 @@ def tile_list_wavelet_tree_contexts_kernel(
             )
         for a in range(2):
             quantise_w1(a, 0, 0, round_w1(a, 0, 0, ("scalar",) * PACK, 9 * KIB)[:])
+        gain_rows = held("gain_rows", [P, P], F32, "w1_raw00", 4 * KIB)
+        nc.gpsimd.memset(gain_rows[:], 0.0)
+        for b in range(2):
+            nc.sync.dma_start(
+                out=gain_rows[b * PACK : (b + 1) * PACK, :].rearrange("t (g i) -> t g i", i=8),
+                in_=gain[b * PASS : (b + 1) * PASS].rearrange("(g t i) -> t g i", t=PACK, i=8),
+            )
         tab2_w = [held(f"tab2_w{a}", [P, T2], U32, after, at) for a, (after, at) in enumerate((("w1_raw10", 0), ("w1_g100", KIB)))]
         for a in range(2):
             load_words(tab2_w[a][:], tab2_words, a)
@@ -190,14 +184,14 @@ def tile_list_wavelet_tree_contexts_kernel(
         for half in range(2):
             v_w[1, half] = gather(f"v_w1{half}", U32, tab_w[1][:], idx[:, 32 * half : 32 * (half + 1)], BANK)
 
-        def load_w3(b):
-            raw = held(f"w3_raw{b}", [P, PACK * N], F32, "tab_w1", 8 * b * KIB)
-            rows = w3[b * PASS : (b + 1) * PASS, :].rearrange("(g t i) n -> t g i n", t=PACK, i=8)
+        def load_w3(b, lo, hi):
+            raw = held(f"w3_raw{b}{lo}", [P, PACK * (hi - lo)], F32, "tab_w1", 4 * PACK * (b * N + lo))
+            rows = w3[b * PASS : (b + 1) * PASS, lo:hi].rearrange("(g t i) n -> t g i n", t=PACK, i=8)
             for t in range(PACK):
-                nc.sync.dma_start(out=raw[:, t * N : (t + 1) * N], in_=rows[t])
+                nc.sync.dma_start(out=raw[:, t * (hi - lo) : (t + 1) * (hi - lo)], in_=rows[t])
             return raw
 
-        w3_raw = [load_w3(b) for b in range(2)]
+        w3_raw = {part: load_w3(*part) for part in ((0, 0, N), (1, 0, N // 2), (1, N // 2, N))}
 
         damping = {}
 
@@ -252,6 +246,13 @@ def tile_list_wavelet_tree_contexts_kernel(
             for half in range(2):
                 first_pass(accs[t, half], 1, 1, t, half)
                 empty(accs[t, half], 1, t, half)
+            if t == 0:
+                turned = bank("turned", 0)
+                nc.tensor.transpose(turned[:, 0:P], gain_rows[:], identity[:])
+                gains = held("gains", [P, 2 * PACK], F32)
+                nc.scalar.copy(out=gains[:], in_=turned[:, 0 : 2 * PACK])
+                gains_squared = held("gains_squared", [P, 2 * PACK], F32)
+                nc.scalar.activation(out=gains_squared[:], in_=turned[:, 0 : 2 * PACK], func=ACT.Square)
 
         inv_gains = held("inv_gains", [P, 2 * PACK], F32, "no_bias")
         nc.scalar.activation(out=inv_gains[:], in_=gains_squared[:], func=ACT.Abs_reciprocal_sqrt)
@@ -302,9 +303,10 @@ def tile_list_wavelet_tree_contexts_kernel(
             )
 
         w3_g = held("w3_g", [P, 2, N * PACK], BF16, "w2_w_raw")
-        for b in range(2):
+        for (b, lo, hi), raw in w3_raw.items():
             round_on_gpsimd(
-                w3_g[:, b].rearrange("p (n t) -> p n t", t=PACK), w3_raw[b][:].rearrange("p (t n) -> p n t", t=PACK)
+                w3_g[:, b, lo * PACK : hi * PACK].rearrange("p (n t) -> p n t", t=PACK),
+                raw[:].rearrange("p (t n) -> p n t", t=PACK),
             )
         picked.append([pick(held("picked10", [P, M], F32, "tab2_w1")[:], 1, 0)])
         for t in range(PACK):
@@ -359,7 +361,7 @@ def tile_list_wavelet_tree_contexts_kernel(
             return held(name, [P, width * PACK], BF16, after)[:]
 
         early = children(values("z_early0", half, "picked02"), 0, 0, half)
-        w3_c, w3_s = quantise("w3", w3_g[:].rearrange("p b c -> p (b c)"), "w3_raw1")
+        w3_c, w3_s = quantise("w3", w3_g[:].rearrange("p b c -> p (b c)"), f"w3_raw1{N // 2}")
         z0 = quantise("z_early0", early, "w3_g")
         early = children(values("z_early1", half), 1, 0, half)
         rest = children(values("z_rest", half), 1, half, M)

@@ -73,11 +73,11 @@ def tile_list_wavelet_tree_contexts_kernel(
             )
             return raw
 
-        def to_plane(queue, name, rows, first, width, after=None, at=0):
+        def to_plane(engine, name, rows, first, width, after=None, at=0):
             plane = held(name, [P, 2 * width], U8, after, at)
-            nc.vector.memset(plane[:].bitcast(I32), 0)
+            engine.memset(plane[:].bitcast(I32), 0)
             for q in range(4):
-                queue.dma_start(
+                nc.sync.dma_start(
                     out=plane[32 * q : 32 * q + 4, :].bitcast(I32),
                     in_=rows[first + 8 * q : first + 8 * q + 8, :].bitcast(I32),
                 )
@@ -94,24 +94,25 @@ def tile_list_wavelet_tree_contexts_kernel(
             else:
                 nc.scalar.copy(out=dst, in_=src)
 
-        def round_on_gpsimd(dst, src):
-            nc.gpsimd.tensor_scalar(out=dst, in0=src, scalar1=1.0, scalar2=0.0, op0=MULT, op1=ADD)
+        def round_on_gpsimd(dst, src, unit=1.0):
+            nc.gpsimd.tensor_scalar(out=dst, in0=src, scalar1=unit, scalar2=0.0, op0=MULT, op1=ADD)
 
-        def round_w1(a, b, t0, engines, room=0, after=None, at=0):
-            grouped = held(f"w1_g{a}{b}{t0}", [P, len(engines) * PASS], BF16, after, at, room)
-            raw = w1_raw[a, b]
-            for u, engine in enumerate(engines):
+        def round_w1(name, engine, parts, room=0, after=None, at=0, last_unit=1.0):
+            grouped = held(name, [P, len(parts) * PASS], BF16, after, at, room)
+            for u, (a, b, t) in enumerate(parts):
                 dst = grouped[:, u * PASS : (u + 1) * PASS]
+                raw = w1_raw[a, b]
                 if engine == "gpsimd":
                     round_on_gpsimd(
                         dst.rearrange("p (g i j) -> p g i j", g=16, j=PACK),
-                        raw[:].rearrange("p j (g t i) -> p t g i j", t=PACK, i=8)[:, t0 + u],
+                        raw[:].rearrange("p j (g t i) -> p t g i j", t=PACK, i=8)[:, t],
+                        last_unit if u == len(parts) - 1 else 1.0,
                     )
                 else:
                     round_on(
                         engine,
                         dst.rearrange("p (g h i j) -> p g h j i", g=16, h=2, i=4),
-                        raw[:].rearrange("p j (g t h i) -> p t g h j i", t=PACK, h=2, i=4)[:, t0 + u],
+                        raw[:].rearrange("p j (g t h i) -> p t g h j i", t=PACK, h=2, i=4)[:, t],
                     )
             return grouped
 
@@ -124,10 +125,10 @@ def tile_list_wavelet_tree_contexts_kernel(
 
         w1_q = {}
 
-        def quantise_w1(a, b, t0, values, after=None, at=0, room=0):
-            codes, scales = quantise(f"w1_{a}{b}{t0}", values, after, at, room)
-            for u in range(values.shape[1] // PASS):
-                w1_q[a, b, t0 + u] = codes[:, u * P : (u + 1) * P], scales[:, u * P : (u + 1) * P]
+        def quantise_w1(name, parts, values, after=None, at=0, room=0):
+            codes, scales = quantise(name, values, after, at, room)
+            for u, part in enumerate(parts):
+                w1_q[part] = codes[:, u * P : (u + 1) * P], scales[:, u * P : (u + 1) * P]
 
         nc.sync.dma_start(idx[:], offs)
         tab_s = load_scale_rows("tab_s", tab_scales, T, 0, 16 * KIB)
@@ -138,6 +139,9 @@ def tile_list_wavelet_tree_contexts_kernel(
         tab_w = [held("tab_w0", [P, T], U32)]
         load_words(tab_w[0][:], tab_words, 0)
         nc.sync.dma_start(parent[:], pos1)
+        gain_rows = held("gain_rows", [P, PASS], F32)
+        nc.gpsimd.memset(gain_rows[:], 0.0)
+        nc.sync.dma_start(out=gain_rows[0:2, :], in_=gain.rearrange("(b c) -> b c", b=2))
         for rows, spans in ((tab_s, ((32, 64), (64, P))), (tab2_s, ((0, 64), (96, P)))):
             for lo, hi in spans:
                 nc.vector.memset(rows[lo:hi, :].bitcast(I32), 0)
@@ -145,7 +149,7 @@ def tile_list_wavelet_tree_contexts_kernel(
         make_identity(nc, identity[:])
 
         picked_s = gather("picked_s", U8, tab_s[:], idx[:], S, room=2 * KIB)
-        v_s = to_plane(nc.sync, "v_s", picked_s, 0, S)
+        v_s = to_plane(nc.vector, "v_s", picked_s, 0, S)
         tab_w.append(held("tab_w1", [P, T], U32, "tab_s"))
         load_words(tab_w[1][:], tab_words, 1)
         picked2_s = gather("picked2_s", U8, tab2_s[:], idx2[:], M)
@@ -155,32 +159,40 @@ def tile_list_wavelet_tree_contexts_kernel(
 
         w1_raw[0, 1] = load_w1(0, 1, "tab2_s", -7 * KIB)
         w1_raw[1, 1] = load_w1(1, 1, "tab2_s", KIB)
-        w2_s_raw = held("w2_s_raw", [P, 2 * H], U8, "picked_s")
+        for a in range(2):
+            parts = [(a, 0, t) for t in range(PACK)]
+            quantise_w1(f"w1_{a}0", parts, round_w1(f"w1_g{a}0", "scalar", parts, 9 * KIB, at=KIB)[:])
+        tab2_w = [held(f"tab2_w{a}", [P, T2], U32, after, at) for a, (after, at) in enumerate((("w1_raw10", 0), ("w1_g10", KIB)))]
+        for a in range(2):
+            load_words(tab2_w[a][:], tab2_words, a)
+        w2_s_raw = held("w2_s_raw", [P, 2 * H], U8, "w1_g10", -KIB)
         nc.gpsimd.memset(w2_s_raw[:].bitcast(I32), 0)
         for q in range(4):
             nc.sync.dma_start(
                 out=w2_s_raw[32 * q : 32 * q + 4, :].bitcast(I32).rearrange("r (a c) -> r a c", a=2),
                 in_=w2_scales.bitcast(I32)[:, 4 * q : 4 * q + 4, :].rearrange("a r c -> r a c"),
             )
-        for a in range(2):
-            quantise_w1(a, 0, 0, round_w1(a, 0, 0, ("scalar",) * PACK, 9 * KIB)[:])
-        gain_rows = held("gain_rows", [P, P], F32, "w1_raw00", 4 * KIB)
-        nc.gpsimd.memset(gain_rows[:], 0.0)
-        for b in range(2):
-            nc.sync.dma_start(
-                out=gain_rows[b * PACK : (b + 1) * PACK, :].rearrange("t (g i) -> t g i", i=8),
-                in_=gain[b * PASS : (b + 1) * PASS].rearrange("(g t i) -> t g i", t=PACK, i=8),
-            )
-        tab2_w = [held(f"tab2_w{a}", [P, T2], U32, after, at) for a, (after, at) in enumerate((("w1_raw10", 0), ("w1_g100", KIB)))]
-        for a in range(2):
-            load_words(tab2_w[a][:], tab2_words, a)
-        v2_s = to_plane(nc.sync, "v2_s", picked2_s, 64, M, "w1_g100")
+
+        gain_dealt = held("gain_dealt", [P, PASS], F32)
+        nc.scalar.copy(
+            out=gain_dealt[:].rearrange("p (t g i) -> p t g i", t=PACK, i=8),
+            in_=gain_rows[:].rearrange("p (g t i) -> p t g i", t=PACK, i=8),
+        )
+        turned = bank("turned", 7)
+        for u in range(PACK):
+            nc.tensor.transpose(turned[:, u * P : (u + 1) * P], gain_dealt[:, u * P : (u + 1) * P], identity[:])
+        turned_gains = turned[:].rearrange("p (t b) -> p b t", t=PACK)[:, 0:2, :]
+        gains = held("gains", [P, 2 * PACK], F32)
+        nc.scalar.copy(out=gains[:].rearrange("p (b t) -> p b t", b=2), in_=turned_gains)
+        gains_squared = held("gains_squared", [P, 2 * PACK], F32)
+        nc.scalar.activation(out=gains_squared[:].rearrange("p (b t) -> p b t", b=2), in_=turned_gains, func=ACT.Square)
 
         v_w = {}
         for half in range(2):
             v_w[0, half] = gather(f"v_w0{half}", U32, tab_w[0][:], idx[:, 32 * half : 32 * (half + 1)], BANK)
         w2_w_raw = held("w2_w_raw", [P, 2, H // 2], I32, "tab_w0")
         nc.sync.dma_start(out=w2_w_raw[:], in_=w2_words.bitcast(I32).rearrange("a p c -> p a c"))
+        v2_s = to_plane(nc.gpsimd, "v2_s", picked2_s, 64, M, "tab_w0", 8 * KIB)
         for half in range(2):
             v_w[1, half] = gather(f"v_w1{half}", U32, tab_w[1][:], idx[:, 32 * half : 32 * (half + 1)], BANK)
 
@@ -230,15 +242,17 @@ def tile_list_wavelet_tree_contexts_kernel(
             first_pass(accs[t, half], 1, 0, t, half)
             empty(accs[t, half], 0, t, half)
 
-        for t0 in range(2):
-            quantise_w1(0, 1, t0, round_w1(0, 1, t0, ("vector",), 3 * KIB, at=2 * KIB)[:])
-        third = round_w1(0, 1, 2, ("gpsimd",) * 2, after="w1_g011", at=KIB // 2)
+        for t in range(2):
+            quantise_w1(f"w1_01{t}", [(0, 1, t)], round_w1(f"w1_g01{t}", "vector", [(0, 1, t)], 4 * KIB, at=2 * KIB)[:])
+        unit = held("unit", [P, 1], F32, room=2 * KIB)
+        nc.gpsimd.memset(unit[:], 1.0)
+        by_gpsimd, by_scalar = [(0, 1, 2), (0, 1, 3), (1, 1, 0)], [(1, 1, 1), (1, 1, 2), (1, 1, 3)]
+        rounded = round_w1("w1_g_gpsimd", "gpsimd", by_gpsimd, after="w1_g011", at=KIB // 2, last_unit=unit[:])
         picked = [[pick(held(f"picked0{t}", [P, M], F32, f"w1_g01{t}", -3 * KIB // 2)[:], 0, t) for t in range(2)]]
         picked[0].append(pick(held("picked02", [P, M], F32, "w1_raw00")[:], 0, 2))
-        quantise_w1(1, 1, 0, round_w1(1, 1, 0, ("gpsimd",) * 2)[:])
-        quantise_w1(0, 1, 2, third[:], "w1_raw11", 4 * KIB)
-        quantise_w1(1, 1, 2, round_w1(1, 1, 2, ("scalar",) * 2)[:], "w1_g110")
-        picked[0].append(pick(held("picked03", [P, M], F32, "w1_raw11", 6 * KIB)[:], 0, 3))
+        quantise_w1("w1_gpsimd", by_gpsimd, rounded[:])
+        picked[0].append(pick(held("picked03", [P, M], F32, "unit")[:], 0, 3))
+        quantise_w1("w1_scalar", by_scalar, round_w1("w1_g_scalar", "scalar", by_scalar)[:])
         v2_w = [gather("v2_w0", U32, tab2_w[0][:], idx2[:], M, "w1_raw11")]
         v2_w.append(gather("v2_w1", U32, tab2_w[1][:], idx2[:], M, "w1_raw11", 2 * KIB))
         accs = open_banks(1)
@@ -246,31 +260,24 @@ def tile_list_wavelet_tree_contexts_kernel(
             for half in range(2):
                 first_pass(accs[t, half], 1, 1, t, half)
                 empty(accs[t, half], 1, t, half)
-            if t == 0:
-                turned = bank("turned", 0)
-                nc.tensor.transpose(turned[:, 0:P], gain_rows[:], identity[:])
-                gains = held("gains", [P, 2 * PACK], F32)
-                nc.scalar.copy(out=gains[:], in_=turned[:, 0 : 2 * PACK])
-                gains_squared = held("gains_squared", [P, 2 * PACK], F32)
-                nc.scalar.activation(out=gains_squared[:], in_=turned[:, 0 : 2 * PACK], func=ACT.Square)
 
         inv_gains = held("inv_gains", [P, 2 * PACK], F32, "no_bias")
         nc.scalar.activation(out=inv_gains[:], in_=gains_squared[:], func=ACT.Abs_reciprocal_sqrt)
 
-        w2_s = held("w2_s", [P, 2 * H], U8, "w1_g112")
+        w2_s = held("w2_s", [P, 2 * H], U8, "w1_g_scalar")
         nc.gpsimd.tensor_copy(
             out=w2_s[:].bitcast(I32).rearrange("p (ab t g w) -> p ab t g w", t=PACK, g=16, w=2),
             in_=w2_s_raw[:].bitcast(I32).rearrange("p (ab g t w) -> p ab t g w", t=PACK, g=16, w=2),
         )
         w2_w = []
-        for b, after in enumerate(("picked_s", None)):
+        for b, after in enumerate(("w2_s_raw", None)):
             w2_w.append(held(f"w2_w{b}", [P, 2 * H], U8, after))
             nc.gpsimd.tensor_copy(
                 out=w2_w[b][:].bitcast(I32).rearrange("p (a t g w) -> p a t g w", t=PACK, g=16, w=4),
                 in_=w2_w_raw[:].rearrange("p a (b g t w) -> p b a t g w", t=PACK, g=16, w=4)[:, b],
             )
 
-        ratio = [held("ratio0", [P, PACK, M], F32, "tab_w0", 8 * KIB), held("ratio1", [P, PACK, M], F32)]
+        ratio = [held("ratio0", [P, PACK, M], F32), held("ratio1", [P, PACK, M], F32)]
         square = [held(f"square{b}", [P, PACK, M], F32) for b in range(2)]
 
         def second_product(b, t):

@@ -154,7 +154,7 @@ def tile_list_wavelet_tree_contexts_kernel(
         load_words(tab_w[1][:], tab_words, 1)
         picked2_s = gather("picked2_s", U8, tab2_s[:], idx2[:], M)
 
-        no_bias = held("no_bias", [P, 1], F32)
+        no_bias = held("no_bias", [P, 1], F32, room=2 * KIB)
         nc.gpsimd.memset(no_bias[:], 0.0)
 
         w1_raw[0, 1] = load_w1(0, 1, "tab2_s", -7 * KIB)
@@ -326,15 +326,16 @@ def tile_list_wavelet_tree_contexts_kernel(
             picked[1].append(pick(held(f"picked1{t}", [P, M], F32, after)[:], 1, t))
             second_product(1, t)
         inverse_root(1, 0, half)
+        inverse_root(0, *PIECES[1], "inv_gains")
         inverse_root(1, half, M)
-        for place, (lo, hi) in enumerate(PIECES[1:]):
-            inverse_root(0, lo, hi, "square1", 2 * place * KIB)
+        inverse_root(0, *PIECES[2], "square1")
 
-        def children(values, b, lo, hi):
+        def children(values, b, lo, hi, first=None):
+            first = lo if first is None else first
             nc.vector.tensor_tensor(
                 out=values.rearrange("p (c i t) -> p c t i", i=4, t=PACK),
                 in0=ratio[b][:, :, lo:hi].rearrange("p t (c i) -> p c t i", i=4),
-                in1=norm[b, lo][:].rearrange("p t (c i) -> p c t i", i=4),
+                in1=norm[b, first][:, :, lo - first : hi - first].rearrange("p t (c i) -> p c t i", i=4),
                 op=MULT,
             )
             return values
@@ -343,25 +344,27 @@ def tile_list_wavelet_tree_contexts_kernel(
 
         def last_product(piece, operands):
             lo, hi = PIECES[piece]
-            accs = [bank(f"o{piece}{pair}", 2 * piece + pair) for pair in range(2)]
+            share = 2 if piece else 1
+            accs = [bank(f"o{piece}{group}", (2 + 2 * piece if piece else 0) + group) for group in range(PACK // share)]
             for step, (b, z, first) in enumerate(operands):
-                for pair in range(2):
-                    for place in range(2):
-                        j = 2 * pair + place
+                for group in range(PACK // share):
+                    for place in range(share):
+                        j = share * group + place
                         nc.tensor.matmul_mx(
-                            out=accs[pair][:, place * (hi - lo) : (place + 1) * (hi - lo)],
+                            out=accs[group][:, place * (hi - lo) : (place + 1) * (hi - lo)],
                             lhsT=w3_c[:, b * N + j * P : b * N + (j + 1) * P].bitcast(FP8X4),
                             lhsT_scale=w3_s[:, b * N + j * P : b * N + (j + 1) * P],
                             rhs=z[0][:, lo - first : hi - first].bitcast(FP8X4),
                             rhs_scale=z[1][:, lo - first : hi - first],
                             start=(step == 0 and place == 0),
-                            stop=(step == 1 and place == 1),
+                            stop=(step == 1 and place == share - 1),
                         )
-            for pair in range(2):
-                staged = held(f"staged{piece}{pair}", [P, 2 * (hi - lo)], F32)
-                round_on("vector" if hi == M and pair else "scalar", staged[:], accs[pair][:, 0 : 2 * (hi - lo)])
+            for group, acc in enumerate(accs):
+                staged = held(f"staged{piece}{group}", [P, share * (hi - lo)], F32)
+                round_on("vector" if hi == M and group else "scalar", staged[:], acc[:, 0 : share * (hi - lo)])
                 nc.sync.dma_start(
-                    out=out_rows[:, 2 * pair : 2 * pair + 2, lo:hi], in_=staged[:].rearrange("p (j m) -> p j m", j=2)
+                    out=out_rows[:, share * group : share * (group + 1), lo:hi],
+                    in_=staged[:].rearrange("p (j m) -> p j m", j=share),
                 )
 
         def values(name, width, after=None):
@@ -371,13 +374,14 @@ def tile_list_wavelet_tree_contexts_kernel(
         w3_c, w3_s = quantise("w3", w3_g[:].rearrange("p b c -> p (b c)"), f"w3_raw1{N // 2}")
         z0 = quantise("z_early0", early, "w3_g")
         early = children(values("z_early1", half), 1, 0, half)
-        rest = children(values("z_rest", half), 1, half, M)
-        z1 = quantise("z_early1", early, f"one1{half}")
+        middle = values("z_middle", 2 * P)
+        children(middle[:, 0:PASS], 0, *PIECES[1])
+        z1 = quantise("z_early1", early, f"one0{half}")
         last_product(0, ((0, z0, 0), (1, z1, 0)))
-        late = [children(values("z_late1", P), 0, *PIECES[1])]
-        z1 = quantise("z_rest", rest, f"one0{half}")
-        late.append(children(values("z_late2", P), 0, *PIECES[2]))
-        for piece, after in ((1, f"one0{PIECES[2][0]}"), (2, None)):
-            lo, hi = PIECES[piece]
-            z0 = quantise(f"z_late{piece}", late[piece - 1], after)
-            last_product(piece, ((1, z1, half), (0, z0, lo)))
+        children(middle[:, PASS : 2 * PASS], 1, *PIECES[1], half)
+        lo, hi = PIECES[2]
+        late = [children(values("z_late0", P), 0, lo, hi)]
+        both = quantise("z_middle", middle, f"one0{lo}")
+        last_product(1, ((0, both, half), (1, both, half - P)))
+        late.append(children(values("z_late1", P), 1, lo, hi, half))
+        last_product(2, [(b, quantise(f"z_late{b}", late[b]), lo) for b in range(2)])

@@ -344,8 +344,8 @@ def tile_list_wavelet_tree_contexts_kernel(
 
         def last_product(piece, operands):
             lo, hi = PIECES[piece]
-            share = 2 if piece else 1
-            accs = [bank(f"o{piece}{group}", (2 + 2 * piece if piece else 0) + group) for group in range(PACK // share)]
+            share = 2 if piece == 1 else 1
+            accs = [bank(f"o{piece}{group}", ((0, 4, 6)[piece] + group) % 8) for group in range(PACK // share)]
             for step, (b, z, first) in enumerate(operands):
                 for group in range(PACK // share):
                     for place in range(share):
@@ -359,12 +359,15 @@ def tile_list_wavelet_tree_contexts_kernel(
                             start=(step == 0 and place == 0),
                             stop=(step == 1 and place == share - 1),
                         )
-            for group, acc in enumerate(accs):
-                staged = held(f"staged{piece}{group}", [P, share * (hi - lo)], F32)
-                round_on("vector" if hi == M and group else "scalar", staged[:], acc[:, 0 : share * (hi - lo)])
+            width = share * (hi - lo)
+            engines = ("scalar", "vector") if hi == M else ("scalar",)
+            for first in range(0, len(accs), len(engines)):
+                staged = held(f"staged{piece}{first}", [P, len(engines) * width], F32)
+                for place, engine in enumerate(engines):
+                    round_on(engine, staged[:, place * width : (place + 1) * width], accs[first + place][:, 0:width])
                 nc.sync.dma_start(
-                    out=out_rows[:, share * group : share * (group + 1), lo:hi],
-                    in_=staged[:].rearrange("p (j m) -> p j m", j=share),
+                    out=out_rows[:, share * first : share * (first + len(engines)), lo:hi],
+                    in_=staged[:].rearrange("p (j m) -> p j m", m=hi - lo),
                 )
 
         def values(name, width, after=None):
@@ -374,14 +377,11 @@ def tile_list_wavelet_tree_contexts_kernel(
         w3_c, w3_s = quantise("w3", w3_g[:].rearrange("p b c -> p (b c)"), f"w3_raw1{N // 2}")
         z0 = quantise("z_early0", early, "w3_g")
         early = children(values("z_early1", half), 1, 0, half)
-        middle = values("z_middle", 2 * P)
-        children(middle[:, 0:PASS], 0, *PIECES[1])
+        middle = [children(values("z_middle0", P), 0, *PIECES[1])]
         z1 = quantise("z_early1", early, f"one0{half}")
         last_product(0, ((0, z0, 0), (1, z1, 0)))
-        children(middle[:, PASS : 2 * PASS], 1, *PIECES[1], half)
+        middle.append(children(values("z_middle1", P), 1, *PIECES[1], half))
+        last_product(1, [(b, quantise(f"z_middle{b}", middle[b], (f"one1{half}", None)[b]), half) for b in range(2)])
         lo, hi = PIECES[2]
-        late = [children(values("z_late0", P), 0, lo, hi)]
-        both = quantise("z_middle", middle, f"one0{lo}")
-        last_product(1, ((0, both, half), (1, both, half - P)))
-        late.append(children(values("z_late1", P), 1, lo, hi, half))
+        late = [children(values(f"z_late{b}", P, f"z_middle{b}"), b, lo, hi, (lo, half)[b]) for b in range(2)]
         last_product(2, [(b, quantise(f"z_late{b}", late[b]), lo) for b in range(2)])

@@ -249,7 +249,7 @@ def tile_list_wavelet_tree_contexts_kernel(
         by_gpsimd, by_scalar = [(0, 1, 2), (0, 1, 3), (1, 1, 0)], [(1, 1, 1), (1, 1, 2), (1, 1, 3)]
         rounded = round_w1("w1_g_gpsimd", "gpsimd", by_gpsimd, after="w1_g011", at=KIB // 2, last_unit=unit[:])
         picked = [[pick(held(f"picked0{t}", [P, M], F32, f"w1_g01{t}", -3 * KIB // 2)[:], 0, t) for t in range(2)]]
-        picked[0].append(pick(held("picked02", [P, M], F32, "w1_raw00")[:], 0, 2))
+        picked[0].append(pick(held("picked02", [P, M], F32, "w1_raw00", 2 * KIB)[:], 0, 2))
         quantise_w1("w1_gpsimd", by_gpsimd, rounded[:])
         picked[0].append(pick(held("picked03", [P, M], F32, "unit")[:], 0, 3))
         quantise_w1("w1_scalar", by_scalar, round_w1("w1_g_scalar", "scalar", by_scalar)[:])
@@ -374,8 +374,8 @@ def tile_list_wavelet_tree_contexts_kernel(
             return held(name, [P, width * PACK], BF16, after)[:]
 
         early = children(values("z_early0", half, "picked02"), 0, 0, half)
-        w3_c, w3_s = quantise("w3", w3_g[:].rearrange("p b c -> p (b c)"), f"w3_raw1{N // 2}")
-        z0 = quantise("z_early0", early, "w3_g")
+        w3_c, w3_s = quantise("w3", w3_g[:].rearrange("p b c -> p (b c)"), f"w3_raw1{N // 2}", KIB)
+        z0 = quantise("z_early0", early, f"w3_raw1{N // 2}")
         early = children(values("z_early1", half), 1, 0, half)
         middle = [children(values("z_middle0", P), 0, *PIECES[1])]
         z1 = quantise("z_early1", early, f"one0{half}")

@@ -161,11 +161,11 @@ def tile_list_wavelet_tree_contexts_kernel(
         w1_raw[1, 1] = load_w1(1, 1, "tab2_s", KIB)
         for a in range(2):
             parts = [(a, 0, t) for t in range(PACK)]
-            quantise_w1(f"w1_{a}0", parts, round_w1(f"w1_g{a}0", "scalar", parts, 9 * KIB, at=KIB)[:])
-        tab2_w = [held(f"tab2_w{a}", [P, T2], U32, after, at) for a, (after, at) in enumerate((("w1_raw10", 0), ("w1_g10", KIB)))]
+            quantise_w1(f"w1_{a}0", parts, round_w1(f"w1_g{a}0", "scalar", parts, 11 * KIB, at=KIB)[:])
+        tab2_w = [held(f"tab2_w{a}", [P, T2], U32, after, at) for a, (after, at) in enumerate((("w1_raw10", 0), ("w1_g10", 3 * KIB)))]
         for a in range(2):
             load_words(tab2_w[a][:], tab2_words, a)
-        w2_s_raw = held("w2_s_raw", [P, 2 * H], U8, "w1_g10", -KIB)
+        w2_s_raw = held("w2_s_raw", [P, 2 * H], U8, "w1_g10")
         nc.gpsimd.memset(w2_s_raw[:].bitcast(I32), 0)
         for q in range(4):
             nc.sync.dma_start(
@@ -270,8 +270,8 @@ def tile_list_wavelet_tree_contexts_kernel(
             in_=w2_s_raw[:].bitcast(I32).rearrange("p (ab g t w) -> p ab t g w", t=PACK, g=16, w=2),
         )
         w2_w = []
-        for b, after in enumerate(("w2_s_raw", None)):
-            w2_w.append(held(f"w2_w{b}", [P, 2 * H], U8, after))
+        for b, (after, at) in enumerate((("w2_s_raw", -KIB), (None, 0))):
+            w2_w.append(held(f"w2_w{b}", [P, 2 * H], U8, after, at))
             nc.gpsimd.tensor_copy(
                 out=w2_w[b][:].bitcast(I32).rearrange("p (a t g w) -> p a t g w", t=PACK, g=16, w=4),
                 in_=w2_w_raw[:].rearrange("p a (b g t w) -> p b a t g w", t=PACK, g=16, w=4)[:, b],
@@ -315,7 +315,7 @@ def tile_list_wavelet_tree_contexts_kernel(
                 w3_g[:, b, lo * PACK : hi * PACK].rearrange("p (n t) -> p n t", t=PACK),
                 raw[:].rearrange("p (t n) -> p n t", t=PACK),
             )
-        picked.append([pick(held("picked10", [P, M], F32, "tab2_w1")[:], 1, 0)])
+        picked.append([pick(held("picked10", [P, M], F32, "w2_s_raw", KIB)[:], 1, 0)])
         for t in range(PACK):
             second_product(0, t)
         half = M // 2
@@ -381,7 +381,9 @@ def tile_list_wavelet_tree_contexts_kernel(
         z1 = quantise("z_early1", early, f"one0{half}")
         last_product(0, ((0, z0, 0), (1, z1, 0)))
         middle.append(children(values("z_middle1", P), 1, *PIECES[1], half))
-        last_product(1, [(b, quantise(f"z_middle{b}", middle[b], (f"one1{half}", None)[b]), half) for b in range(2)])
         lo, hi = PIECES[2]
-        late = [children(values(f"z_late{b}", P, f"z_middle{b}"), b, lo, hi, (lo, half)[b]) for b in range(2)]
+        z0 = quantise("z_middle0", middle[0], f"one1{half}")
+        late = [children(values("z_late0", P), 0, lo, hi)]
+        last_product(1, ((0, z0, half), (1, quantise("z_middle1", middle[1], f"one0{lo}"), half)))
+        late.append(children(values("z_late1", P, "z_middle0"), 1, lo, hi, half))
         last_product(2, [(b, quantise(f"z_late{b}", late[b]), lo) for b in range(2)])

import math
from contextlib import ExitStack

import concourse.mybir as mybir
from concourse.masks import make_identity

K, T, S, T2, M, H, N = 1024, 4096, 1024, 2048, 512, 1024, 512
FLOPS = 2 * K * H * S + 2 * K * H * M + 2 * H * N * M

F32 = mybir.dt.float32
BF16 = mybir.dt.bfloat16
I32 = mybir.dt.int32
U32 = mybir.dt.uint32
U16 = mybir.dt.uint16
U8 = mybir.dt.uint8
FP8X4 = mybir.dt.float8_e4m3fn_x4
FP4X4 = mybir.dt.float4_e2m1fn_x4
ACT = mybir.ActivationFunctionType
MULT = mybir.AluOpType.mult
ADD = mybir.AluOpType.add

SIZES = {F32: 4, I32: 4, U32: 4, BF16: 2, U8: 1}
KIB = 1024

P = 128
PACK = 4
PASS = P * PACK
BANK = 512
PIECES = ((0, 256), (256, 384), (384, 512))


def tile_list_wavelet_tree_contexts_kernel(
    tc, tab_words, tab_scales, offs, w1, pos1, tab2_words, tab2_scales, offs2, w2_words, w2_scales, gain, w3, out
):
    nc = tc.nc
    with ExitStack() as ctx:
        lists = ctx.enter_context(tc.tile_pool(name="lists", bufs=1))
        keep = ctx.enter_context(tc.tile_pool(name="keep", bufs=1))
        psum = ctx.enter_context(tc.psum_pool(name="psum", bufs=1))

        places = {"end": 0}

        def held(name, shape, dtype, after=None, at=0, room=0):
            if after is None:
                places[name] = places["end"] + at
                places["end"] = places[name] + max(room, 64, math.prod(shape[1:]) * SIZES[dtype])
            else:
                places[name] = places[after] + at
            return keep.tile(shape, dtype, name=name, offset=places[name], align_bytes=64)

        def bank(name, number):
            return psum.tile([P, BANK], F32, name=name, tag=f"bank{number}")

        idx = lists.tile([P, S // 16], U16, name="idx")
        idx2 = lists.tile([P, M // 16], U16, name="idx2")
        parent = lists.tile([P, M // 16], U16, name="parent")

        def load_scale_rows(name, src, width, first, room, at=0):
            rows = held(name, [P, width], U8, at=at, room=room)
            nc.sync.dma_start(
                out=rows[first : first + 32, :].bitcast(I32), in_=src.bitcast(I32).rearrange("a q c -> q a c")
            )
            return rows

        def load_words(dst, src, a):
            nc.sync.dma_start(out=dst.bitcast(I32), in_=src[a].rearrange("p c i -> p (c i)").bitcast(I32))

        def load_w1(a, b, after=None, at=0):
            raw = held(f"w1_raw{a}{b}", [P, PACK, PASS], F32, after, at)
            nc.sync.dma_start(
                out=raw[:],
                in_=w1[a * PASS : (a + 1) * PASS, b * PASS : (b + 1) * PASS].rearrange("(p j) c -> p j c", j=PACK),
            )
            return raw

        def to_plane(engine, name, rows, first, width, after=None, at=0):
            plane = held(name, [P, 2 * width], U8, after, at)
            engine.memset(plane[:].bitcast(I32), 0)
            for q in range(4):
                nc.sync.dma_start(
                    out=plane[32 * q : 32 * q + 4, :].bitcast(I32),
                    in_=rows[first + 8 * q : first + 8 * q + 8, :].bitcast(I32),
                )
            return plane

        def gather(name, dtype, window, offsets, width, after=None, at=0, room=0):
            picked = held(name, [P, width], dtype, after, at, room)
            nc.vector.tensor_copy(out=picked[:], in_=window.indirect(offsets))
            return picked

        def round_on(engine, dst, src):
            if engine == "vector":
                nc.vector.tensor_copy(out=dst, in_=src)
            else:
                nc.scalar.copy(out=dst, in_=src)

        def round_on_gpsimd(dst, src, unit=1.0):
            nc.gpsimd.tensor_scalar(out=dst, in0=src, scalar1=unit, scalar2=0.0, op0=MULT, op1=ADD)

        def round_w1(name, engine, parts, room=0, after=None, at=0, last_unit=1.0):
            grouped = held(name, [P, len(parts) * PASS], BF16, after, at, room)
            for u, (a, b, t) in enumerate(parts):
                dst = grouped[:, u * PASS : (u + 1) * PASS]
                raw = w1_raw[a, b]
                if engine == "gpsimd":
                    round_on_gpsimd(
                        dst.rearrange("p (g i j) -> p g i j", g=16, j=PACK),
                        raw[:].rearrange("p j (g t i) -> p t g i j", t=PACK, i=8)[:, t],
                        last_unit if u == len(parts) - 1 else 1.0,
                    )
                else:
                    round_on(
                        engine,
                        dst.rearrange("p (g h i j) -> p g h j i", g=16, h=2, i=4),
                        raw[:].rearrange("p j (g t h i) -> p t g h j i", t=PACK, h=2, i=4)[:, t],
                    )
            return grouped

        def quantise(name, values, after=None, at=0, room=0):
            width = values.shape[1] // PACK
            codes = held(name + "_c", [P, width], U32, after, at, room)
            scales = held(name + "_s", [P, width], U8)
            nc.vector.quantize_mx(out=codes[:].bitcast(FP8X4), scales=scales[:], in_=values)
            return codes, scales

        w1_q = {}

        def quantise_w1(name, parts, values, after=None, at=0, room=0):
            codes, scales = quantise(name, values, after, at, room)
            for u, part in enumerate(parts):
                w1_q[part] = codes[:, u * P : (u + 1) * P], scales[:, u * P : (u + 1) * P]

        nc.sync.dma_start(idx[:], offs)
        tab_s = load_scale_rows("tab_s", tab_scales, T, 0, 16 * KIB)
        w1_raw = {(0, 0): load_w1(0, 0)}
        nc.sync.dma_start(idx2[:], offs2)
        tab2_s = load_scale_rows("tab2_s", tab2_scales, T2, 64, 11 * KIB, 7 * KIB)
        w1_raw[1, 0] = load_w1(1, 0)
        tab_w = [held("tab_w0", [P, T], U32)]
        load_words(tab_w[0][:], tab_words, 0)
        nc.sync.dma_start(parent[:], pos1)
        gain_rows = held("gain_rows", [P, PASS], F32)
        nc.gpsimd.memset(gain_rows[:], 0.0)
        nc.sync.dma_start(out=gain_rows[0:2, :], in_=gain.rearrange("(b c) -> b c", b=2))
        for rows, spans in ((tab_s, ((32, 64), (64, P))), (tab2_s, ((0, 64), (96, P)))):
            for lo, hi in spans:
                nc.vector.memset(rows[lo:hi, :].bitcast(I32), 0)
        identity = held("identity", [P, P], F32)
        make_identity(nc, identity[:])

        picked_s = gather("picked_s", U8, tab_s[:], idx[:], S, room=2 * KIB)
        v_s = to_plane(nc.vector, "v_s", picked_s, 0, S)
        tab_w.append(held("tab_w1", [P, T], U32, "tab_s"))
        load_words(tab_w[1][:], tab_words, 1)
        picked2_s = gather("picked2_s", U8, tab2_s[:], idx2[:], M)

        no_bias = held("no_bias", [P, 1], F32, room=2 * KIB)
        nc.gpsimd.memset(no_bias[:], 0.0)

        w1_raw[0, 1] = load_w1(0, 1, "tab2_s", -7 * KIB)
        w1_raw[1, 1] = load_w1(1, 1, "tab2_s", KIB)
        for a in range(2):
            parts = [(a, 0, t) for t in range(PACK)]
            quantise_w1(f"w1_{a}0", parts, round_w1(f"w1_g{a}0", "scalar", parts, 11 * KIB, at=KIB)[:])
        tab2_w = [held(f"tab2_w{a}", [P, T2], U32, after, at) for a, (after, at) in enumerate((("w1_raw10", 0), ("w1_g10", 3 * KIB)))]
        for a in range(2):
            load_words(tab2_w[a][:], tab2_words, a)
        w2_s_raw = held("w2_s_raw", [P, 2 * H], U8, "w1_g10")
        nc.gpsimd.memset(w2_s_raw[:].bitcast(I32), 0)
        for q in range(4):
            nc.sync.dma_start(
                out=w2_s_raw[32 * q : 32 * q + 4, :].bitcast(I32).rearrange("r (a c) -> r a c", a=2),
                in_=w2_scales.bitcast(I32)[:, 4 * q : 4 * q + 4, :].rearrange("a r c -> r a c"),
            )

        gain_dealt = held("gain_dealt", [P, PASS], F32)
        nc.scalar.copy(
            out=gain_dealt[:].rearrange("p (t g i) -> p t g i", t=PACK, i=8),
            in_=gain_rows[:].rearrange("p (g t i) -> p t g i", t=PACK, i=8),
        )
        turned = bank("turned", 7)
        for u in range(PACK):
            nc.tensor.transpose(turned[:, u * P : (u + 1) * P], gain_dealt[:, u * P : (u + 1) * P], identity[:])
        turned_gains = turned[:].rearrange("p (t b) -> p b t", t=PACK)[:, 0:2, :]
        gains = held("gains", [P, 2 * PACK], F32)
        nc.scalar.copy(out=gains[:].rearrange("p (b t) -> p b t", b=2), in_=turned_gains)
        gains_squared = held("gains_squared", [P, 2 * PACK], F32)
        nc.scalar.activation(out=gains_squared[:].rearrange("p (b t) -> p b t", b=2), in_=turned_gains, func=ACT.Square)

        v_w = {}
        for half in range(2):
            v_w[0, half] = gather(f"v_w0{half}", U32, tab_w[0][:], idx[:, 32 * half : 32 * (half + 1)], BANK)
        w2_w_raw = held("w2_w_raw", [P, 2, H // 2], I32, "tab_w0")
        nc.sync.dma_start(out=w2_w_raw[:], in_=w2_words.bitcast(I32).rearrange("a p c -> p a c"))
        v2_s = to_plane(nc.gpsimd, "v2_s", picked2_s, 64, M, "tab_w0", 8 * KIB)
        for half in range(2):
            v_w[1, half] = gather(f"v_w1{half}", U32, tab_w[1][:], idx[:, 32 * half : 32 * (half + 1)], BANK)

        def load_w3(b, lo, hi):
            raw = held(f"w3_raw{b}{lo}", [P, PACK * (hi - lo)], F32, "tab_w1", 4 * PACK * (b * N + lo))
            rows = w3[b * PASS : (b + 1) * PASS, lo:hi].rearrange("(g t i) n -> t g i n", t=PACK, i=8)
            for t in range(PACK):
                nc.sync.dma_start(out=raw[:, t * (hi - lo) : (t + 1) * (hi - lo)], in_=rows[t])
            return raw

        w3_raw = {part: load_w3(*part) for part in ((0, 0, N), (1, 0, N // 2), (1, N // 2, N))}

        damping = {}

        def first_pass(acc, a, b, t, half):
            codes, scales = w1_q[a, b, t]
            nc.tensor.matmul_mx(
                out=acc[:],
                lhsT=codes.bitcast(FP8X4),
                lhsT_scale=scales,
                rhs=v_w[a, half][:].bitcast(FP8X4),
                rhs_scale=v_s[:, a * S + half * BANK : a * S + (half + 1) * BANK],
                start=(a == 0),
                stop=(a == 1),
            )

        def empty(acc, b, t, half):
            nc.scalar.activation(
                out=damping[b, t][:, half * BANK : (half + 1) * BANK], in_=acc[:], func=ACT.Exp, scale=-0.5, bias=no_bias[:]
            )

        def open_banks(b):
            accs = {}
            for t in range(PACK):
                damping[b, t] = held(f"damping{b}{t}", [P, S], F32, f"damping0{t}" if b else None)
                for half in range(2):
                    accs[t, half] = bank(f"h{b}{t}{half}", 2 * t + half)
                    first_pass(accs[t, half], 0, b, t, half)
            return accs

        def pick(dst, b, t):
            nc.vector.tensor_copy(out=dst, in_=damping[b, t][:].indirect(parent[:]))
            return dst

        accs = open_banks(0)
        for t, half in ((0, 0), (1, 0), (0, 1), (1, 1), (2, 0), (2, 1), (3, 0), (3, 1)):
            first_pass(accs[t, half], 1, 0, t, half)
            empty(accs[t, half], 0, t, half)

        for t in range(2):
            quantise_w1(f"w1_01{t}", [(0, 1, t)], round_w1(f"w1_g01{t}", "vector", [(0, 1, t)], 4 * KIB, at=2 * KIB)[:])
        unit = held("unit", [P, 1], F32, room=2 * KIB)
        nc.gpsimd.memset(unit[:], 1.0)
        by_gpsimd, by_scalar = [(0, 1, 2), (0, 1, 3), (1, 1, 0)], [(1, 1, 1), (1, 1, 2), (1, 1, 3)]
        rounded = round_w1("w1_g_gpsimd", "gpsimd", by_gpsimd, after="w1_g011", at=KIB // 2, last_unit=unit[:])
        picked = [[pick(held(f"picked0{t}", [P, M], F32, f"w1_g01{t}", -3 * KIB // 2)[:], 0, t) for t in range(2)]]
        picked[0].append(pick(held("picked02", [P, M], F32, "w1_raw00", 2 * KIB)[:], 0, 2))
        quantise_w1("w1_gpsimd", by_gpsimd, rounded[:])
        picked[0].append(pick(held("picked03", [P, M], F32, "unit")[:], 0, 3))
        quantise_w1("w1_scalar", by_scalar, round_w1("w1_g_scalar", "scalar", by_scalar)[:])
        v2_w = [gather("v2_w0", U32, tab2_w[0][:], idx2[:], M, "w1_raw11")]
        v2_w.append(gather("v2_w1", U32, tab2_w[1][:], idx2[:], M, "w1_raw11", 2 * KIB))
        accs = open_banks(1)
        for t in range(PACK):
            for half in range(2):
                first_pass(accs[t, half], 1, 1, t, half)
                empty(accs[t, half], 1, t, half)

        inv_gains = held("inv_gains", [P, 2 * PACK], F32, "no_bias")
        nc.scalar.activation(out=inv_gains[:], in_=gains_squared[:], func=ACT.Abs_reciprocal_sqrt)

        w2_s = held("w2_s", [P, 2 * H], U8, "w1_g_scalar")
        nc.gpsimd.tensor_copy(
            out=w2_s[:].bitcast(I32).rearrange("p (ab t g w) -> p ab t g w", t=PACK, g=16, w=2),
            in_=w2_s_raw[:].bitcast(I32).rearrange("p (ab g t w) -> p ab t g w", t=PACK, g=16, w=2),
        )
        w2_w = []
        for b, (after, at) in enumerate((("w2_s_raw", -KIB), (None, 0))):
            w2_w.append(held(f"w2_w{b}", [P, 2 * H], U8, after, at))
            nc.gpsimd.tensor_copy(
                out=w2_w[b][:].bitcast(I32).rearrange("p (a t g w) -> p a t g w", t=PACK, g=16, w=4),
                in_=w2_w_raw[:].rearrange("p a (b g t w) -> p b a t g w", t=PACK, g=16, w=4)[:, b],
            )

        ratio = [held("ratio0", [P, PACK, M], F32), held("ratio1", [P, PACK, M], F32)]
        square = [held(f"square{b}", [P, PACK, M], F32) for b in range(2)]

        def second_product(b, t):
            acc = bank(f"b{b}{t}", PACK * b + t)
            for a in range(2):
                col = ((2 * a + b) * PACK + t) * P
                nc.tensor.matmul_mx(
                    out=acc[:],
                    lhsT=w2_w[b][:, 2 * P * (PACK * a + t) : 2 * P * (PACK * a + t + 1)].bitcast(FP4X4),
                    lhsT_scale=w2_s[:, col : col + P],
                    rhs=v2_w[a][:].bitcast(FP8X4),
                    rhs_scale=v2_s[:, a * M : (a + 1) * M],
                    start=(a == 0),
                    stop=(a == 1),
                )
            slot = b * PACK + t
            nc.vector.scalar_tensor_tensor(
                out=ratio[b][:, t, :], in0=acc[:], scalar=gains[:, slot : slot + 1], in1=picked[b][t], op0=MULT, op1=MULT
            )
            nc.scalar.activation(
                out=square[b][:, t, :], in_=ratio[b][:, t, :], func=ACT.Square, scale=inv_gains[:, slot : slot + 1]
            )

        def inverse_root(b, lo, hi, after=None, at=0):
            one = held(f"one{b}{lo}", [P, 1], F32, room=2 * KIB)
            nc.gpsimd.memset(one[:], 1.0)
            norm[b, lo] = held(f"norm{b}{lo}", [P, PACK, hi - lo], F32, after, at)
            nc.scalar.activation(
                out=norm[b, lo][:], in_=square[b][:, :, lo:hi], func=ACT.Abs_reciprocal_sqrt, bias=one[:]
            )

        w3_g = held("w3_g", [P, 2, N * PACK], BF16, "w2_w_raw")
        for (b, lo, hi), raw in w3_raw.items():
            round_on_gpsimd(
                w3_g[:, b, lo * PACK : hi * PACK].rearrange("p (n t) -> p n t", t=PACK),
                raw[:].rearrange("p (t n) -> p n t", t=PACK),
            )
        picked.append([pick(held("picked10", [P, M], F32, "w2_s_raw", KIB)[:], 1, 0)])
        for t in range(PACK):
            second_product(0, t)
        half = M // 2
        norm = {}
        inverse_root(0, 0, half)
        second_product(1, 0)
        for t, after in ((1, "picked02"), (2, "picked03"), (3, "picked10")):
            picked[1].append(pick(held(f"picked1{t}", [P, M], F32, after)[:], 1, t))
            second_product(1, t)
        inverse_root(1, 0, half)
        inverse_root(0, *PIECES[1], "inv_gains")
        inverse_root(1, half, M)
        inverse_root(0, *PIECES[2], "square1")

        def children(values, b, lo, hi, first=None):
            first = lo if first is None else first
            nc.vector.tensor_tensor(
                out=values.rearrange("p (c i t) -> p c t i", i=4, t=PACK),
                in0=ratio[b][:, :, lo:hi].rearrange("p t (c i) -> p c t i", i=4),
                in1=norm[b, first][:, :, lo - first : hi - first].rearrange("p t (c i) -> p c t i", i=4),
                op=MULT,
            )
            return values

        out_rows = out.rearrange("(j p) m -> p j m", p=P)

        def last_product(piece, operands):
            lo, hi = PIECES[piece]
            share = 2 if piece == 1 else 1
            accs = [bank(f"o{piece}{group}", ((0, 4, 6)[piece] + group) % 8) for group in range(PACK // share)]
            for step, (b, z, first) in enumerate(operands):
                for group in range(PACK // share):
                    for place in range(share):
                        j = share * group + place
                        nc.tensor.matmul_mx(
                            out=accs[group][:, place * (hi - lo) : (place + 1) * (hi - lo)],
                            lhsT=w3_c[:, b * N + j * P : b * N + (j + 1) * P].bitcast(FP8X4),
                            lhsT_scale=w3_s[:, b * N + j * P : b * N + (j + 1) * P],
                            rhs=z[0][:, lo - first : hi - first].bitcast(FP8X4),
                            rhs_scale=z[1][:, lo - first : hi - first],
                            start=(step == 0 and place == 0),
                            stop=(step == 1 and place == share - 1),
                        )
            width = share * (hi - lo)
            engines = ("scalar", "vector") if hi == M else ("scalar",)
            for first in range(0, len(accs), len(engines)):
                staged = held(f"staged{piece}{first}", [P, len(engines) * width], F32)
                for place, engine in enumerate(engines):
                    round_on(engine, staged[:, place * width : (place + 1) * width], accs[first + place][:, 0:width])
                nc.sync.dma_start(
                    out=out_rows[:, share * first : share * (first + len(engines)), lo:hi],
                    in_=staged[:].rearrange("p (j m) -> p j m", m=hi - lo),
                )

        def values(name, width, after=None):
            return held(name, [P, width * PACK], BF16, after)[:]

        early = children(values("z_early0", half, "picked02"), 0, 0, half)
        w3_c, w3_s = quantise("w3", w3_g[:].rearrange("p b c -> p (b c)"), f"w3_raw1{N // 2}", KIB)
        z0 = quantise("z_early0", early, f"w3_raw1{N // 2}")
        early = children(values("z_early1", half), 1, 0, half)
        middle = [children(values("z_middle0", P), 0, *PIECES[1])]
        z1 = quantise("z_early1", early, f"one0{half}")
        last_product(0, ((0, z0, 0), (1, z1, 0)))
        middle.append(children(values("z_middle1", P), 1, *PIECES[1], half))
        lo, hi = PIECES[2]
        z0 = quantise("z_middle0", middle[0], f"one1{half}")
        late = [children(values("z_late0", P), 0, lo, hi)]
        last_product(1, ((0, z0, half), (1, quantise("z_middle1", middle[1], f"one0{lo}"), half)))
        late.append(children(values("z_late1", P, "z_middle0"), 1, lo, hi, half))
        last_product(2, [(b, quantise(f"z_late{b}", late[b]), lo) for b in range(2)])
